import numpy as np
import ml_dtypes


def mxq(x, axis, fmt="e4m3"):
    dtype, down = {"e4m3": (ml_dtypes.float8_e4m3fn, 7), "e5m2": (ml_dtypes.float8_e5m2, 14)}[fmt]
    v = np.moveaxis(np.asarray(x, np.float32).astype(ml_dtypes.bfloat16).astype(np.float64), axis, -1)
    blocks = v.reshape(v.shape[:-1] + (-1, 32))
    amax = np.abs(blocks).max(-1, keepdims=True)
    byte = np.maximum(np.where(amax > 0, np.frexp(amax)[1] - 1 + 127, 0) - down, 1)
    scale = np.exp2(byte - 127.0)
    codes = (blocks / scale).astype(np.float32).astype(dtype).astype(np.float64)
    return np.moveaxis((codes * scale).reshape(v.shape), -1, axis)


WIDE = False


def mx_kscale(k):
    if not WIDE:
        return np.ones(k)
    levels = np.array([18, -18])
    if k % 512:
        return np.exp2(np.random.permutation(np.resize(levels, k // 32))).repeat(32)
    a = np.empty((k // 512, 16))
    for p in range(k // 512):
        a[p, :8] = np.random.permutation(np.resize(levels, 8))
        for g in range(8):
            far = levels[np.abs(levels - a[p, g]) >= 10]
            a[p, g + 8] = far[np.random.randint(len(far))]
    return np.exp2(a.ravel()).repeat(32)


def f64(x):
    return np.asarray(x).astype(np.float64)


def striped(idx):
    return np.tile(np.asarray(idx).reshape(-1, 16).T, (8, 1)).astype(np.uint16)


def unstriped(offs):
    return offs[:16].T.reshape(-1).astype(np.int64)


B, N, T, D, R = 2, 512, 2048, 512, 512


def setup_inputs():
    n = np.random.standard_normal
    idx = np.random.permutation(T)[:B * N]
    s = mx_kscale(D)[:, None]
    z = mx_kscale(R)[:, None]
    u = np.ones(T)
    u[idx] = mx_kscale(B * N)
    r = np.random.uniform(0.5, 2.0, T) * u
    x = n((B, D, R))
    return {
        "xT": (x * s).astype(np.float32),
        "wT": (n((D, T)) * (1.00 / np.sqrt(D)) / s / r).astype(np.float32),
        "wt": (np.random.uniform(0.5, 1.5, (B, R, 1)) * 1.0 / np.sqrt(R) * z).astype(np.float32),
        "ts": np.tile(r, (128, 1)).astype(np.float32),
        "xm": (x.transpose(0, 2, 1) / z).astype(np.float32),
        "offs": striped(idx),
    }


def reference(xT, wT, wt, ts, xm, offs):
    idx = unstriped(offs)
    pick = lambda x: x[:, idx].reshape(x.shape[0], B, N).transpose(1, 0, 2)
    w = pick(f64(wT))
    a = mxq(f64(xT), 1, "e4m3").transpose(0, 2, 1) @ mxq(w, 1, "e4m3")
    ts_ = pick(f64(ts))[:, :1, :]
    a = a * ts_
    t = a[:, :, :N // 2] - a[:, :, N // 2:]
    q = f64(wt) / (1.0 + np.exp(t))
    g = np.concatenate([-q, q], -1)
    g = g * ts_
    dw = mxq(f64(xm), 1, "e4m3").transpose(0, 2, 1) @ mxq(g, 1, "e5m2")
    gw = np.zeros((D, T))
    gw[:, idx] = dw.transpose(1, 0, 2).reshape(D, B * N)
    gx = mxq(g, 2, "e5m2") @ mxq(w, 2, "e4m3").transpose(0, 2, 1)
    return gw, gx

@@ -1,0 +1,284 @@
+from contextlib import ExitStack
+
+import concourse.mybir as mybir
+from concourse.masks import make_identity
+
+B, N, T, D, R = 2, 512, 2048, 512, 512
+FLOPS = 3 * 2 * B * N * D * R
+
+F32 = mybir.dt.float32
+BF16 = mybir.dt.bfloat16
+U32 = mybir.dt.uint32
+U16 = mybir.dt.uint16
+U8 = mybir.dt.uint8
+E4M3 = mybir.dt.float8_e4m3fn_x4
+E5M2 = mybir.dt.float8_e5m2_x4
+MULT = mybir.AluOpType.mult
+ADD = mybir.AluOpType.add
+COPY = mybir.ActivationFunctionType.Copy
+SIGMOID = mybir.ActivationFunctionType.Sigmoid
+
+P = 128
+PACK = 4
+K = P * PACK
+ALIGN = 64
+
+
+def tile_attend_gbpr_wx_ts_kernel(tc, xT, wT, wt, ts, xm, offs, out_0, out_1):
+    nc = tc.nc
+    with ExitStack() as ctx:
+        lists = ctx.enter_context(tc.tile_pool(name="lists", bufs=1))
+        sb = ctx.enter_context(tc.tile_pool(name="sb", bufs=1))
+        ps = ctx.enter_context(tc.psum_pool(name="ps", bufs=1))
+
+        def held(shape, dtype, name, tag=None):
+            return sb.tile(shape, dtype, name=name, tag=tag or name, align_bytes=ALIGN)
+
+        def bank(k, name):
+            return ps.tile([P, K], F32, name=name, tag="bank%d" % k)
+
+        def mx_operand(name):
+            return held([P, K], U32, name + "_codes"), held([P, K], U8, name + "_scales")
+
+        def quantize(operand, fmt, src, c0=0, c1=K):
+            codes, scales = operand
+            nc.vector.quantize_mx(out=codes[:, c0:c1].bitcast(fmt), scales=scales[:, c0:c1], in_=src[:, PACK * c0:PACK * c1])
+
+        def product(out, fixed, fixed_fmt, j, moving, moving_fmt):
+            cols = slice(P * j, P * (j + 1))
+            nc.tensor.matmul_mx(out=out[:], lhsT=fixed[0][:, cols].bitcast(fixed_fmt), lhsT_scale=fixed[1][:, cols],
+                                rhs=moving[0][:].bitcast(moving_fmt), rhs_scale=moving[1][:], start=True, stop=True)
+
+        offsets = lists.tile([P, B * N // 16], U16, name="offsets")
+        nc.sync.dma_start(offsets[:], offs)
+        group_offsets = [offsets[:, b * (N // 16):(b + 1) * (N // 16)] for b in range(B)]
+
+        ts_row = held([P, T], F32, "ts_row")
+        nc.sync.dma_start(out=ts_row[0:32, :], in_=ts[0:32, :])
+        nc.vector.memset(ts_row[32:64, :], 0.0)
+        nc.gpsimd.memset(ts_row[64:128, :], 0.0)
+        row_weight = held([P, B, PACK], F32, "row_weight")
+        nc.scalar.dma_start(out=row_weight[:], in_=wt.rearrange("b (p t) o -> p b (t o)", t=PACK))
+
+        w_rows = wT.rearrange("(p t) c -> t p c", t=PACK)
+        w_plane = [held([P, T], F32, "w_plane%d" % t) for t in range(PACK)]
+        for t in range(PACK):
+            nc.sync.dma_start(out=w_plane[t][:], in_=w_rows[t])
+        x0_half = [held([P, PACK, R // 2], F32, "x0_half%d" % h) for h in range(2)]
+        for h in range(2):
+            nc.sync.dma_start(out=x0_half[h][:], in_=xT[0].rearrange("(p j) r -> p j r", j=PACK)[:, :, h * (R // 2):(h + 1) * (R // 2)])
+        xm_raw = [held([P, PACK, D], F32, "xm_raw%d" % b) for b in range(B)]
+        x1_raw = held([P, PACK, R], F32, "x1_raw")
+        nc.sync.dma_start(out=xm_raw[0][:], in_=xm[0].rearrange("(p t) d -> p t d", t=PACK))
+        nc.sync.dma_start(out=x1_raw[:], in_=xT[1].rearrange("(p j) r -> p j r", j=PACK))
+        nc.sync.dma_start(out=xm_raw[1][:], in_=xm[1].rearrange("(p t) d -> p t d", t=PACK))
+
+        ident = held([P, P], F32, "ident")
+        make_identity(nc, ident[:])
+        warm = held([P, 1], F32, "warm")
+        nc.scalar.activation(warm[:], ident[:, 0:1], SIGMOID)
+        window = [held([P, T], F32, "window%d" % j) for j in range(PACK)]
+        for j in range(PACK):
+            nc.gpsimd.memset(window[j][:], 0.0)
+
+        STRETCH = PACK * K
+        work = held([P, 5 * STRETCH], BF16, "work")
+        w0_planes = held([P, PACK * N], BF16, "w0_planes")
+        w_planes = [w0_planes[:].rearrange("p (t c) -> p t c", t=PACK), work[:, 0:4 * STRETCH].rearrange("p (t c) -> p t c", t=PACK)[:, :, 0:N]]
+        x0_packed = work[:, STRETCH:2 * STRETCH]
+        pos0 = work[:, 2 * STRETCH:3 * STRETCH].bitcast(F32)
+        factor1 = held([P, PACK * N], F32, "factor1")
+        factor = [work[:, 3 * STRETCH:5 * STRETCH].bitcast(F32), factor1[:]]
+
+        ts_listed = held([P, B * N], F32, "ts_listed")
+        nc.vector.tensor_copy(ts_listed[:], ts_row[:].indirect(offsets[:]))
+        signed = []
+        for half, sign in ((0, -1.0), (1, 1.0)):
+            turned = bank(half, "ts_turned%d" % half)
+            for b in range(B):
+                for j in range(2):
+                    c0 = N * b + 256 * half + P * j
+                    nc.tensor.transpose(turned[:, P * (2 * b + j):P * (2 * b + j + 1)], ts_listed[:, c0:c0 + P], ident[:])
+            col = held([P, 2 * B], F32, "signed%d" % half)
+            nc.scalar.activation(col[:], turned[:].rearrange("p (k c) -> p k c", c=P)[:, :, 0], COPY, scale=sign)
+            signed.append(col)
+        for b in range(B):
+            spread = bank(6 + b, "ts_spread%d" % b)
+            for half in range(2):
+                for j in range(2):
+                    k = 2 * half + j
+                    nc.tensor.transpose(spread[:, P * k:P * (k + 1)],
+                                        signed[half][:, 2 * b + j:2 * b + j + 1].to_broadcast([P, P]), ident[:])
+            for t in range(PACK):
+                nc.scalar.activation(factor[b][:, N * t:N * (t + 1)], spread[:], COPY, scale=row_weight[:, b, t:t + 1])
+
+        def woven(packed):
+            return packed.rearrange("p (c i t) -> p c t i", i=4, t=PACK)
+
+        def planes(ap):
+            return ap.rearrange("p t (c i) -> p c t i", i=4)
+
+        def gather(b, t):
+            nc.vector.tensor_copy(w_planes[b][:, t, :], w_plane[t][:].indirect(group_offsets[b]))
+
+        w_packed = [held([P, PACK * N], BF16, "w_packed%d" % b) for b in range(B)]
+        w_d = [mx_operand("w_d%d" % b) for b in range(B)]
+        x_d = [mx_operand("x_d%d" % b) for b in range(B)]
+
+        def pack_w(b):
+            for k in (0, 2, 1, 3):
+                nc.scalar.copy(woven(w_packed[b][:, PACK * P * k:PACK * P * (k + 1)]), planes(w_planes[b][:, :, P * k:P * (k + 1)]))
+                quantize(w_d[b], E4M3, w_packed[b], P * k, P * (k + 1))
+
+        def deal_x(copy, packed, raw):
+            copy(packed.rearrange("p (t m j) -> p m j t", t=PACK, j=PACK), raw.rearrange("p j (m t) -> p m j t", t=PACK))
+
+        for t in range(PACK):
+            gather(0, t)
+        for h in range(2):
+            deal_x(nc.vector.tensor_copy, x0_packed[:, 2 * R * h:2 * R * (h + 1)], x0_half[h][:])
+            quantize(x_d[0], E4M3, x0_packed, h * R // 2, (h + 1) * R // 2)
+        pack_w(0)
+
+        def scores(b, banks):
+            score = [bank(banks[k], "score%d_%d" % (b, k)) for k in range(4)]
+            for k in (0, 2, 1, 3):
+                product(score[k], w_d[b], E4M3, k, x_d[b], E4M3)
+            return score
+
+        h_packed = [held([P, PACK * N], BF16, "h_packed%d" % b) for b in range(B)]
+        h_r = [mx_operand("h_r%d" % b) for b in range(B)]
+        xm_r = [mx_operand("xm_r%d" % b) for b in range(B)]
+
+        score = scores(0, (0, 1, 2, 3))
+        diff = [held([P, R], F32, "diff%d" % j) for j in range(2)]
+        for j in range(2):
+            pos = pos0[:, R * (1 - j):R * (2 - j)]
+            nc.scalar.activation(pos, score[j][:], COPY, scale=signed[0][:, j:j + 1])
+            nc.vector.scalar_tensor_tensor(diff[j][:], score[2 + j][:], signed[1][:, j:j + 1], pos, MULT, ADD)
+        turned = []
+        for j in range(2):
+            sig = held([P, R], F32, "sig%d" % j)
+            nc.scalar.activation(sig[:].rearrange("p (t h m) -> p t h m", t=PACK, h=2),
+                                 diff[j][:].rearrange("p (h t m) -> p t h m", t=PACK, h=2), SIGMOID)
+            turn = bank(4 + j, "sig_turned%d" % j)
+            for t in range(PACK):
+                nc.tensor.transpose(turn[:, P * t:P * (t + 1)], sig[:, P * t:P * (t + 1)], ident[:])
+            turned.append(turn)
+
+        def pack_xm(b, tag):
+            packed = held([P, PACK * D], BF16, "xm_packed%d" % b, tag)
+            for k in range(4):
+                nc.scalar.copy(woven(packed[:, PACK * P * k:PACK * P * (k + 1)]), planes(xm_raw[b][:, :, P * k:P * (k + 1)]))
+                quantize(xm_r[b], E4M3, packed, P * k, P * (k + 1))
+
+        def weigh(b, sig):
+            by_plane = factor[b].rearrange("p (t s) -> p t s", t=PACK)
+            for j in range(2):
+                for half in (1, 0):
+                    s0 = 256 * half + P * j
+                    nc.vector.tensor_tensor(woven(h_packed[b][:, PACK * s0:PACK * (s0 + P)]),
+                                            planes(sig[j][:].rearrange("p (t s) -> p t s", t=PACK)),
+                                            planes(by_plane[:, :, s0:s0 + P]), MULT)
+
+        weigh(0, turned)
+        for k in (2, 0, 3, 1):
+            quantize(h_r[0], E5M2, h_packed[0], P * k, P * (k + 1))
+        pack_xm(0, "diff1")
+
+        def table_gradient(b, banks):
+            tiles = [bank(banks[j], "dw%d_%d" % (b, j)) for j in range(4)]
+            for j in range(4):
+                product(tiles[j], xm_r[b], E4M3, j, h_r[b], E5M2)
+            return tiles
+
+        def place(b, tiles, dw, tag):
+            staged = held([P, len(tiles), N], F32, "dw_staged%d_%d" % (b, tiles[0]), tag)
+            for a, j in enumerate(tiles):
+                nc.scalar.copy(staged[:, a, :], dw[j][:])
+                nc.vector.tensor_copy(window[j][:].indirect(group_offsets[b]), staged[:, a, :])
+                if b == B - 1:
+                    nc.sync.dma_start(out=out_0[P * j:P * (j + 1), :], in_=window[j][:])
+
+        dw0 = table_gradient(0, (0, 1, 2, 3))
+
+        place(0, [0], dw0, "x0_half0")
+
+        for t in range(PACK):
+            gather(1, t)
+        x1_packed = held([P, PACK * R], BF16, "x1_packed", "sig1")
+        for h in range(2):
+            dealt = x1_packed[:, 2 * R * h:2 * R * (h + 1)].rearrange("p (t m j) -> p m j t", t=PACK, j=PACK)
+            for c in range(2):
+                r0 = 256 * h + P * c
+                nc.scalar.copy(dealt[:, 32 * c:32 * (c + 1)], x1_raw[:, :, r0:r0 + P].rearrange("p j (m t) -> p m j t", t=PACK))
+        quantize(x_d[1], E4M3, x1_packed)
+        pack_w(1)
+        place(0, [1], dw0, "w_packed1")
+        place(0, [2], dw0, "x0_half1")
+        score = scores(1, (4, 5, 6, 7))
+        scaled = [held([P, R], F32, "scaled%d" % k) for k in range(4)]
+        for k in (0, 2, 1, 3):
+            nc.scalar.activation(scaled[k][:].rearrange("p (t h m) -> p t h m", t=PACK, h=2),
+                                 score[k][:].rearrange("p (h t m) -> p t h m", t=PACK, h=2), COPY,
+                                 scale=signed[k // 2][:, 2 + k % 2:3 + k % 2])
+        sig1 = []
+        for j in range(2):
+            summed = bank(4 + j, "summed%d" % j)
+            for t in range(PACK):
+                for half in range(2):
+                    nc.tensor.matmul(summed[:, P * t:P * (t + 1)], scaled[2 * half + j][:, P * t:P * (t + 1)], ident[:],
+                                     start=(half == 0), stop=(half == 1), is_transpose=True)
+            sig = held([P, R], F32, "sig1_%d" % j, "sig%d" % j)
+            nc.scalar.activation(sig[:], summed[:], SIGMOID)
+            sig1.append(sig)
+        weigh(1, sig1)
+        quantize(h_r[1], E5M2, h_packed[1])
+        place(0, [3], dw0, "factor1")
+        pack_xm(1, "xm_r0_codes")
+        dw1 = table_gradient(1, (6, 7, 4, 5))
+        place(1, [0], dw1, "x0_half0")
+        place(1, [1], dw1, "x0_half1")
+
+        def turn_h(b, banks):
+            words = h_packed[b][:].bitcast(F32)
+            out = held([P, PACK * K], BF16, "h_turned%d" % b)
+            for u in range(2):
+                turn = bank(banks[u], "h_turn%d_%d" % (b, u))
+                for t in range(PACK):
+                    nc.tensor.transpose(turn[:, P * t:P * (t + 1)], words[:, 2 * t + u::2 * PACK], ident[:])
+                nc.scalar.copy(out[:].rearrange("s (p u e t) -> s u p e t", u=2, e=2, t=PACK)[:, u],
+                               turn[:].bitcast(BF16).rearrange("s (t p e) -> s p e t", t=PACK, e=2))
+            return out
+
+        def turn_w(b, banks):
+            out = held([P, PACK * K], BF16, "w_turned%d" % b)
+            for g in range(2):
+                turn = bank(banks[g], "w_turn%d_%d" % (b, g))
+                for c in range(4):
+                    words = w_planes[b][:, 2 * g + c // 2, :].bitcast(F32)
+                    nc.tensor.transpose(turn[:, P * c:P * (c + 1)], words[:, c % 2::2], ident[:])
+                nc.scalar.copy(out[:].bitcast(F32).rearrange("s (p g c) -> s g p c", g=2, c=4)[:, g],
+                               turn[:].rearrange("s (c p) -> s p c", c=4))
+            return out
+
+        w_i = [mx_operand("w_i%d" % b) for b in range(B)]
+        h_i = [mx_operand("h_i%d" % b) for b in range(B)]
+
+        def row_gradient(b, banks, tags):
+            for g in range(2):
+                staged = held([P, 2, D], F32, "gx_staged%d_%d" % (b, g), tags[g])
+                for a in range(2):
+                    j = 2 * g + a
+                    gx = bank(banks[j], "gx%d_%d" % (b, j))
+                    product(gx, h_i[b], E5M2, j, w_i[b], E4M3)
+                    nc.scalar.copy(staged[:, a, :], gx[:])
+                nc.sync.dma_start(out=out_1[b, 2 * P * g:2 * P * (g + 1), :].rearrange("(a m) d -> m a d", m=P), in_=staged[:])
+
+        quantize(w_i[0], E4M3, turn_w(0, (0, 2)))
+        quantize(h_i[0], E5M2, turn_h(0, (0, 2)))
+        quantize(w_i[1], E4M3, turn_w(1, (0, 1)))
+        quantize(h_i[1], E5M2, turn_h(1, (2, 3)))
+        place(1, [2, 3], dw1, "h_turned1")
+        row_gradient(0, (0, 1, 2, 3), ("xm_raw0", "xm_raw1"))
+        row_gradient(1, (0, 1, 2, 3), ("x1_raw", "ts_row"))

@@ -37,12 +37,12 @@ def tile_attend_gbpr_wx_ts_kernel(tc, xT, wT, wt, ts, xm, offs, out_0, out_1):
         def bank(k, name):
             return ps.tile([P, K], F32, name=name, tag="bank%d" % k)
 
-        def mx_operand(name):
-            return held([P, K], U32, name + "_codes"), held([P, K], U8, name + "_scales")
+        def mx_operand(name, tag=None):
+            return held([P, K], U32, name + "_codes", tag), held([P, K], U8, name + "_scales")
 
         def quantize(operand, fmt, src, c0=0, c1=K):
             codes, scales = operand
-            nc.vector.quantize_mx(out=codes[:, c0:c1].bitcast(fmt), scales=scales[:, c0:c1], in_=src[:, PACK * c0:PACK * c1])
+            nc.vector.quantize_mx(out=codes[:, c0:c1].bitcast(fmt), scales=scales[:, c0:c1], in_=src)
 
         def product(out, fixed, fixed_fmt, j, moving, moving_fmt):
             cols = slice(P * j, P * (j + 1))
@@ -53,20 +53,21 @@ def tile_attend_gbpr_wx_ts_kernel(tc, xT, wT, wt, ts, xm, offs, out_0, out_1):
         nc.sync.dma_start(offsets[:], offs)
         group_offsets = [offsets[:, b * (N // 16):(b + 1) * (N // 16)] for b in range(B)]
 
+        row_weight = held([P, B, PACK], F32, "row_weight")
+        nc.sync.dma_start(out=row_weight[:], in_=wt.rearrange("b (p t) o -> p b (t o)", t=PACK))
         ts_row = held([P, T], F32, "ts_row")
         nc.sync.dma_start(out=ts_row[0:32, :], in_=ts[0:32, :])
         nc.vector.memset(ts_row[32:64, :], 0.0)
         nc.gpsimd.memset(ts_row[64:128, :], 0.0)
-        row_weight = held([P, B, PACK], F32, "row_weight")
-        nc.scalar.dma_start(out=row_weight[:], in_=wt.rearrange("b (p t) o -> p b (t o)", t=PACK))
 
         w_rows = wT.rearrange("(p t) c -> t p c", t=PACK)
         w_plane = [held([P, T], F32, "w_plane%d" % t) for t in range(PACK)]
+        x0_half = [held([P, PACK, R // 2], F32, "x0_half%d" % h) for h in range(2)]
+        x0_rows = xT[0].rearrange("(p j) (h r) -> h p j r", j=PACK, h=2)
         for t in range(PACK):
             nc.sync.dma_start(out=w_plane[t][:], in_=w_rows[t])
-        x0_half = [held([P, PACK, R // 2], F32, "x0_half%d" % h) for h in range(2)]
         for h in range(2):
-            nc.sync.dma_start(out=x0_half[h][:], in_=xT[0].rearrange("(p j) r -> p j r", j=PACK)[:, :, h * (R // 2):(h + 1) * (R // 2)])
+            nc.sync.dma_start(out=x0_half[h][:], in_=x0_rows[h])
         xm_raw = [held([P, PACK, D], F32, "xm_raw%d" % b) for b in range(B)]
         x1_raw = held([P, PACK, R], F32, "x1_raw")
         nc.sync.dma_start(out=xm_raw[0][:], in_=xm[0].rearrange("(p t) d -> p t d", t=PACK))
@@ -81,14 +82,12 @@ def tile_attend_gbpr_wx_ts_kernel(tc, xT, wT, wt, ts, xm, offs, out_0, out_1):
         for j in range(PACK):
             nc.gpsimd.memset(window[j][:], 0.0)
 
-        STRETCH = PACK * K
-        work = held([P, 5 * STRETCH], BF16, "work")
-        w0_planes = held([P, PACK * N], BF16, "w0_planes")
-        w_planes = [w0_planes[:].rearrange("p (t c) -> p t c", t=PACK), work[:, 0:4 * STRETCH].rearrange("p (t c) -> p t c", t=PACK)[:, :, 0:N]]
-        x0_packed = work[:, STRETCH:2 * STRETCH]
-        pos0 = work[:, 2 * STRETCH:3 * STRETCH].bitcast(F32)
+        stretch = 2 * N
+        work = held([P, 3 * stretch + 2 * PACK * N], BF16, "work")
+        w0_planes = held([P, PACK, N], BF16, "w0_planes")
+        w_planes = [w0_planes[:], work[:, 0:PACK * stretch].rearrange("p (t c) -> p t c", t=PACK)[:, :, 0:N]]
         factor1 = held([P, PACK * N], F32, "factor1")
-        factor = [work[:, 3 * STRETCH:5 * STRETCH].bitcast(F32), factor1[:]]
+        factor = [work[:, 3 * stretch:].bitcast(F32), factor1[:]]
 
         ts_listed = held([P, B * N], F32, "ts_listed")
         nc.vector.tensor_copy(ts_listed[:], ts_row[:].indirect(offsets[:]))
@@ -102,6 +101,7 @@ def tile_attend_gbpr_wx_ts_kernel(tc, xT, wT, wt, ts, xm, offs, out_0, out_1):
             col = held([P, 2 * B], F32, "signed%d" % half)
             nc.scalar.activation(col[:], turned[:].rearrange("p (k c) -> p k c", c=P)[:, :, 0], COPY, scale=sign)
             signed.append(col)
+
         for b in range(B):
             spread = bank(6 + b, "ts_spread%d" % b)
             for half in range(2):
@@ -112,79 +112,86 @@ def tile_attend_gbpr_wx_ts_kernel(tc, xT, wT, wt, ts, xm, offs, out_0, out_1):
             for t in range(PACK):
                 nc.scalar.activation(factor[b][:, N * t:N * (t + 1)], spread[:], COPY, scale=row_weight[:, b, t:t + 1])
 
-        def woven(packed):
-            return packed.rearrange("p (c i t) -> p c t i", i=4, t=PACK)
+        def woven(packed, run=4):
+            return packed.rearrange("p (c i t) -> p c t i", i=run, t=PACK)
 
-        def planes(ap):
-            return ap.rearrange("p t (c i) -> p c t i", i=4)
+        def planes(ap, run=4):
+            return ap.rearrange("p t (c i) -> p c t i", i=run)
+
+        def by_plane(flat):
+            return flat.rearrange("p (t c) -> p t c", t=PACK)
+
+        def dealt(rows):
+            return rows.rearrange("p (m t) -> p t m", t=PACK)
 
         def gather(b, t):
             nc.vector.tensor_copy(w_planes[b][:, t, :], w_plane[t][:].indirect(group_offsets[b]))
 
-        w_packed = [held([P, PACK * N], BF16, "w_packed%d" % b) for b in range(B)]
-        w_d = [mx_operand("w_d%d" % b) for b in range(B)]
         x_d = [mx_operand("x_d%d" % b) for b in range(B)]
 
-        def pack_w(b):
-            for k in (0, 2, 1, 3):
-                nc.scalar.copy(woven(w_packed[b][:, PACK * P * k:PACK * P * (k + 1)]), planes(w_planes[b][:, :, P * k:P * (k + 1)]))
-                quantize(w_d[b], E4M3, w_packed[b], P * k, P * (k + 1))
-
-        def deal_x(copy, packed, raw):
-            copy(packed.rearrange("p (t m j) -> p m j t", t=PACK, j=PACK), raw.rearrange("p j (m t) -> p m j t", t=PACK))
+        def weave(packed, source, k):
+            nc.scalar.copy(woven(packed), planes(source[:, :, P * k:P * (k + 1)]))
 
         for t in range(PACK):
             gather(0, t)
+        x0_packed = held([P, PACK * R], BF16, "x0_packed")
+        w0_first = held([P, 2 * N], BF16, "w0_first")
         for h in range(2):
-            deal_x(nc.vector.tensor_copy, x0_packed[:, 2 * R * h:2 * R * (h + 1)], x0_half[h][:])
-            quantize(x_d[0], E4M3, x0_packed, h * R // 2, (h + 1) * R // 2)
-        pack_w(0)
-
-        def scores(b, banks):
-            score = [bank(banks[k], "score%d_%d" % (b, k)) for k in range(4)]
-            for k in (0, 2, 1, 3):
-                product(score[k], w_d[b], E4M3, k, x_d[b], E4M3)
-            return score
+            x_half = x0_packed[:, 2 * R * h:2 * R * (h + 1)]
+            nc.vector.tensor_copy(woven(x_half), planes(x0_half[h][:]))
+            quantize(x_d[0], E4M3, x_half, h * R // 2, (h + 1) * R // 2)
+        w_d = [mx_operand("w_d0", "x0_half1"), mx_operand("w_d1")]
+        for j, packed in enumerate((w0_first[:], work[:, 2 * stretch:3 * stretch])):
+            for half in range(2):
+                weave(packed[:, N * half:N * (half + 1)], w_planes[0], 2 * half + j)
+            quantize(w_d[0], E4M3, packed, 2 * P * j, 2 * P * (j + 1))
 
         h_packed = [held([P, PACK * N], BF16, "h_packed%d" % b) for b in range(B)]
         h_r = [mx_operand("h_r%d" % b) for b in range(B)]
         xm_r = [mx_operand("xm_r%d" % b) for b in range(B)]
 
+        def scores(b, banks):
+            tiles = [bank(banks[c], "score%d_%d" % (b, c)) for c in range(4)]
+            for c in range(4):
+                product(tiles[c], w_d[b], E4M3, c, x_d[b], E4M3)
+            return tiles
+
+        def scale_items(b, score, c):
+            out = held([P, R], F32, "scaled%d_%d" % (b, c))
+            k = 2 * b + c // 2
+            nc.scalar.activation(by_plane(out[:]), dealt(score[c][:]), COPY, scale=signed[c % 2][:, k:k + 1])
+            return out
+
+        def weigh(b, sig):
+            for j in range(2):
+                for half in (1, 0):
+                    s0 = 256 * half + P * j
+                    nc.vector.tensor_tensor(woven(h_packed[b][:, PACK * s0:PACK * (s0 + P)], 2), planes(by_plane(sig[j][:]), 2),
+                                            planes(by_plane(factor[b])[:, :, s0:s0 + P], 2), MULT)
+
         score = scores(0, (0, 1, 2, 3))
         diff = [held([P, R], F32, "diff%d" % j) for j in range(2)]
         for j in range(2):
-            pos = pos0[:, R * (1 - j):R * (2 - j)]
-            nc.scalar.activation(pos, score[j][:], COPY, scale=signed[0][:, j:j + 1])
-            nc.vector.scalar_tensor_tensor(diff[j][:], score[2 + j][:], signed[1][:, j:j + 1], pos, MULT, ADD)
+            positive = scale_items(0, score, 2 * j)
+            nc.vector.scalar_tensor_tensor(by_plane(diff[j][:]), dealt(score[2 * j + 1][:]), signed[1][:, j:j + 1],
+                                           by_plane(positive[:]), MULT, ADD)
         turned = []
         for j in range(2):
-            sig = held([P, R], F32, "sig%d" % j)
-            nc.scalar.activation(sig[:].rearrange("p (t h m) -> p t h m", t=PACK, h=2),
-                                 diff[j][:].rearrange("p (h t m) -> p t h m", t=PACK, h=2), SIGMOID)
+            sig = held([P, R], F32, "sig0_%d" % j, "sig%d" % j)
+            nc.scalar.activation(sig[:], diff[j][:], SIGMOID)
             turn = bank(4 + j, "sig_turned%d" % j)
             for t in range(PACK):
                 nc.tensor.transpose(turn[:, P * t:P * (t + 1)], sig[:, P * t:P * (t + 1)], ident[:])
             turned.append(turn)
-
-        def pack_xm(b, tag):
-            packed = held([P, PACK * D], BF16, "xm_packed%d" % b, tag)
-            for k in range(4):
-                nc.scalar.copy(woven(packed[:, PACK * P * k:PACK * P * (k + 1)]), planes(xm_raw[b][:, :, P * k:P * (k + 1)]))
-                quantize(xm_r[b], E4M3, packed, P * k, P * (k + 1))
-
-        def weigh(b, sig):
-            by_plane = factor[b].rearrange("p (t s) -> p t s", t=PACK)
-            for j in range(2):
-                for half in (1, 0):
-                    s0 = 256 * half + P * j
-                    nc.vector.tensor_tensor(woven(h_packed[b][:, PACK * s0:PACK * (s0 + P)]),
-                                            planes(sig[j][:].rearrange("p (t s) -> p t s", t=PACK)),
-                                            planes(by_plane[:, :, s0:s0 + P]), MULT)
-
         weigh(0, turned)
+        xm0_packed = held([P, PACK * D], BF16, "xm0_packed", "diff1")
+        for k in range(4):
+            weave(xm0_packed[:, N * k:N * (k + 1)], xm_raw[0], k)
+        quantize(xm_r[0], E4M3, xm0_packed[:, 0:N], 0, P)
         for k in (2, 0, 3, 1):
-            quantize(h_r[0], E5M2, h_packed[0], P * k, P * (k + 1))
-        pack_xm(0, "diff1")
+            quantize(h_r[0], E5M2, h_packed[0][:, N * k:N * (k + 1)], P * k, P * (k + 1))
+        for c0, c1 in ((P, 2 * P), (2 * P, D)):
+            quantize(xm_r[0], E4M3, xm0_packed[:, PACK * c0:PACK * c1], c0, c1)
 
         def table_gradient(b, banks):
             tiles = [bank(banks[j], "dw%d_%d" % (b, j)) for j in range(4)]
@@ -202,42 +209,55 @@ def tile_attend_gbpr_wx_ts_kernel(tc, xT, wT, wt, ts, xm, offs, out_0, out_1):
 
         dw0 = table_gradient(0, (0, 1, 2, 3))
 
-        place(0, [0], dw0, "x0_half0")
+        place(0, [0], dw0, "scaled0_0")
+
+        def turn_w(b, banks, tag):
+            out = held([P, PACK * K], BF16, "w_turned%d" % b, tag)
+            for g in range(2):
+                turn = bank(banks[g], "w_turn%d_%d" % (b, g))
+                for c in range(4):
+                    words = w_planes[b][:, 2 * g + c // 2, :].bitcast(F32)
+                    nc.tensor.transpose(turn[:, P * c:P * (c + 1)], words[:, c % 2::2], ident[:])
+                nc.scalar.copy(out[:].bitcast(F32).rearrange("s (p g c) -> s g p c", g=2, c=4)[:, g],
+                               turn[:].rearrange("s (c p) -> s p c", c=4))
+            return out
+
+        w_i = [mx_operand("w_i%d" % b) for b in range(B)]
+        quantize(w_i[0], E4M3, turn_w(0, (7, 6), "w0_first")[:])
 
         for t in range(PACK):
             gather(1, t)
         x1_packed = held([P, PACK * R], BF16, "x1_packed", "sig1")
-        for h in range(2):
-            dealt = x1_packed[:, 2 * R * h:2 * R * (h + 1)].rearrange("p (t m j) -> p m j t", t=PACK, j=PACK)
-            for c in range(2):
-                r0 = 256 * h + P * c
-                nc.scalar.copy(dealt[:, 32 * c:32 * (c + 1)], x1_raw[:, :, r0:r0 + P].rearrange("p j (m t) -> p m j t", t=PACK))
-        quantize(x_d[1], E4M3, x1_packed)
-        pack_w(1)
-        place(0, [1], dw0, "w_packed1")
+        for k in range(4):
+            weave(x1_packed[:, N * k:N * (k + 1)], x1_raw, k)
+        quantize(x_d[1], E4M3, x1_packed[:])
+        w1_packed = held([P, PACK * N], BF16, "w1_packed")
+        for c in range(4):
+            weave(w1_packed[:, N * c:N * (c + 1)], w_planes[1], 2 * (c % 2) + c // 2)
+        quantize(w_d[1], E4M3, w1_packed[:])
+        place(0, [1], dw0, "w1_packed")
         place(0, [2], dw0, "x0_half1")
         score = scores(1, (4, 5, 6, 7))
-        scaled = [held([P, R], F32, "scaled%d" % k) for k in range(4)]
-        for k in (0, 2, 1, 3):
-            nc.scalar.activation(scaled[k][:].rearrange("p (t h m) -> p t h m", t=PACK, h=2),
-                                 score[k][:].rearrange("p (h t m) -> p t h m", t=PACK, h=2), COPY,
-                                 scale=signed[k // 2][:, 2 + k % 2:3 + k % 2])
+        scaled = [scale_items(1, score, c) for c in range(4)]
         sig1 = []
         for j in range(2):
-            summed = bank(4 + j, "summed%d" % j)
+            summed = bank(4 + 2 * j, "summed%d" % j)
             for t in range(PACK):
                 for half in range(2):
-                    nc.tensor.matmul(summed[:, P * t:P * (t + 1)], scaled[2 * half + j][:, P * t:P * (t + 1)], ident[:],
+                    nc.tensor.matmul(summed[:, P * t:P * (t + 1)], scaled[2 * j + half][:, P * t:P * (t + 1)], ident[:],
                                      start=(half == 0), stop=(half == 1), is_transpose=True)
             sig = held([P, R], F32, "sig1_%d" % j, "sig%d" % j)
             nc.scalar.activation(sig[:], summed[:], SIGMOID)
             sig1.append(sig)
         weigh(1, sig1)
-        quantize(h_r[1], E5M2, h_packed[1])
+        quantize(h_r[1], E5M2, h_packed[1][:])
         place(0, [3], dw0, "factor1")
-        pack_xm(1, "xm_r0_codes")
-        dw1 = table_gradient(1, (6, 7, 4, 5))
-        place(1, [0], dw1, "x0_half0")
+        xm1_packed = held([P, PACK * D], BF16, "xm1_packed", "xm_r0_codes")
+        for k in range(4):
+            weave(xm1_packed[:, N * k:N * (k + 1)], xm_raw[1], k)
+        quantize(xm_r[1], E4M3, xm1_packed[:])
+        dw1 = table_gradient(1, (5, 7, 4, 6))
+        place(1, [0], dw1, "scaled0_0")
         place(1, [1], dw1, "x0_half1")
 
         def turn_h(b, banks):
@@ -251,18 +271,6 @@ def tile_attend_gbpr_wx_ts_kernel(tc, xT, wT, wt, ts, xm, offs, out_0, out_1):
                                turn[:].bitcast(BF16).rearrange("s (t p e) -> s p e t", t=PACK, e=2))
             return out
 
-        def turn_w(b, banks):
-            out = held([P, PACK * K], BF16, "w_turned%d" % b)
-            for g in range(2):
-                turn = bank(banks[g], "w_turn%d_%d" % (b, g))
-                for c in range(4):
-                    words = w_planes[b][:, 2 * g + c // 2, :].bitcast(F32)
-                    nc.tensor.transpose(turn[:, P * c:P * (c + 1)], words[:, c % 2::2], ident[:])
-                nc.scalar.copy(out[:].bitcast(F32).rearrange("s (p g c) -> s g p c", g=2, c=4)[:, g],
-                               turn[:].rearrange("s (c p) -> s p c", c=4))
-            return out
-
-        w_i = [mx_operand("w_i%d" % b) for b in range(B)]
         h_i = [mx_operand("h_i%d" % b) for b in range(B)]
 
         def row_gradient(b, banks, tags):
@@ -273,12 +281,12 @@ def tile_attend_gbpr_wx_ts_kernel(tc, xT, wT, wt, ts, xm, offs, out_0, out_1):
                     gx = bank(banks[j], "gx%d_%d" % (b, j))
                     product(gx, h_i[b], E5M2, j, w_i[b], E4M3)
                     nc.scalar.copy(staged[:, a, :], gx[:])
-                nc.sync.dma_start(out=out_1[b, 2 * P * g:2 * P * (g + 1), :].rearrange("(a m) d -> m a d", m=P), in_=staged[:])
+                nc.scalar.dma_start(out=out_1[b, 2 * P * g:2 * P * (g + 1), :].rearrange("(a m) d -> m a d", m=P), in_=staged[:])
 
-        quantize(w_i[0], E4M3, turn_w(0, (0, 2)))
-        quantize(h_i[0], E5M2, turn_h(0, (0, 2)))
-        quantize(w_i[1], E4M3, turn_w(1, (0, 1)))
-        quantize(h_i[1], E5M2, turn_h(1, (2, 3)))
-        place(1, [2, 3], dw1, "h_turned1")
-        row_gradient(0, (0, 1, 2, 3), ("xm_raw0", "xm_raw1"))
-        row_gradient(1, (0, 1, 2, 3), ("x1_raw", "ts_row"))
+        quantize(h_i[0], E5M2, turn_h(0, (0, 2))[:])
+        row_gradient(0, (1, 0, 2, 1), ("xm_raw0", "x1_raw"))
+        quantize(w_i[1], E4M3, turn_w(1, (0, 2), "w_turned1")[:])
+        quantize(h_i[1], E5M2, turn_h(1, (3, 1))[:])
+        place(1, [2], dw1, "w_turned1")
+        place(1, [3], dw1, "h_turned1")
+        row_gradient(1, (0, 2, 3, 1), ("xm_raw1", "ts_row"))

@@ -54,11 +54,10 @@ def tile_attend_gbpr_wx_ts_kernel(tc, xT, wT, wt, ts, xm, offs, out_0, out_1):
         group_offsets = [offsets[:, b * (N // 16):(b + 1) * (N // 16)] for b in range(B)]
 
         row_weight = held([P, B, PACK], F32, "row_weight")
-        nc.sync.dma_start(out=row_weight[:], in_=wt.rearrange("b (p t) o -> p b (t o)", t=PACK))
+        nc.scalar.dma_start(out=row_weight[:], in_=wt.rearrange("b (p t) o -> p b (t o)", t=PACK))
         ts_row = held([P, T], F32, "ts_row")
-        nc.sync.dma_start(out=ts_row[0:32, :], in_=ts[0:32, :])
-        nc.vector.memset(ts_row[32:64, :], 0.0)
-        nc.gpsimd.memset(ts_row[64:128, :], 0.0)
+        nc.sync.dma_start(out=ts_row[P - 1:P, :], in_=ts[0:1, :])
+        nc.vector.memset(ts_row[0:P - 1, :], 0.0)
 
         w_rows = wT.rearrange("(p t) c -> t p c", t=PACK)
         w_plane = [held([P, T], F32, "w_plane%d" % t) for t in range(PACK)]
@@ -99,7 +98,7 @@ def tile_attend_gbpr_wx_ts_kernel(tc, xT, wT, wt, ts, xm, offs, out_0, out_1):
                     c0 = N * b + 256 * half + P * j
                     nc.tensor.transpose(turned[:, P * (2 * b + j):P * (2 * b + j + 1)], ts_listed[:, c0:c0 + P], ident[:])
             col = held([P, 2 * B], F32, "signed%d" % half)
-            nc.scalar.activation(col[:], turned[:].rearrange("p (k c) -> p k c", c=P)[:, :, 0], COPY, scale=sign)
+            nc.scalar.activation(col[:], turned[:].rearrange("p (k c) -> p k c", c=P)[:, :, P - 1], COPY, scale=sign)
             signed.append(col)
 
         for b in range(B):

@@ -9,6 +9,7 @@ FLOPS = 3 * 2 * B * N * D * R
 F32 = mybir.dt.float32
 BF16 = mybir.dt.bfloat16
 U32 = mybir.dt.uint32
+I32 = mybir.dt.int32
 U16 = mybir.dt.uint16
 U8 = mybir.dt.uint8
 E4M3 = mybir.dt.float8_e4m3fn_x4
@@ -57,15 +58,15 @@ def tile_attend_gbpr_wx_ts_kernel(tc, xT, wT, wt, ts, xm, offs, out_0, out_1):
         nc.scalar.dma_start(out=row_weight[:], in_=wt.rearrange("b (p t) o -> p b (t o)", t=PACK))
         ts_row = held([P, T], F32, "ts_row")
         nc.sync.dma_start(out=ts_row[P - 1:P, :], in_=ts[0:1, :])
-        nc.vector.memset(ts_row[0:P - 1, :], 0.0)
+        nc.vector.memset(ts_row[0:P - 1, :].bitcast(I32), 0)
 
         w_rows = wT.rearrange("(p t) c -> t p c", t=PACK)
         w_plane = [held([P, T], F32, "w_plane%d" % t) for t in range(PACK)]
         x0_half = [held([P, PACK, R // 2], F32, "x0_half%d" % h) for h in range(2)]
         x0_rows = xT[0].rearrange("(p j) (h r) -> h p j r", j=PACK, h=2)
-        for t in range(PACK):
-            nc.sync.dma_start(out=w_plane[t][:], in_=w_rows[t])
         for h in range(2):
+            for t in ((0, 1, 2), (3,))[h]:
+                nc.sync.dma_start(out=w_plane[t][:], in_=w_rows[t])
             nc.sync.dma_start(out=x0_half[h][:], in_=x0_rows[h])
         xm_raw = [held([P, PACK, D], F32, "xm_raw%d" % b) for b in range(B)]
         x1_raw = held([P, PACK, R], F32, "x1_raw")
@@ -81,12 +82,27 @@ def tile_attend_gbpr_wx_ts_kernel(tc, xT, wT, wt, ts, xm, offs, out_0, out_1):
         for j in range(PACK):
             nc.gpsimd.memset(window[j][:], 0.0)
 
-        stretch = 2 * N
-        work = held([P, 3 * stretch + 2 * PACK * N], BF16, "work")
+        def woven(packed, run=4):
+            return packed.rearrange("p (c i t) -> p c t i", i=run, t=PACK)
+
+        def planes(ap, run=4):
+            return ap.rearrange("p t (c i) -> p c t i", i=run)
+
+        def by_plane(flat):
+            return flat.rearrange("p (t c) -> p t c", t=PACK)
+
+        def dealt(rows):
+            return rows.rearrange("p (m t) -> p t m", t=PACK)
+
+        def weave(packed, source, k, engine_copy=nc.scalar.copy):
+            engine_copy(woven(packed), planes(source[:, :, P * k:P * (k + 1)]))
+
+        stretch = 5 * N // 2
+        meet = 3 * stretch + N // 2
+        work = held([P, meet + N // 2 + PACK * D], BF16, "work")
+
         w0_planes = held([P, PACK, N], BF16, "w0_planes")
         w_planes = [w0_planes[:], work[:, 0:PACK * stretch].rearrange("p (t c) -> p t c", t=PACK)[:, :, 0:N]]
-        factor1 = held([P, PACK * N], F32, "factor1")
-        factor = [work[:, 3 * stretch:].bitcast(F32), factor1[:]]
 
         ts_listed = held([P, B * N], F32, "ts_listed")
         nc.vector.tensor_copy(ts_listed[:], ts_row[:].indirect(offsets[:]))
@@ -101,53 +117,49 @@ def tile_attend_gbpr_wx_ts_kernel(tc, xT, wT, wt, ts, xm, offs, out_0, out_1):
             nc.scalar.activation(col[:], turned[:].rearrange("p (k c) -> p k c", c=P)[:, :, P - 1], COPY, scale=sign)
             signed.append(col)
 
-        for b in range(B):
-            spread = bank(6 + b, "ts_spread%d" % b)
+        def gather(b, t):
+            nc.vector.tensor_copy(w_planes[b][:, t, :], w_plane[t][:].indirect(group_offsets[b]))
+
+        x_d = [mx_operand("x_d0")]
+        x0_packed = [held([P, 2 * R], BF16, "x0_packed%d" % h) for h in range(2)]
+        for k in range(2):
+            weave(x0_packed[0][:, N * k:N * (k + 1)], x0_half[0], k)
+
+        def spread_scales(b, k_bank):
+            spread = bank(k_bank, "ts_spread%d" % b)
             for half in range(2):
                 for j in range(2):
                     k = 2 * half + j
                     nc.tensor.transpose(spread[:, P * k:P * (k + 1)],
                                         signed[half][:, 2 * b + j:2 * b + j + 1].to_broadcast([P, P]), ident[:])
-            for t in range(PACK):
-                nc.scalar.activation(factor[b][:, N * t:N * (t + 1)], spread[:], COPY, scale=row_weight[:, b, t:t + 1])
+            return spread
 
-        def woven(packed, run=4):
-            return packed.rearrange("p (c i t) -> p c t i", i=run, t=PACK)
-
-        def planes(ap, run=4):
-            return ap.rearrange("p t (c i) -> p c t i", i=run)
-
-        def by_plane(flat):
-            return flat.rearrange("p (t c) -> p t c", t=PACK)
-
-        def dealt(rows):
-            return rows.rearrange("p (m t) -> p t m", t=PACK)
-
-        def gather(b, t):
-            nc.vector.tensor_copy(w_planes[b][:, t, :], w_plane[t][:].indirect(group_offsets[b]))
-
-        x_d = [mx_operand("x_d%d" % b) for b in range(B)]
-
-        def weave(packed, source, k):
-            nc.scalar.copy(woven(packed), planes(source[:, :, P * k:P * (k + 1)]))
-
+        factor = [held([P, PACK * N], F32, "factor0")]
+        spread0 = spread_scales(0, 4)
         for t in range(PACK):
+            nc.scalar.activation(factor[0][:, N * t:N * (t + 1)], spread0[:], COPY, scale=row_weight[:, 0, t:t + 1])
+        spread1 = held([P, N], F32, "spread1")
+        nc.scalar.copy(spread1[:], spread_scales(1, 5)[:])
+
+        for t in range(PACK - 1):
             gather(0, t)
-        x0_packed = held([P, PACK * R], BF16, "x0_packed")
-        w0_first = held([P, 2 * N], BF16, "w0_first")
-        for h in range(2):
-            x_half = x0_packed[:, 2 * R * h:2 * R * (h + 1)]
-            nc.vector.tensor_copy(woven(x_half), planes(x0_half[h][:]))
-            quantize(x_d[0], E4M3, x_half, h * R // 2, (h + 1) * R // 2)
-        w_d = [mx_operand("w_d0", "x0_half1"), mx_operand("w_d1")]
-        for j, packed in enumerate((w0_first[:], work[:, 2 * stretch:3 * stretch])):
+            gather(1, t)
+        quantize(x_d[0], E4M3, x0_packed[0][:], 0, R // 2)
+        for k in (0, 2, 1, 3):
+            nc.vector.tensor_copy(w_planes[0][:, 3, P * k:P * (k + 1)], w_plane[3][:].indirect(offsets[:, 8 * k:8 * (k + 1)]))
+        nc.vector.tensor_copy(woven(x0_packed[1][:]), planes(x0_half[1][:]))
+        quantize(x_d[0], E4M3, x0_packed[1][:], R // 2, R)
+        w_d = [mx_operand("w_d%d" % b) for b in range(B)]
+        for j, packed in enumerate((work[:, meet - 2 * N:meet], work[:, meet:meet + 2 * N])):
             for half in range(2):
                 weave(packed[:, N * half:N * (half + 1)], w_planes[0], 2 * half + j)
             quantize(w_d[0], E4M3, packed, 2 * P * j, 2 * P * (j + 1))
+        for half in range(2):
+            nc.vector.tensor_copy(w_planes[1][:, 3, 256 * half:256 * (half + 1)],
+                                  w_plane[3][:].indirect(offsets[:, 32 + 16 * half:48 + 16 * half]))
 
         h_packed = [held([P, PACK * N], BF16, "h_packed%d" % b) for b in range(B)]
         h_r = [mx_operand("h_r%d" % b) for b in range(B)]
-        xm_r = [mx_operand("xm_r%d" % b) for b in range(B)]
 
         def scores(b, banks):
             tiles = [bank(banks[c], "score%d_%d" % (b, c)) for c in range(4)]
@@ -160,13 +172,6 @@ def tile_attend_gbpr_wx_ts_kernel(tc, xT, wT, wt, ts, xm, offs, out_0, out_1):
             k = 2 * b + c // 2
             nc.scalar.activation(by_plane(out[:]), dealt(score[c][:]), COPY, scale=signed[c % 2][:, k:k + 1])
             return out
-
-        def weigh(b, sig):
-            for j in range(2):
-                for half in (1, 0):
-                    s0 = 256 * half + P * j
-                    nc.vector.tensor_tensor(woven(h_packed[b][:, PACK * s0:PACK * (s0 + P)], 2), planes(by_plane(sig[j][:]), 2),
-                                            planes(by_plane(factor[b])[:, :, s0:s0 + P], 2), MULT)
 
         score = scores(0, (0, 1, 2, 3))
         diff = [held([P, R], F32, "diff%d" % j) for j in range(2)]
@@ -182,36 +187,40 @@ def tile_attend_gbpr_wx_ts_kernel(tc, xT, wT, wt, ts, xm, offs, out_0, out_1):
             for t in range(PACK):
                 nc.tensor.transpose(turn[:, P * t:P * (t + 1)], sig[:, P * t:P * (t + 1)], ident[:])
             turned.append(turn)
-        weigh(0, turned)
-        xm0_packed = held([P, PACK * D], BF16, "xm0_packed", "diff1")
-        for k in range(4):
-            weave(xm0_packed[:, N * k:N * (k + 1)], xm_raw[0], k)
-        quantize(xm_r[0], E4M3, xm0_packed[:, 0:N], 0, P)
-        for k in (2, 0, 3, 1):
+
+        for j in range(2):
+            for half in (1, 0):
+                s0 = 256 * half + P * j
+                nc.vector.tensor_tensor(woven(h_packed[0][:, PACK * s0:PACK * (s0 + P)], 2), planes(by_plane(turned[j][:]), 2),
+                                        planes(by_plane(factor[0][:])[:, :, s0:s0 + P], 2), MULT)
+
+        def weave_on_gpsimd(packed, source):
+            nc.gpsimd.tensor_scalar(packed.rearrange("p (c t) -> p c t", t=PACK), source.rearrange("p t c -> p c t"), 1.0, 0.0, MULT, ADD)
+
+        xm0_packed = work[:, meet + N // 2:]
+        weave_on_gpsimd(xm0_packed, xm_raw[0][:])
+        xm_r = [mx_operand("xm_r0", "factor0")]
+        for k in (2, 0, 3):
             quantize(h_r[0], E5M2, h_packed[0][:, N * k:N * (k + 1)], P * k, P * (k + 1))
+        quantize(xm_r[0], E4M3, xm0_packed[:, 0:N], 0, P)
+        quantize(h_r[0], E5M2, h_packed[0][:, N:2 * N], P, 2 * P)
         for c0, c1 in ((P, 2 * P), (2 * P, D)):
             quantize(xm_r[0], E4M3, xm0_packed[:, PACK * c0:PACK * c1], c0, c1)
 
-        def table_gradient(b, banks):
-            tiles = [bank(banks[j], "dw%d_%d" % (b, j)) for j in range(4)]
-            for j in range(4):
-                product(tiles[j], xm_r[b], E4M3, j, h_r[b], E5M2)
-            return tiles
+        def table_gradient(b, j, k):
+            tile = bank(k, "dw%d_%d" % (b, j))
+            product(tile, xm_r[b], E4M3, j, h_r[b], E5M2)
+            return tile
 
-        def place(b, tiles, dw, tag):
-            staged = held([P, len(tiles), N], F32, "dw_staged%d_%d" % (b, tiles[0]), tag)
-            for a, j in enumerate(tiles):
-                nc.scalar.copy(staged[:, a, :], dw[j][:])
-                nc.vector.tensor_copy(window[j][:].indirect(group_offsets[b]), staged[:, a, :])
-                if b == B - 1:
-                    nc.sync.dma_start(out=out_0[P * j:P * (j + 1), :], in_=window[j][:])
+        def place(b, j, dw, tag):
+            staged = held([P, N], F32, "dw_staged%d_%d" % (b, j), tag)
+            nc.scalar.copy(staged[:], dw[:])
+            nc.vector.tensor_copy(window[j][:].indirect(group_offsets[b]), staged[:])
+            if b == B - 1:
+                nc.sync.dma_start(out=out_0[P * j:P * (j + 1), :], in_=window[j][:])
 
-        dw0 = table_gradient(0, (0, 1, 2, 3))
-
-        place(0, [0], dw0, "scaled0_0")
-
-        def turn_w(b, banks, tag):
-            out = held([P, PACK * K], BF16, "w_turned%d" % b, tag)
+        def turn_w(b, banks):
+            out = held([P, PACK * K], BF16, "w_turned%d" % b)
             for g in range(2):
                 turn = bank(banks[g], "w_turn%d_%d" % (b, g))
                 for c in range(4):
@@ -220,44 +229,6 @@ def tile_attend_gbpr_wx_ts_kernel(tc, xT, wT, wt, ts, xm, offs, out_0, out_1):
                 nc.scalar.copy(out[:].bitcast(F32).rearrange("s (p g c) -> s g p c", g=2, c=4)[:, g],
                                turn[:].rearrange("s (c p) -> s p c", c=4))
             return out
-
-        w_i = [mx_operand("w_i%d" % b) for b in range(B)]
-        quantize(w_i[0], E4M3, turn_w(0, (7, 6), "w0_first")[:])
-
-        for t in range(PACK):
-            gather(1, t)
-        x1_packed = held([P, PACK * R], BF16, "x1_packed", "sig1")
-        for k in range(4):
-            weave(x1_packed[:, N * k:N * (k + 1)], x1_raw, k)
-        quantize(x_d[1], E4M3, x1_packed[:])
-        w1_packed = held([P, PACK * N], BF16, "w1_packed")
-        for c in range(4):
-            weave(w1_packed[:, N * c:N * (c + 1)], w_planes[1], 2 * (c % 2) + c // 2)
-        quantize(w_d[1], E4M3, w1_packed[:])
-        place(0, [1], dw0, "w1_packed")
-        place(0, [2], dw0, "x0_half1")
-        score = scores(1, (4, 5, 6, 7))
-        scaled = [scale_items(1, score, c) for c in range(4)]
-        sig1 = []
-        for j in range(2):
-            summed = bank(4 + 2 * j, "summed%d" % j)
-            for t in range(PACK):
-                for half in range(2):
-                    nc.tensor.matmul(summed[:, P * t:P * (t + 1)], scaled[2 * j + half][:, P * t:P * (t + 1)], ident[:],
-                                     start=(half == 0), stop=(half == 1), is_transpose=True)
-            sig = held([P, R], F32, "sig1_%d" % j, "sig%d" % j)
-            nc.scalar.activation(sig[:], summed[:], SIGMOID)
-            sig1.append(sig)
-        weigh(1, sig1)
-        quantize(h_r[1], E5M2, h_packed[1][:])
-        place(0, [3], dw0, "factor1")
-        xm1_packed = held([P, PACK * D], BF16, "xm1_packed", "xm_r0_codes")
-        for k in range(4):
-            weave(xm1_packed[:, N * k:N * (k + 1)], xm_raw[1], k)
-        quantize(xm_r[1], E4M3, xm1_packed[:])
-        dw1 = table_gradient(1, (5, 7, 4, 6))
-        place(1, [0], dw1, "scaled0_0")
-        place(1, [1], dw1, "x0_half1")
 
         def turn_h(b, banks):
             words = h_packed[b][:].bitcast(F32)
@@ -270,7 +241,8 @@ def tile_attend_gbpr_wx_ts_kernel(tc, xT, wT, wt, ts, xm, offs, out_0, out_1):
                                turn[:].bitcast(BF16).rearrange("s (t p e) -> s p e t", t=PACK, e=2))
             return out
 
-        h_i = [mx_operand("h_i%d" % b) for b in range(B)]
+        h_i = []
+        w_i = []
 
         def row_gradient(b, banks, tags):
             for g in range(2):
@@ -282,10 +254,58 @@ def tile_attend_gbpr_wx_ts_kernel(tc, xT, wT, wt, ts, xm, offs, out_0, out_1):
                     nc.scalar.copy(staged[:, a, :], gx[:])
                 nc.scalar.dma_start(out=out_1[b, 2 * P * g:2 * P * (g + 1), :].rearrange("(a m) d -> m a d", m=P), in_=staged[:])
 
-        quantize(h_i[0], E5M2, turn_h(0, (0, 2))[:])
-        row_gradient(0, (1, 0, 2, 1), ("xm_raw0", "x1_raw"))
-        quantize(w_i[1], E4M3, turn_w(1, (0, 2), "w_turned1")[:])
-        quantize(h_i[1], E5M2, turn_h(1, (3, 1))[:])
-        place(1, [2], dw1, "w_turned1")
-        place(1, [3], dw1, "h_turned1")
-        row_gradient(1, (0, 2, 3, 1), ("xm_raw1", "ts_row"))
+        w0_turned = turn_w(0, (6, 7))
+        x1_packed = held([P, PACK * R], BF16, "x1_packed")
+        weave_on_gpsimd(x1_packed[:, 0:2 * N], x1_raw[:, :, 0:R // 2])
+        for k in (2, 3):
+            weave(x1_packed[:, N * k:N * (k + 1)], x1_raw, k)
+        w1_packed = held([P, PACK * N], BF16, "w1_packed", "diff0")
+        for c in range(4):
+            weave(w1_packed[:, N * c:N * (c + 1)], w_planes[1], 2 * (c % 2) + c // 2)
+        x_d.append(mx_operand("x_d1", "sig1"))
+        quantize(x_d[1], E4M3, x1_packed[:])
+        quantize(w_d[1], E4M3, w1_packed[:])
+        place(0, 0, table_gradient(0, 0, 0), "diff1")
+        place(0, 1, table_gradient(0, 1, 1), "scaled0_0")
+        xm1_packed = held([P, PACK * D], BF16, "xm1_packed", "diff0")
+        weave_on_gpsimd(xm1_packed[:], xm_raw[1][:])
+        factor.append(held([P, PACK * N], F32, "factor1", "x1_packed"))
+        for t in range(PACK):
+            nc.gpsimd.tensor_scalar(factor[1][:].rearrange("p (c t i) -> p t c i", t=PACK, i=4)[:, t],
+                                    spread1[:].rearrange("p (c i) -> p c i", i=4), row_weight[:, 1, t:t + 1], 0.0, MULT, ADD)
+        score = scores(1, (4, 5, 6, 7))
+        scaled = [scale_items(1, score, c) for c in range(4)]
+        place(0, 2, table_gradient(0, 2, 2), "scaled0_2")
+        place(0, 3, table_gradient(0, 3, 3), "x0_packed0")
+        for j in range(2):
+            summed = bank(4 + 2 * j, "summed%d" % j)
+            for t in range(PACK):
+                for half in range(2):
+                    nc.tensor.matmul(summed[:, P * t:P * (t + 1)], scaled[2 * j + half][:, P * t:P * (t + 1)], ident[:],
+                                     start=(half == 0), stop=(half == 1), is_transpose=True)
+            sig = held([P, R], F32, "sig1_%d" % j, "sig%d" % j)
+            nc.scalar.activation(sig[:].rearrange("p (s t) -> p s t", t=PACK), summed[:].rearrange("p (t s) -> p s t", t=PACK), SIGMOID)
+            for half in range(2):
+                cols = slice(PACK * (256 * half + P * j), PACK * (256 * half + P * (j + 1)))
+                nc.gpsimd.tensor_tensor(h_packed[1][:, cols].rearrange("p (c i t) -> p c i t", i=4, t=PACK),
+                                        sig[:].rearrange("p (c i t) -> p c i t", i=4, t=PACK),
+                                        factor[1][:, cols].rearrange("p (c t i) -> p c i t", i=4, t=PACK), MULT)
+        h0_turned = turn_h(0, (5, 7))
+        w1_turned = turn_w(1, (2, 3))
+        xm_r.append(mx_operand("xm_r1", "sig0"))
+        quantize(xm_r[1], E4M3, xm1_packed[:])
+        quantize(h_r[1], E5M2, h_packed[1][:])
+        late = held([P, 2 * K], U32, "late_codes", "x1_packed")
+        w_i.append((late[:, 0:K], held([P, K], U8, "w_i0_scales")))
+        h_i.append((late[:, K:2 * K], held([P, K], U8, "h_i0_scales")))
+        w_i.append(mx_operand("w_i1", "sig1"))
+        quantize(w_i[0], E4M3, w0_turned[:])
+        quantize(h_i[0], E5M2, h0_turned[:])
+        quantize(w_i[1], E4M3, w1_turned[:])
+        place(1, 0, table_gradient(1, 0, 0), "diff1")
+        h_i.append(mx_operand("h_i1"))
+        quantize(h_i[1], E5M2, turn_h(1, (4, 6))[:])
+        row_gradient(0, (1, 5, 7, 2), ("xm_raw0", "x1_raw"))
+        for j in range(1, 4):
+            place(1, j, table_gradient(1, j, (6, 4, 2)[j - 1]), "scaled1_%d" % j)
+        row_gradient(1, (3, 0, 1, 5), ("xm_raw1", "ts_row"))

@@ -99,7 +99,7 @@ def tile_attend_gbpr_wx_ts_kernel(tc, xT, wT, wt, ts, xm, offs, out_0, out_1):
 
         stretch = 5 * N // 2
         meet = 3 * stretch + N // 2
-        work = held([P, meet + N // 2 + PACK * D], BF16, "work")
+        work = held([P, meet + 2 * N], BF16, "work")
 
         w0_planes = held([P, PACK, N], BF16, "w0_planes")
         w_planes = [w0_planes[:], work[:, 0:PACK * stretch].rearrange("p (t c) -> p t c", t=PACK)[:, :, 0:N]]
@@ -138,8 +138,6 @@ def tile_attend_gbpr_wx_ts_kernel(tc, xT, wT, wt, ts, xm, offs, out_0, out_1):
         spread0 = spread_scales(0, 4)
         for t in range(PACK):
             nc.scalar.activation(factor[0][:, N * t:N * (t + 1)], spread0[:], COPY, scale=row_weight[:, 0, t:t + 1])
-        spread1 = held([P, N], F32, "spread1")
-        nc.scalar.copy(spread1[:], spread_scales(1, 5)[:])
 
         for t in range(PACK - 1):
             gather(0, t)
@@ -158,25 +156,35 @@ def tile_attend_gbpr_wx_ts_kernel(tc, xT, wT, wt, ts, xm, offs, out_0, out_1):
             nc.vector.tensor_copy(w_planes[1][:, 3, 256 * half:256 * (half + 1)],
                                   w_plane[3][:].indirect(offsets[:, 32 + 16 * half:48 + 16 * half]))
 
+        w_turned = [held([P, PACK * K], BF16, "w_turned0"), held([P, PACK * K], BF16, "w_turned1", "x0_half0")]
+
+        def turn_w(b, g, k_bank):
+            turn = bank(k_bank, "w_turn%d_%d" % (b, g))
+            for c in range(4):
+                words = w_planes[b][:, 2 * g + c // 2, :].bitcast(F32)
+                nc.tensor.transpose(turn[:, P * c:P * (c + 1)], words[:, c % 2::2], ident[:])
+            nc.scalar.copy(w_turned[b][:].bitcast(F32).rearrange("s (p g c) -> s g p c", g=2, c=4)[:, g],
+                           turn[:].rearrange("s (c p) -> s p c", c=4))
+
+        turn_w(0, 0, 6)
+        turn_w(1, 0, 5)
+        turn_w(0, 1, 7)
+
         h_packed = [held([P, PACK * N], BF16, "h_packed%d" % b) for b in range(B)]
         h_r = [mx_operand("h_r%d" % b) for b in range(B)]
-
-        def scores(b, banks):
-            tiles = [bank(banks[c], "score%d_%d" % (b, c)) for c in range(4)]
-            for c in range(4):
-                product(tiles[c], w_d[b], E4M3, c, x_d[b], E4M3)
-            return tiles
 
         def scale_items(b, score, c):
             out = held([P, R], F32, "scaled%d_%d" % (b, c))
             k = 2 * b + c // 2
-            nc.scalar.activation(by_plane(out[:]), dealt(score[c][:]), COPY, scale=signed[c % 2][:, k:k + 1])
+            nc.scalar.activation(by_plane(out[:]), dealt(score[:]), COPY, scale=signed[c % 2][:, k:k + 1])
             return out
 
-        score = scores(0, (0, 1, 2, 3))
+        score = [bank(c, "score0_%d" % c) for c in range(4)]
+        for c in range(4):
+            product(score[c], w_d[0], E4M3, c, x_d[0], E4M3)
         diff = [held([P, R], F32, "diff%d" % j) for j in range(2)]
         for j in range(2):
-            positive = scale_items(0, score, 2 * j)
+            positive = scale_items(0, score[2 * j], 2 * j)
             nc.vector.scalar_tensor_tensor(by_plane(diff[j][:]), dealt(score[2 * j + 1][:]), signed[1][:, j:j + 1],
                                            by_plane(positive[:]), MULT, ADD)
         turned = []
@@ -197,38 +205,31 @@ def tile_attend_gbpr_wx_ts_kernel(tc, xT, wT, wt, ts, xm, offs, out_0, out_1):
         def weave_on_gpsimd(packed, source):
             nc.gpsimd.tensor_scalar(packed.rearrange("p (c t) -> p c t", t=PACK), source.rearrange("p t c -> p c t"), 1.0, 0.0, MULT, ADD)
 
-        xm0_packed = work[:, meet + N // 2:]
-        weave_on_gpsimd(xm0_packed, xm_raw[0][:])
+        xm0_packed = [held([P, N], BF16, "xm0_first"), held([P, 3 * N], BF16, "xm0_rest", "scaled0_2")]
+        weave(xm0_packed[0][:], xm_raw[0], 0, nc.vector.tensor_copy)
+        for k in range(1, 4):
+            weave(xm0_packed[1][:, N * (k - 1):N * k], xm_raw[0], k, nc.vector.tensor_copy)
         xm_r = [mx_operand("xm_r0", "factor0")]
         for k in (2, 0, 3):
             quantize(h_r[0], E5M2, h_packed[0][:, N * k:N * (k + 1)], P * k, P * (k + 1))
-        quantize(xm_r[0], E4M3, xm0_packed[:, 0:N], 0, P)
+        quantize(xm_r[0], E4M3, xm0_packed[0][:], 0, P)
         quantize(h_r[0], E5M2, h_packed[0][:, N:2 * N], P, 2 * P)
-        for c0, c1 in ((P, 2 * P), (2 * P, D)):
-            quantize(xm_r[0], E4M3, xm0_packed[:, PACK * c0:PACK * c1], c0, c1)
+        quantize(xm_r[0], E4M3, xm0_packed[1][:, 0:N], P, 2 * P)
+        quantize(xm_r[0], E4M3, xm0_packed[1][:, N:3 * N], 2 * P, D)
 
         def table_gradient(b, j, k):
             tile = bank(k, "dw%d_%d" % (b, j))
             product(tile, xm_r[b], E4M3, j, h_r[b], E5M2)
             return tile
 
-        def place(b, j, dw, tag):
-            staged = held([P, N], F32, "dw_staged%d_%d" % (b, j), tag)
-            nc.scalar.copy(staged[:], dw[:])
-            nc.vector.tensor_copy(window[j][:].indirect(group_offsets[b]), staged[:])
+        def stage(name, tag):
+            return held([P, N], F32, name, tag)
+
+        def place(b, j, dw, staged):
+            nc.scalar.copy(staged, dw[:])
+            nc.vector.tensor_copy(window[j][:].indirect(group_offsets[b]), staged)
             if b == B - 1:
                 nc.sync.dma_start(out=out_0[P * j:P * (j + 1), :], in_=window[j][:])
-
-        def turn_w(b, banks):
-            out = held([P, PACK * K], BF16, "w_turned%d" % b)
-            for g in range(2):
-                turn = bank(banks[g], "w_turn%d_%d" % (b, g))
-                for c in range(4):
-                    words = w_planes[b][:, 2 * g + c // 2, :].bitcast(F32)
-                    nc.tensor.transpose(turn[:, P * c:P * (c + 1)], words[:, c % 2::2], ident[:])
-                nc.scalar.copy(out[:].bitcast(F32).rearrange("s (p g c) -> s g p c", g=2, c=4)[:, g],
-                               turn[:].rearrange("s (c p) -> s p c", c=4))
-            return out
 
         def turn_h(b, banks):
             words = h_packed[b][:].bitcast(F32)
@@ -241,7 +242,6 @@ def tile_attend_gbpr_wx_ts_kernel(tc, xT, wT, wt, ts, xm, offs, out_0, out_1):
                                turn[:].bitcast(BF16).rearrange("s (t p e) -> s p e t", t=PACK, e=2))
             return out
 
-        h_i = []
         w_i = []
 
         def row_gradient(b, banks, tags):
@@ -254,10 +254,8 @@ def tile_attend_gbpr_wx_ts_kernel(tc, xT, wT, wt, ts, xm, offs, out_0, out_1):
                     nc.scalar.copy(staged[:, a, :], gx[:])
                 nc.scalar.dma_start(out=out_1[b, 2 * P * g:2 * P * (g + 1), :].rearrange("(a m) d -> m a d", m=P), in_=staged[:])
 
-        w0_turned = turn_w(0, (6, 7))
         x1_packed = held([P, PACK * R], BF16, "x1_packed")
-        weave_on_gpsimd(x1_packed[:, 0:2 * N], x1_raw[:, :, 0:R // 2])
-        for k in (2, 3):
+        for k in range(4):
             weave(x1_packed[:, N * k:N * (k + 1)], x1_raw, k)
         w1_packed = held([P, PACK * N], BF16, "w1_packed", "diff0")
         for c in range(4):
@@ -265,47 +263,64 @@ def tile_attend_gbpr_wx_ts_kernel(tc, xT, wT, wt, ts, xm, offs, out_0, out_1):
         x_d.append(mx_operand("x_d1", "sig1"))
         quantize(x_d[1], E4M3, x1_packed[:])
         quantize(w_d[1], E4M3, w1_packed[:])
-        place(0, 0, table_gradient(0, 0, 0), "diff1")
-        place(0, 1, table_gradient(0, 1, 1), "scaled0_0")
+        place(0, 0, table_gradient(0, 0, 0), stage("dw_staged0_0", "diff1")[:])
+        turn_w(1, 1, 0)
         xm1_packed = held([P, PACK * D], BF16, "xm1_packed", "diff0")
         weave_on_gpsimd(xm1_packed[:], xm_raw[1][:])
-        factor.append(held([P, PACK * N], F32, "factor1", "x1_packed"))
-        for t in range(PACK):
-            nc.gpsimd.tensor_scalar(factor[1][:].rearrange("p (c t i) -> p t c i", t=PACK, i=4)[:, t],
-                                    spread1[:].rearrange("p (c i) -> p c i", i=4), row_weight[:, 1, t:t + 1], 0.0, MULT, ADD)
-        score = scores(1, (4, 5, 6, 7))
-        scaled = [scale_items(1, score, c) for c in range(4)]
-        place(0, 2, table_gradient(0, 2, 2), "scaled0_2")
-        place(0, 3, table_gradient(0, 3, 3), "x0_packed0")
+        scaled = []
+        for c in range(4):
+            score = bank(4 + c, "score1_%d" % c)
+            product(score, w_d[1], E4M3, c, x_d[1], E4M3)
+            scaled.append(scale_items(1, score, c))
+            if c == 1:
+                place(0, 1, table_gradient(0, 1, 1), stage("dw_staged0_1", "x0_half1")[:])
+        w_codes = held([P, B * K], U32, "w_i_codes", "x0_half1")
+        for b in range(B):
+            w_i.append((w_codes[:, K * b:K * (b + 1)], held([P, K], U8, "w_i%d_scales" % b)))
+            quantize(w_i[b], E4M3, w_turned[b][:])
+        weighted = []
         for j in range(2):
-            summed = bank(4 + 2 * j, "summed%d" % j)
+            summed = bank(4 + j, "summed%d" % j)
             for t in range(PACK):
                 for half in range(2):
                     nc.tensor.matmul(summed[:, P * t:P * (t + 1)], scaled[2 * j + half][:, P * t:P * (t + 1)], ident[:],
                                      start=(half == 0), stop=(half == 1), is_transpose=True)
-            sig = held([P, R], F32, "sig1_%d" % j, "sig%d" % j)
-            nc.scalar.activation(sig[:].rearrange("p (s t) -> p s t", t=PACK), summed[:].rearrange("p (t s) -> p s t", t=PACK), SIGMOID)
-            for half in range(2):
-                cols = slice(PACK * (256 * half + P * j), PACK * (256 * half + P * (j + 1)))
-                nc.gpsimd.tensor_tensor(h_packed[1][:, cols].rearrange("p (c i t) -> p c i t", i=4, t=PACK),
-                                        sig[:].rearrange("p (c i t) -> p c i t", i=4, t=PACK),
-                                        factor[1][:, cols].rearrange("p (c t i) -> p c i t", i=4, t=PACK), MULT)
-        h0_turned = turn_h(0, (5, 7))
-        w1_turned = turn_w(1, (2, 3))
-        xm_r.append(mx_operand("xm_r1", "sig0"))
+            sig = held([P, R], F32, "sig1_%d" % j, "sig0")
+            nc.scalar.activation(sig[:], summed[:], SIGMOID)
+            out = held([P, R], F32, "weighted%d" % j)
+            for t in range(PACK):
+                nc.scalar.activation(out[:, P * t:P * (t + 1)], sig[:, P * t:P * (t + 1)], COPY, scale=row_weight[:, 1, t:t + 1])
+            weighted.append(out)
+            if j == 0:
+                place(0, 2, table_gradient(0, 2, 2), stage("dw_staged0_2", "x0_packed1")[:])
+        xm_r.append(mx_operand("xm_r1", "scaled1_3"))
         quantize(xm_r[1], E4M3, xm1_packed[:])
+        h_slots = held([P, PACK, R], BF16, "h_slots")
+        for j in range(2):
+            back = bank(6 + j, "weighted_turned%d" % j)
+            for t in range(PACK):
+                nc.tensor.transpose(back[:, P * t:P * (t + 1)], weighted[j][:, P * t:P * (t + 1)], ident[:])
+            for half in range(2):
+                nc.scalar.activation(h_slots[:, 2 * half + j, :].rearrange("s (u m e) -> s u m e", u=2, e=2),
+                                     back[:].rearrange("s (u e m) -> s u m e", u=2, e=2), COPY, scale=signed[half][:, 2 + j:3 + j])
+        for j in range(2):
+            turn = bank(4 + j, "h_rows%d" % j)
+            for half in range(2):
+                words = h_slots[:, 2 * half + j, :].bitcast(F32)
+                for u in range(2):
+                    c = 2 * half + u
+                    nc.tensor.transpose(turn[:, P * c:P * (c + 1)], words[:, P * u:P * (u + 1)], ident[:])
+            nc.scalar.copy(h_packed[1][:].bitcast(F32).rearrange("m (h j s u) -> m j h s u", h=2, j=2, u=2)[:, j],
+                           turn[:].rearrange("m (h u s) -> m h s u", h=2, u=2))
         quantize(h_r[1], E5M2, h_packed[1][:])
-        late = held([P, 2 * K], U32, "late_codes", "x1_packed")
-        w_i.append((late[:, 0:K], held([P, K], U8, "w_i0_scales")))
-        h_i.append((late[:, K:2 * K], held([P, K], U8, "h_i0_scales")))
-        w_i.append(mx_operand("w_i1", "sig1"))
-        quantize(w_i[0], E4M3, w0_turned[:])
+        place(0, 3, table_gradient(0, 3, 3), stage("dw_staged0_3", "h_slots")[:])
+        h0_turned = turn_h(0, (4, 5))
+        place(1, 0, table_gradient(1, 0, 1), stage("dw_staged1_0", "scaled1_0")[:])
+        h_i = [mx_operand("h_i%d" % b) for b in range(B)]
         quantize(h_i[0], E5M2, h0_turned[:])
-        quantize(w_i[1], E4M3, w1_turned[:])
-        place(1, 0, table_gradient(1, 0, 0), "diff1")
-        h_i.append(mx_operand("h_i1"))
-        quantize(h_i[1], E5M2, turn_h(1, (4, 6))[:])
-        row_gradient(0, (1, 5, 7, 2), ("xm_raw0", "x1_raw"))
-        for j in range(1, 4):
-            place(1, j, table_gradient(1, j, (6, 4, 2)[j - 1]), "scaled1_%d" % j)
-        row_gradient(1, (3, 0, 1, 5), ("xm_raw1", "ts_row"))
+        place(1, 1, table_gradient(1, 1, 0), stage("dw_staged1_1", "scaled1_1")[:])
+        row_gradient(0, (2, 4, 5, 7), ("xm_raw0", "x1_raw"))
+        quantize(h_i[1], E5M2, turn_h(1, (6, 2))[:])
+        place(1, 2, table_gradient(1, 2, 3), stage("dw_staged1_2", "h_packed1")[:])
+        place(1, 3, table_gradient(1, 3, 0), stage("dw_staged1_3", "h_turned1")[:])
+        row_gradient(1, (1, 6, 4, 5), ("xm_raw1", "ts_row"))

@@ -38,8 +38,8 @@ def tile_attend_gbpr_wx_ts_kernel(tc, xT, wT, wt, ts, xm, offs, out_0, out_1):
         def bank(k, name):
             return ps.tile([P, K], F32, name=name, tag="bank%d" % k)
 
-        def mx_operand(name, tag=None):
-            return held([P, K], U32, name + "_codes", tag), held([P, K], U8, name + "_scales")
+        def mx_operand(name, tag=None, width=K):
+            return held([P, width], U32, name + "_codes", tag), held([P, width], U8, name + "_scales")
 
         def quantize(operand, fmt, src, c0=0, c1=K):
             codes, scales = operand
@@ -205,21 +205,28 @@ def tile_attend_gbpr_wx_ts_kernel(tc, xT, wT, wt, ts, xm, offs, out_0, out_1):
         def weave_on_gpsimd(packed, source):
             nc.gpsimd.tensor_scalar(packed.rearrange("p (c t) -> p c t", t=PACK), source.rearrange("p t c -> p c t"), 1.0, 0.0, MULT, ADD)
 
-        xm0_packed = [held([P, N], BF16, "xm0_first"), held([P, 3 * N], BF16, "xm0_rest", "scaled0_2")]
-        weave(xm0_packed[0][:], xm_raw[0], 0, nc.vector.tensor_copy)
-        for k in range(1, 4):
-            weave(xm0_packed[1][:, N * (k - 1):N * k], xm_raw[0], k, nc.vector.tensor_copy)
-        xm_r = [mx_operand("xm_r0", "factor0")]
+        xm0_first = held([P, N], BF16, "xm0_first")
+        weave(xm0_first[:], xm_raw[0], 0, nc.vector.tensor_copy)
+        w_i = [mx_operand("w_i0", "scaled0_0")]
+        quantize(w_i[0], E4M3, w_turned[0][:])
+        behind_sums = held([P, 3 * N + PACK * R], BF16, "behind_sums", "scaled0_2")
+        xm0_packed = [xm0_first, behind_sums[:, 0:3 * N]]
+        x1_packed = behind_sums[:, 3 * N:]
+        weave_on_gpsimd(xm0_packed[1], xm_raw[0][:, :, P:D])
+        weave_on_gpsimd(x1_packed[:, 0:N], x1_raw[:, :, 0:P])
+        xm0_r = mx_operand("xm_r0", "factor0")
+        xm_blocks = [[(xm0_r, j) for j in range(4)]]
         for k in (2, 0, 3):
             quantize(h_r[0], E5M2, h_packed[0][:, N * k:N * (k + 1)], P * k, P * (k + 1))
-        quantize(xm_r[0], E4M3, xm0_packed[0][:], 0, P)
+        quantize(xm0_r, E4M3, xm0_packed[0][:], 0, P)
         quantize(h_r[0], E5M2, h_packed[0][:, N:2 * N], P, 2 * P)
-        quantize(xm_r[0], E4M3, xm0_packed[1][:, 0:N], P, 2 * P)
-        quantize(xm_r[0], E4M3, xm0_packed[1][:, N:3 * N], 2 * P, D)
+        quantize(xm0_r, E4M3, xm0_packed[1][:, 0:N], P, 2 * P)
+        quantize(xm0_r, E4M3, xm0_packed[1][:, N:3 * N], 2 * P, D)
 
         def table_gradient(b, j, k):
             tile = bank(k, "dw%d_%d" % (b, j))
-            product(tile, xm_r[b], E4M3, j, h_r[b], E5M2)
+            operand, block = xm_blocks[b][j]
+            product(tile, operand, E4M3, block, h_r[b], E5M2)
             return tile
 
         def stage(name, tag):
@@ -233,7 +240,7 @@ def tile_attend_gbpr_wx_ts_kernel(tc, xT, wT, wt, ts, xm, offs, out_0, out_1):
 
         def turn_h(b, banks):
             words = h_packed[b][:].bitcast(F32)
-            out = held([P, PACK * K], BF16, "h_turned%d" % b)
+            out = held([P, PACK * K], BF16, "h_turned%d" % b, ("scaled1_0", "h_turned1")[b])
             for u in range(2):
                 turn = bank(banks[u], "h_turn%d_%d" % (b, u))
                 for t in range(PACK):
@@ -242,7 +249,6 @@ def tile_attend_gbpr_wx_ts_kernel(tc, xT, wT, wt, ts, xm, offs, out_0, out_1):
                                turn[:].bitcast(BF16).rearrange("s (t p e) -> s p e t", t=PACK, e=2))
             return out
 
-        w_i = []
 
         def row_gradient(b, banks, tags):
             for g in range(2):
@@ -254,17 +260,15 @@ def tile_attend_gbpr_wx_ts_kernel(tc, xT, wT, wt, ts, xm, offs, out_0, out_1):
                     nc.scalar.copy(staged[:, a, :], gx[:])
                 nc.scalar.dma_start(out=out_1[b, 2 * P * g:2 * P * (g + 1), :].rearrange("(a m) d -> m a d", m=P), in_=staged[:])
 
-        x1_packed = held([P, PACK * R], BF16, "x1_packed")
-        for k in range(4):
+        for k in range(1, 4):
             weave(x1_packed[:, N * k:N * (k + 1)], x1_raw, k)
         w1_packed = held([P, PACK * N], BF16, "w1_packed", "diff0")
         for c in range(4):
             weave(w1_packed[:, N * c:N * (c + 1)], w_planes[1], 2 * (c % 2) + c // 2)
         x_d.append(mx_operand("x_d1", "sig1"))
-        quantize(x_d[1], E4M3, x1_packed[:])
+        quantize(x_d[1], E4M3, x1_packed)
         quantize(w_d[1], E4M3, w1_packed[:])
         place(0, 0, table_gradient(0, 0, 0), stage("dw_staged0_0", "diff1")[:])
-        turn_w(1, 1, 0)
         xm1_packed = held([P, PACK * D], BF16, "xm1_packed", "diff0")
         weave_on_gpsimd(xm1_packed[:], xm_raw[1][:])
         scaled = []
@@ -273,11 +277,7 @@ def tile_attend_gbpr_wx_ts_kernel(tc, xT, wT, wt, ts, xm, offs, out_0, out_1):
             product(score, w_d[1], E4M3, c, x_d[1], E4M3)
             scaled.append(scale_items(1, score, c))
             if c == 1:
-                place(0, 1, table_gradient(0, 1, 1), stage("dw_staged0_1", "x0_half1")[:])
-        w_codes = held([P, B * K], U32, "w_i_codes", "x0_half1")
-        for b in range(B):
-            w_i.append((w_codes[:, K * b:K * (b + 1)], held([P, K], U8, "w_i%d_scales" % b)))
-            quantize(w_i[b], E4M3, w_turned[b][:])
+                place(0, 1, table_gradient(0, 1, 1), stage("dw_staged0_1", "x0_packed0")[:])
         weighted = []
         for j in range(2):
             summed = bank(4 + j, "summed%d" % j)
@@ -285,7 +285,7 @@ def tile_attend_gbpr_wx_ts_kernel(tc, xT, wT, wt, ts, xm, offs, out_0, out_1):
                 for half in range(2):
                     nc.tensor.matmul(summed[:, P * t:P * (t + 1)], scaled[2 * j + half][:, P * t:P * (t + 1)], ident[:],
                                      start=(half == 0), stop=(half == 1), is_transpose=True)
-            sig = held([P, R], F32, "sig1_%d" % j, "sig0")
+            sig = held([P, R], F32, "sig1_%d" % j)
             nc.scalar.activation(sig[:], summed[:], SIGMOID)
             out = held([P, R], F32, "weighted%d" % j)
             for t in range(PACK):
@@ -293,8 +293,9 @@ def tile_attend_gbpr_wx_ts_kernel(tc, xT, wT, wt, ts, xm, offs, out_0, out_1):
             weighted.append(out)
             if j == 0:
                 place(0, 2, table_gradient(0, 2, 2), stage("dw_staged0_2", "x0_packed1")[:])
-        xm_r.append(mx_operand("xm_r1", "scaled1_3"))
-        quantize(xm_r[1], E4M3, xm1_packed[:])
+        place(0, 3, table_gradient(0, 3, 3), stage("dw_staged0_3", "x0_half1")[:])
+        xm1_first = mx_operand("xm_r1_first", "scaled1_3", P)
+        quantize(xm1_first, E4M3, xm1_packed[:, 0:N], 0, P)
         h_slots = held([P, PACK, R], BF16, "h_slots")
         for j in range(2):
             back = bank(6 + j, "weighted_turned%d" % j)
@@ -313,14 +314,20 @@ def tile_attend_gbpr_wx_ts_kernel(tc, xT, wT, wt, ts, xm, offs, out_0, out_1):
             nc.scalar.copy(h_packed[1][:].bitcast(F32).rearrange("m (h j s u) -> m j h s u", h=2, j=2, u=2)[:, j],
                            turn[:].rearrange("m (h u s) -> m h s u", h=2, u=2))
         quantize(h_r[1], E5M2, h_packed[1][:])
-        place(0, 3, table_gradient(0, 3, 3), stage("dw_staged0_3", "h_slots")[:])
-        h0_turned = turn_h(0, (4, 5))
-        place(1, 0, table_gradient(1, 0, 1), stage("dw_staged1_0", "scaled1_0")[:])
+        turn_w(1, 1, 4)
+        w_i.append(mx_operand("w_i1"))
+        quantize(w_i[1], E4M3, w_turned[1][:])
+        h0_turned = turn_h(0, (6, 7))
+        xm1_rest = mx_operand("xm_r1_rest", "h_packed0", 3 * P)
+        quantize(xm1_rest, E4M3, xm1_packed[:, N:2 * N], 0, P)
+        quantize(xm1_rest, E4M3, xm1_packed[:, 2 * N:], P, 3 * P)
+        xm_blocks.append([(xm1_first, 0)] + [(xm1_rest, j) for j in range(3)])
+        place(1, 0, table_gradient(1, 0, 1), stage("dw_staged1_0", "weighted0")[:])
         h_i = [mx_operand("h_i%d" % b) for b in range(B)]
         quantize(h_i[0], E5M2, h0_turned[:])
         place(1, 1, table_gradient(1, 1, 0), stage("dw_staged1_1", "scaled1_1")[:])
-        row_gradient(0, (2, 4, 5, 7), ("xm_raw0", "x1_raw"))
-        quantize(h_i[1], E5M2, turn_h(1, (6, 2))[:])
+        row_gradient(0, (2, 4, 6, 7), ("xm_raw0", "x1_raw"))
+        quantize(h_i[1], E5M2, turn_h(1, (5, 2))[:])
         place(1, 2, table_gradient(1, 2, 3), stage("dw_staged1_2", "h_packed1")[:])
         place(1, 3, table_gradient(1, 3, 0), stage("dw_staged1_3", "h_turned1")[:])
-        row_gradient(1, (1, 6, 4, 5), ("xm_raw1", "ts_row"))
+        row_gradient(1, (1, 5, 4, 6), ("xm_raw1", "ts_row"))

@@ -120,7 +120,7 @@ def tile_attend_gbpr_wx_ts_kernel(tc, xT, wT, wt, ts, xm, offs, out_0, out_1):
         def gather(b, t):
             nc.vector.tensor_copy(w_planes[b][:, t, :], w_plane[t][:].indirect(group_offsets[b]))
 
-        x_d = [mx_operand("x_d0")]
+        x_d = [mx_operand("x_d%d" % b) for b in range(B)]
         x0_packed = [held([P, 2 * R], BF16, "x0_packed%d" % h) for h in range(2)]
         for k in range(2):
             weave(x0_packed[0][:, N * k:N * (k + 1)], x0_half[0], k)
@@ -147,7 +147,7 @@ def tile_attend_gbpr_wx_ts_kernel(tc, xT, wT, wt, ts, xm, offs, out_0, out_1):
             nc.vector.tensor_copy(w_planes[0][:, 3, P * k:P * (k + 1)], w_plane[3][:].indirect(offsets[:, 8 * k:8 * (k + 1)]))
         nc.vector.tensor_copy(woven(x0_packed[1][:]), planes(x0_half[1][:]))
         quantize(x_d[0], E4M3, x0_packed[1][:], R // 2, R)
-        w_d = [mx_operand("w_d%d" % b) for b in range(B)]
+        w_d = [mx_operand("w_d0")]
         for j, packed in enumerate((work[:, meet - 2 * N:meet], work[:, meet:meet + 2 * N])):
             for half in range(2):
                 weave(packed[:, N * half:N * (half + 1)], w_planes[0], 2 * half + j)
@@ -156,7 +156,7 @@ def tile_attend_gbpr_wx_ts_kernel(tc, xT, wT, wt, ts, xm, offs, out_0, out_1):
             nc.vector.tensor_copy(w_planes[1][:, 3, 256 * half:256 * (half + 1)],
                                   w_plane[3][:].indirect(offsets[:, 32 + 16 * half:48 + 16 * half]))
 
-        w_turned = [held([P, PACK * K], BF16, "w_turned0"), held([P, PACK * K], BF16, "w_turned1", "x0_half0")]
+        w_turned = [held([P, PACK * K], BF16, "w_turned0")]
 
         def turn_w(b, g, k_bank):
             turn = bank(k_bank, "w_turn%d_%d" % (b, g))
@@ -167,7 +167,6 @@ def tile_attend_gbpr_wx_ts_kernel(tc, xT, wT, wt, ts, xm, offs, out_0, out_1):
                            turn[:].rearrange("s (c p) -> s p c", c=4))
 
         turn_w(0, 0, 6)
-        turn_w(1, 0, 5)
         turn_w(0, 1, 7)
 
         h_packed = [held([P, PACK * N], BF16, "h_packed%d" % b) for b in range(B)]
@@ -209,19 +208,15 @@ def tile_attend_gbpr_wx_ts_kernel(tc, xT, wT, wt, ts, xm, offs, out_0, out_1):
         weave(xm0_first[:], xm_raw[0], 0, nc.vector.tensor_copy)
         w_i = [mx_operand("w_i0", "scaled0_0")]
         quantize(w_i[0], E4M3, w_turned[0][:])
-        behind_sums = held([P, 3 * N + PACK * R], BF16, "behind_sums", "scaled0_2")
-        xm0_packed = [xm0_first, behind_sums[:, 0:3 * N]]
-        x1_packed = behind_sums[:, 3 * N:]
-        weave_on_gpsimd(xm0_packed[1], xm_raw[0][:, :, P:D])
-        weave_on_gpsimd(x1_packed[:, 0:N], x1_raw[:, :, 0:P])
+        x1_packed = held([P, PACK * R], BF16, "x1_packed", "scaled0_2")
+        weave(x1_packed[:, 3 * N:], x1_raw, 3, nc.vector.tensor_copy)
         xm0_r = mx_operand("xm_r0", "factor0")
         xm_blocks = [[(xm0_r, j) for j in range(4)]]
-        for k in (2, 0, 3):
-            quantize(h_r[0], E5M2, h_packed[0][:, N * k:N * (k + 1)], P * k, P * (k + 1))
-        quantize(xm0_r, E4M3, xm0_packed[0][:], 0, P)
-        quantize(h_r[0], E5M2, h_packed[0][:, N:2 * N], P, 2 * P)
-        quantize(xm0_r, E4M3, xm0_packed[1][:, 0:N], P, 2 * P)
-        quantize(xm0_r, E4M3, xm0_packed[1][:, N:3 * N], 2 * P, D)
+        quantize(h_r[0], E5M2, h_packed[0][:, 2 * N:], 2 * P, N)
+        quantize(xm0_r, E4M3, xm0_first[:], 0, P)
+        quantize(h_r[0], E5M2, h_packed[0][:, 0:2 * N], 0, 2 * P)
+        xm0_second = held([P, N], BF16, "xm0_second", "xm0_first")
+        weave(xm0_second[:], xm_raw[0], 1, nc.vector.tensor_copy)
 
         def table_gradient(b, j, k):
             tile = bank(k, "dw%d_%d" % (b, j))
@@ -250,26 +245,31 @@ def tile_attend_gbpr_wx_ts_kernel(tc, xT, wT, wt, ts, xm, offs, out_0, out_1):
             return out
 
 
-        def row_gradient(b, banks, tags):
-            for g in range(2):
-                staged = held([P, 2, D], F32, "gx_staged%d_%d" % (b, g), tags[g])
-                for a in range(2):
-                    j = 2 * g + a
-                    gx = bank(banks[j], "gx%d_%d" % (b, j))
-                    product(gx, h_i[b], E5M2, j, w_i[b], E4M3)
-                    nc.scalar.copy(staged[:, a, :], gx[:])
-                nc.scalar.dma_start(out=out_1[b, 2 * P * g:2 * P * (g + 1), :].rearrange("(a m) d -> m a d", m=P), in_=staged[:])
+        def row_gradient(b, banks, tag):
+            staged = held([P, PACK * D], F32, "gx_staged%d" % b, tag)
+            for j in range(4):
+                gx = bank(banks[j], "gx%d_%d" % (b, j))
+                product(gx, h_i[b], E5M2, j, w_i[b], E4M3)
+                nc.scalar.copy(staged[:, D * j:D * (j + 1)], gx[:])
+                nc.scalar.dma_start(out=out_1[b, P * j:P * (j + 1), :], in_=staged[:, D * j:D * (j + 1)])
 
-        for k in range(1, 4):
-            weave(x1_packed[:, N * k:N * (k + 1)], x1_raw, k)
         w1_packed = held([P, PACK * N], BF16, "w1_packed", "diff0")
         for c in range(4):
             weave(w1_packed[:, N * c:N * (c + 1)], w_planes[1], 2 * (c % 2) + c // 2)
-        x_d.append(mx_operand("x_d1", "sig1"))
-        quantize(x_d[1], E4M3, x1_packed)
+        for k in range(3):
+            weave(x1_packed[:, N * k:N * (k + 1)], x1_raw, k)
+        w_d.append(mx_operand("w_d1", "sig1"))
         quantize(w_d[1], E4M3, w1_packed[:])
+        quantize(xm0_r, E4M3, xm0_second[:], P, 2 * P)
+        quantize(x_d[1], E4M3, x1_packed[:])
         place(0, 0, table_gradient(0, 0, 0), stage("dw_staged0_0", "diff1")[:])
-        xm1_packed = held([P, PACK * D], BF16, "xm1_packed", "diff0")
+        w_turned.append(held([P, PACK * K], BF16, "w_turned1", "diff0"))
+        for g in range(2):
+            turn_w(1, g, 6 + g)
+        xm0_rest = held([P, 2 * N], BF16, "xm0_rest", "scaled0_2")
+        weave_on_gpsimd(xm0_rest[:], xm_raw[0][:, :, 2 * P:D])
+        quantize(xm0_r, E4M3, xm0_rest[:], 2 * P, D)
+        xm1_packed = held([P, PACK * D], BF16, "xm1_packed", "scaled0_2")
         weave_on_gpsimd(xm1_packed[:], xm_raw[1][:])
         scaled = []
         for c in range(4):
@@ -277,7 +277,7 @@ def tile_attend_gbpr_wx_ts_kernel(tc, xT, wT, wt, ts, xm, offs, out_0, out_1):
             product(score, w_d[1], E4M3, c, x_d[1], E4M3)
             scaled.append(scale_items(1, score, c))
             if c == 1:
-                place(0, 1, table_gradient(0, 1, 1), stage("dw_staged0_1", "x0_packed0")[:])
+                place(0, 1, table_gradient(0, 1, 1), stage("dw_staged0_1", "xm_raw0")[:])
         weighted = []
         for j in range(2):
             summed = bank(4 + j, "summed%d" % j)
@@ -292,20 +292,20 @@ def tile_attend_gbpr_wx_ts_kernel(tc, xT, wT, wt, ts, xm, offs, out_0, out_1):
                 nc.scalar.activation(out[:, P * t:P * (t + 1)], sig[:, P * t:P * (t + 1)], COPY, scale=row_weight[:, 1, t:t + 1])
             weighted.append(out)
             if j == 0:
-                place(0, 2, table_gradient(0, 2, 2), stage("dw_staged0_2", "x0_packed1")[:])
-        place(0, 3, table_gradient(0, 3, 3), stage("dw_staged0_3", "x0_half1")[:])
-        xm1_first = mx_operand("xm_r1_first", "scaled1_3", P)
-        quantize(xm1_first, E4M3, xm1_packed[:, 0:N], 0, P)
+                place(0, 2, table_gradient(0, 2, 7), stage("dw_staged0_2", "x0_packed1")[:])
+        place(0, 3, table_gradient(0, 3, 7), stage("dw_staged0_3", "x0_half1")[:])
+        xm1_first = mx_operand("xm_r1_first", "sig1_1", 2 * P)
+        quantize(xm1_first, E4M3, xm1_packed[:, 0:2 * N], 0, 2 * P)
         h_slots = held([P, PACK, R], BF16, "h_slots")
         for j in range(2):
-            back = bank(6 + j, "weighted_turned%d" % j)
+            back = bank((6, 4)[j], "weighted_turned%d" % j)
             for t in range(PACK):
                 nc.tensor.transpose(back[:, P * t:P * (t + 1)], weighted[j][:, P * t:P * (t + 1)], ident[:])
             for half in range(2):
                 nc.scalar.activation(h_slots[:, 2 * half + j, :].rearrange("s (u m e) -> s u m e", u=2, e=2),
                                      back[:].rearrange("s (u e m) -> s u m e", u=2, e=2), COPY, scale=signed[half][:, 2 + j:3 + j])
         for j in range(2):
-            turn = bank(4 + j, "h_rows%d" % j)
+            turn = bank(2 + j, "h_rows%d" % j)
             for half in range(2):
                 words = h_slots[:, 2 * half + j, :].bitcast(F32)
                 for u in range(2):
@@ -314,20 +314,19 @@ def tile_attend_gbpr_wx_ts_kernel(tc, xT, wT, wt, ts, xm, offs, out_0, out_1):
             nc.scalar.copy(h_packed[1][:].bitcast(F32).rearrange("m (h j s u) -> m j h s u", h=2, j=2, u=2)[:, j],
                            turn[:].rearrange("m (h u s) -> m h s u", h=2, u=2))
         quantize(h_r[1], E5M2, h_packed[1][:])
-        turn_w(1, 1, 4)
-        w_i.append(mx_operand("w_i1"))
+        h0_turned = turn_h(0, (6, 3))
+        late_codes = held([P, K + 2 * P], U32, "late_codes", "h_packed0")
+        xm1_rest = late_codes[:, K:], held([P, 2 * P], U8, "xm_r1_rest_scales")
+        quantize(xm1_rest, E4M3, xm1_packed[:, 2 * N:], 0, 2 * P)
+        w_i.append((late_codes[:, 0:K], held([P, K], U8, "w_i1_scales")))
         quantize(w_i[1], E4M3, w_turned[1][:])
-        h0_turned = turn_h(0, (6, 7))
-        xm1_rest = mx_operand("xm_r1_rest", "h_packed0", 3 * P)
-        quantize(xm1_rest, E4M3, xm1_packed[:, N:2 * N], 0, P)
-        quantize(xm1_rest, E4M3, xm1_packed[:, 2 * N:], P, 3 * P)
-        xm_blocks.append([(xm1_first, 0)] + [(xm1_rest, j) for j in range(3)])
+        xm_blocks.append([(xm1_first, 0), (xm1_first, 1), (xm1_rest, 0), (xm1_rest, 1)])
         place(1, 0, table_gradient(1, 0, 1), stage("dw_staged1_0", "weighted0")[:])
         h_i = [mx_operand("h_i%d" % b) for b in range(B)]
         quantize(h_i[0], E5M2, h0_turned[:])
         place(1, 1, table_gradient(1, 1, 0), stage("dw_staged1_1", "scaled1_1")[:])
-        row_gradient(0, (2, 4, 6, 7), ("xm_raw0", "x1_raw"))
-        quantize(h_i[1], E5M2, turn_h(1, (5, 2))[:])
-        place(1, 2, table_gradient(1, 2, 3), stage("dw_staged1_2", "h_packed1")[:])
-        place(1, 3, table_gradient(1, 3, 0), stage("dw_staged1_3", "h_turned1")[:])
-        row_gradient(1, (1, 5, 4, 6), ("xm_raw1", "ts_row"))
+        row_gradient(0, (4, 5, 7, 2), "x1_raw")
+        quantize(h_i[1], E5M2, turn_h(1, (4, 5))[:])
+        place(1, 2, table_gradient(1, 2, 6), stage("dw_staged1_2", "h_packed1")[:])
+        place(1, 3, table_gradient(1, 3, 3), stage("dw_staged1_3", "h_turned1")[:])
+        row_gradient(1, (0, 1, 7, 2), "xm_raw1")

@@ -120,7 +120,7 @@ def tile_attend_gbpr_wx_ts_kernel(tc, xT, wT, wt, ts, xm, offs, out_0, out_1):
         def gather(b, t):
             nc.vector.tensor_copy(w_planes[b][:, t, :], w_plane[t][:].indirect(group_offsets[b]))
 
-        x_d = [mx_operand("x_d%d" % b) for b in range(B)]
+        x_d = [mx_operand("x_d0")]
         x0_packed = [held([P, 2 * R], BF16, "x0_packed%d" % h) for h in range(2)]
         for k in range(2):
             weave(x0_packed[0][:, N * k:N * (k + 1)], x0_half[0], k)
@@ -156,18 +156,18 @@ def tile_attend_gbpr_wx_ts_kernel(tc, xT, wT, wt, ts, xm, offs, out_0, out_1):
             nc.vector.tensor_copy(w_planes[1][:, 3, 256 * half:256 * (half + 1)],
                                   w_plane[3][:].indirect(offsets[:, 32 + 16 * half:48 + 16 * half]))
 
-        w_turned = [held([P, PACK * K], BF16, "w_turned0")]
-
-        def turn_w(b, g, k_bank):
+        def turn_w(b, g, k_bank, out):
             turn = bank(k_bank, "w_turn%d_%d" % (b, g))
             for c in range(4):
                 words = w_planes[b][:, 2 * g + c // 2, :].bitcast(F32)
                 nc.tensor.transpose(turn[:, P * c:P * (c + 1)], words[:, c % 2::2], ident[:])
-            nc.scalar.copy(w_turned[b][:].bitcast(F32).rearrange("s (p g c) -> s g p c", g=2, c=4)[:, g],
-                           turn[:].rearrange("s (c p) -> s p c", c=4))
+            nc.scalar.copy(out.bitcast(F32).rearrange("s (p c) -> s p c", c=4), turn[:].rearrange("s (c p) -> s p c", c=4))
 
-        turn_w(0, 0, 6)
-        turn_w(0, 1, 7)
+        w0_turned = held([P, PACK * K], BF16, "w0_turned")
+        w1_turned = [held([P, 2 * K], BF16, "w1_turned_first", "x0_half0")]
+        turn_w(0, 0, 6, w0_turned[:, 0:2 * K])
+        turn_w(1, 0, 5, w1_turned[0][:])
+        turn_w(0, 1, 7, w0_turned[:, 2 * K:])
 
         h_packed = [held([P, PACK * N], BF16, "h_packed%d" % b) for b in range(B)]
         h_r = [mx_operand("h_r%d" % b) for b in range(B)]
@@ -206,10 +206,10 @@ def tile_attend_gbpr_wx_ts_kernel(tc, xT, wT, wt, ts, xm, offs, out_0, out_1):
 
         xm0_first = held([P, N], BF16, "xm0_first")
         weave(xm0_first[:], xm_raw[0], 0, nc.vector.tensor_copy)
-        w_i = [mx_operand("w_i0", "scaled0_0")]
-        quantize(w_i[0], E4M3, w_turned[0][:])
-        x1_packed = held([P, PACK * R], BF16, "x1_packed", "scaled0_2")
-        weave(x1_packed[:, 3 * N:], x1_raw, 3, nc.vector.tensor_copy)
+        w_i = [mx_operand("w_i0", "scaled0_2")]
+        quantize(w_i[0], E4M3, w0_turned[:])
+        x1_half = [held([P, 2 * N], BF16, "x1_first", "w0_turned"), held([P, 2 * N], BF16, "x1_second", "diff1")]
+        weave_on_gpsimd(x1_half[0][:], x1_raw[:, :, 0:R // 2])
         xm0_r = mx_operand("xm_r0", "factor0")
         xm_blocks = [[(xm0_r, j) for j in range(4)]]
         quantize(h_r[0], E5M2, h_packed[0][:, 2 * N:], 2 * P, N)
@@ -217,6 +217,7 @@ def tile_attend_gbpr_wx_ts_kernel(tc, xT, wT, wt, ts, xm, offs, out_0, out_1):
         quantize(h_r[0], E5M2, h_packed[0][:, 0:2 * N], 0, 2 * P)
         xm0_second = held([P, N], BF16, "xm0_second", "xm0_first")
         weave(xm0_second[:], xm_raw[0], 1, nc.vector.tensor_copy)
+        quantize(xm0_r, E4M3, xm0_second[:], P, 2 * P)
 
         def table_gradient(b, j, k):
             tile = bank(k, "dw%d_%d" % (b, j))
@@ -250,27 +251,26 @@ def tile_attend_gbpr_wx_ts_kernel(tc, xT, wT, wt, ts, xm, offs, out_0, out_1):
             for j in range(4):
                 gx = bank(banks[j], "gx%d_%d" % (b, j))
                 product(gx, h_i[b], E5M2, j, w_i[b], E4M3)
-                nc.scalar.copy(staged[:, D * j:D * (j + 1)], gx[:])
+                nc.scalar.copy(staged[:, D * j:D * (j + 1)].rearrange("m (p g a) -> m p g a", g=2, a=2),
+                               gx[:].rearrange("m (g p a) -> m p g a", g=2, a=2))
                 nc.scalar.dma_start(out=out_1[b, P * j:P * (j + 1), :], in_=staged[:, D * j:D * (j + 1)])
 
         w1_packed = held([P, PACK * N], BF16, "w1_packed", "diff0")
         for c in range(4):
             weave(w1_packed[:, N * c:N * (c + 1)], w_planes[1], 2 * (c % 2) + c // 2)
-        for k in range(3):
-            weave(x1_packed[:, N * k:N * (k + 1)], x1_raw, k)
+        for k in range(2):
+            weave(x1_half[1][:, N * k:N * (k + 1)], x1_raw, 2 + k)
         w_d.append(mx_operand("w_d1", "sig1"))
+        x_d.append(mx_operand("x_d1", "sig0"))
         quantize(w_d[1], E4M3, w1_packed[:])
-        quantize(xm0_r, E4M3, xm0_second[:], P, 2 * P)
-        quantize(x_d[1], E4M3, x1_packed[:])
-        place(0, 0, table_gradient(0, 0, 0), stage("dw_staged0_0", "diff1")[:])
-        w_turned.append(held([P, PACK * K], BF16, "w_turned1", "diff0"))
-        for g in range(2):
-            turn_w(1, g, 6 + g)
-        xm0_rest = held([P, 2 * N], BF16, "xm0_rest", "scaled0_2")
+        for h in range(2):
+            quantize(x_d[1], E4M3, x1_half[h][:], h * R // 2, (h + 1) * R // 2)
+        place(0, 0, table_gradient(0, 0, 0), stage("dw_staged0_0", "x0_packed0")[:])
+        w1_turned.append(held([P, 2 * K], BF16, "w1_turned_second", "diff0"))
+        turn_w(1, 1, 6, w1_turned[1][:])
+        xm0_rest = held([P, 2 * N], BF16, "xm0_rest", "diff1")
         weave_on_gpsimd(xm0_rest[:], xm_raw[0][:, :, 2 * P:D])
         quantize(xm0_r, E4M3, xm0_rest[:], 2 * P, D)
-        xm1_packed = held([P, PACK * D], BF16, "xm1_packed", "scaled0_2")
-        weave_on_gpsimd(xm1_packed[:], xm_raw[1][:])
         scaled = []
         for c in range(4):
             score = bank(4 + c, "score1_%d" % c)
@@ -289,12 +289,14 @@ def tile_attend_gbpr_wx_ts_kernel(tc, xT, wT, wt, ts, xm, offs, out_0, out_1):
             nc.scalar.activation(sig[:], summed[:], SIGMOID)
             out = held([P, R], F32, "weighted%d" % j)
             for t in range(PACK):
-                nc.scalar.activation(out[:, P * t:P * (t + 1)], sig[:, P * t:P * (t + 1)], COPY, scale=row_weight[:, 1, t:t + 1])
+                nc.gpsimd.tensor_scalar(out[:, P * t:P * (t + 1)], sig[:, P * t:P * (t + 1)], row_weight[:, 1, t:t + 1], 0.0, MULT, ADD)
             weighted.append(out)
             if j == 0:
                 place(0, 2, table_gradient(0, 2, 7), stage("dw_staged0_2", "x0_packed1")[:])
         place(0, 3, table_gradient(0, 3, 7), stage("dw_staged0_3", "x0_half1")[:])
-        xm1_first = mx_operand("xm_r1_first", "sig1_1", 2 * P)
+        xm1_packed = held([P, PACK * D], BF16, "xm1_packed", "sig1_1")
+        weave_on_gpsimd(xm1_packed[:], xm_raw[1][:])
+        xm1_first = mx_operand("xm_r1_first", None, 2 * P)
         quantize(xm1_first, E4M3, xm1_packed[:, 0:2 * N], 0, 2 * P)
         h_slots = held([P, PACK, R], BF16, "h_slots")
         for j in range(2):
@@ -319,7 +321,8 @@ def tile_attend_gbpr_wx_ts_kernel(tc, xT, wT, wt, ts, xm, offs, out_0, out_1):
         xm1_rest = late_codes[:, K:], held([P, 2 * P], U8, "xm_r1_rest_scales")
         quantize(xm1_rest, E4M3, xm1_packed[:, 2 * N:], 0, 2 * P)
         w_i.append((late_codes[:, 0:K], held([P, K], U8, "w_i1_scales")))
-        quantize(w_i[1], E4M3, w_turned[1][:])
+        for g in range(2):
+            quantize(w_i[1], E4M3, w1_turned[g][:], 2 * P * g, 2 * P * (g + 1))
         xm_blocks.append([(xm1_first, 0), (xm1_first, 1), (xm1_rest, 0), (xm1_rest, 1)])
         place(1, 0, table_gradient(1, 0, 1), stage("dw_staged1_0", "weighted0")[:])
         h_i = [mx_operand("h_i%d" % b) for b in range(B)]

@@ -22,6 +22,7 @@ SIGMOID = mybir.ActivationFunctionType.Sigmoid
 P = 128
 PACK = 4
 K = P * PACK
+HALF = N // 2
 ALIGN = 64
 
 
@@ -45,42 +46,15 @@ def tile_attend_gbpr_wx_ts_kernel(tc, xT, wT, wt, ts, xm, offs, out_0, out_1):
             codes, scales = operand
             nc.vector.quantize_mx(out=codes[:, c0:c1].bitcast(fmt), scales=scales[:, c0:c1], in_=src)
 
-        def product(out, fixed, fixed_fmt, j, moving, moving_fmt):
+        def product(out, fixed, fixed_fmt, j, moving, moving_fmt, c0=0, c1=K):
             cols = slice(P * j, P * (j + 1))
-            nc.tensor.matmul_mx(out=out[:], lhsT=fixed[0][:, cols].bitcast(fixed_fmt), lhsT_scale=fixed[1][:, cols],
-                                rhs=moving[0][:].bitcast(moving_fmt), rhs_scale=moving[1][:], start=True, stop=True)
+            nc.tensor.matmul_mx(out=out, lhsT=fixed[0][:, cols].bitcast(fixed_fmt), lhsT_scale=fixed[1][:, cols],
+                                rhs=moving[0][:, c0:c1].bitcast(moving_fmt), rhs_scale=moving[1][:, c0:c1], start=True, stop=True)
 
-        offsets = lists.tile([P, B * N // 16], U16, name="offsets")
-        nc.sync.dma_start(offsets[:], offs)
-        group_offsets = [offsets[:, b * (N // 16):(b + 1) * (N // 16)] for b in range(B)]
+        on_vector, on_scalar = nc.vector.tensor_copy, nc.scalar.copy
 
-        row_weight = held([P, B, PACK], F32, "row_weight")
-        nc.scalar.dma_start(out=row_weight[:], in_=wt.rearrange("b (p t) o -> p b (t o)", t=PACK))
-        ts_row = held([P, T], F32, "ts_row")
-        nc.sync.dma_start(out=ts_row[P - 1:P, :], in_=ts[0:1, :])
-        nc.vector.memset(ts_row[0:P - 1, :].bitcast(I32), 0)
-
-        w_rows = wT.rearrange("(p t) c -> t p c", t=PACK)
-        w_plane = [held([P, T], F32, "w_plane%d" % t) for t in range(PACK)]
-        x0_half = [held([P, PACK, R // 2], F32, "x0_half%d" % h) for h in range(2)]
-        x0_rows = xT[0].rearrange("(p j) (h r) -> h p j r", j=PACK, h=2)
-        for h in range(2):
-            for t in ((0, 1, 2), (3,))[h]:
-                nc.sync.dma_start(out=w_plane[t][:], in_=w_rows[t])
-            nc.sync.dma_start(out=x0_half[h][:], in_=x0_rows[h])
-        xm_raw = [held([P, PACK, D], F32, "xm_raw%d" % b) for b in range(B)]
-        x1_raw = held([P, PACK, R], F32, "x1_raw")
-        nc.sync.dma_start(out=xm_raw[0][:], in_=xm[0].rearrange("(p t) d -> p t d", t=PACK))
-        nc.sync.dma_start(out=x1_raw[:], in_=xT[1].rearrange("(p j) r -> p j r", j=PACK))
-        nc.sync.dma_start(out=xm_raw[1][:], in_=xm[1].rearrange("(p t) d -> p t d", t=PACK))
-
-        ident = held([P, P], F32, "ident")
-        make_identity(nc, ident[:])
-        warm = held([P, 1], F32, "warm")
-        nc.scalar.activation(warm[:], ident[:, 0:1], SIGMOID)
-        window = [held([P, T], F32, "window%d" % j) for j in range(PACK)]
-        for j in range(PACK):
-            nc.gpsimd.memset(window[j][:], 0.0)
+        def indirect_on_scalar(out, in_):
+            nc.scalar.activation(out, in_, COPY)
 
         def woven(packed, run=4):
             return packed.rearrange("p (c i t) -> p c t i", i=run, t=PACK)
@@ -91,245 +65,256 @@ def tile_attend_gbpr_wx_ts_kernel(tc, xT, wT, wt, ts, xm, offs, out_0, out_1):
         def by_plane(flat):
             return flat.rearrange("p (t c) -> p t c", t=PACK)
 
-        def dealt(rows):
-            return rows.rearrange("p (m t) -> p t m", t=PACK)
+        def weave(copy, packed, source):
+            copy(woven(packed), planes(source))
 
-        def weave(packed, source, k, engine_copy=nc.scalar.copy):
-            engine_copy(woven(packed), planes(source[:, :, P * k:P * (k + 1)]))
+        def weave_on_gpsimd(packed, source):
+            nc.gpsimd.tensor_scalar(packed.rearrange("p (c t) -> p c t", t=PACK), source.rearrange("p t c -> p c t"), 1.0, 0.0, MULT, ADD)
 
-        stretch = 5 * N // 2
-        meet = 3 * stretch + N // 2
-        work = held([P, meet + 2 * N], BF16, "work")
+        offsets = lists.tile([P, B * N // 16], U16, name="offsets")
+        nc.sync.dma_start(offsets[:], offs)
 
-        w0_planes = held([P, PACK, N], BF16, "w0_planes")
-        w_planes = [w0_planes[:], work[:, 0:PACK * stretch].rearrange("p (t c) -> p t c", t=PACK)[:, :, 0:N]]
+        def listed(b, s0=0, s1=N):
+            return offsets[:, (N * b + s0) // 16:(N * b + s1) // 16]
+
+        row_weight = held([P, B, PACK], F32, "row_weight")
+        nc.scalar.dma_start(out=row_weight[:], in_=wt.rearrange("b (p t) o -> p b (t o)", t=PACK))
+        ts_row = held([P, T], F32, "ts_row")
+        nc.sync.dma_start(out=ts_row[P - 1:P, :], in_=ts[0:1, :])
+        nc.vector.memset(ts_row[0:P - 1, :].bitcast(I32), 0)
+
+        w_rows = wT.rearrange("(p t) c -> t p c", t=PACK)
+        w_plane = [held([P, T], F32, "w_plane%d" % t) for t in range(PACK)]
+        for t in range(PACK):
+            nc.sync.dma_start(out=w_plane[t][:], in_=w_rows[t])
+        x0_half = [held([P, PACK, R // 2], F32, "x0_half%d" % h) for h in range(2)]
+        x0_rows = xT[0].rearrange("(p j) (h r) -> h p j r", j=PACK, h=2)
+        for h in range(2):
+            nc.sync.dma_start(out=x0_half[h][:], in_=x0_rows[h])
+        x1_raw = held([P, PACK, R], F32, "x1_raw")
+        xm_raw = [held([P, PACK, D], F32, "xm_raw%d" % b) for b in range(B)]
+        nc.sync.dma_start(out=x1_raw[:], in_=xT[1].rearrange("(p j) r -> p j r", j=PACK))
+        for b in range(B):
+            nc.sync.dma_start(out=xm_raw[b][:], in_=xm[b].rearrange("(p t) d -> p t d", t=PACK))
+
+        ident = held([P, P], F32, "ident")
+        make_identity(nc, ident[:])
+        warm = held([P, 1], F32, "warm")
+        nc.scalar.activation(warm[:], ident[:, 0:1], SIGMOID)
+        window = [held([P, T], F32, "window%d" % j) for j in range(PACK)]
+        for j in range(PACK):
+            nc.gpsimd.memset(window[j][:], 0.0)
 
         ts_listed = held([P, B * N], F32, "ts_listed")
-        nc.vector.tensor_copy(ts_listed[:], ts_row[:].indirect(offsets[:]))
+        for b, gather in enumerate((on_vector, indirect_on_scalar)):
+            gather(ts_listed[:, N * b:N * (b + 1)], ts_row[:].indirect(listed(b)))
         signed = []
         for half, sign in ((0, -1.0), (1, 1.0)):
             turned = bank(half, "ts_turned%d" % half)
             for b in range(B):
                 for j in range(2):
-                    c0 = N * b + 256 * half + P * j
+                    c0 = N * b + HALF * half + P * j
                     nc.tensor.transpose(turned[:, P * (2 * b + j):P * (2 * b + j + 1)], ts_listed[:, c0:c0 + P], ident[:])
             col = held([P, 2 * B], F32, "signed%d" % half)
             nc.scalar.activation(col[:], turned[:].rearrange("p (k c) -> p k c", c=P)[:, :, P - 1], COPY, scale=sign)
             signed.append(col)
-
-        def gather(b, t):
-            nc.vector.tensor_copy(w_planes[b][:, t, :], w_plane[t][:].indirect(group_offsets[b]))
-
-        x_d = [mx_operand("x_d0")]
-        x0_packed = [held([P, 2 * R], BF16, "x0_packed%d" % h) for h in range(2)]
-        for k in range(2):
-            weave(x0_packed[0][:, N * k:N * (k + 1)], x0_half[0], k)
-
-        def spread_scales(b, k_bank):
-            spread = bank(k_bank, "ts_spread%d" % b)
+        ts_spread = []
+        for b in range(B):
+            spread = bank(6 + b, "ts_spread_bank%d" % b)
             for half in range(2):
                 for j in range(2):
                     k = 2 * half + j
                     nc.tensor.transpose(spread[:, P * k:P * (k + 1)],
                                         signed[half][:, 2 * b + j:2 * b + j + 1].to_broadcast([P, P]), ident[:])
-            return spread
+            ts_spread.append(held([P, N], F32, "ts_spread%d" % b))
+            on_scalar(ts_spread[b][:], spread[:])
 
-        factor = [held([P, PACK * N], F32, "factor0")]
-        spread0 = spread_scales(0, 4)
-        for t in range(PACK):
-            nc.scalar.activation(factor[0][:, N * t:N * (t + 1)], spread0[:], COPY, scale=row_weight[:, 0, t:t + 1])
+        w_planes = [held([P, PACK * N], BF16, "w_planes%d" % b) for b in range(B)]
+        w_turned = [held([P, PACK * D], BF16, "w_turned%d" % b) for b in range(B)]
 
-        for t in range(PACK - 1):
-            gather(0, t)
-            gather(1, t)
-        quantize(x_d[0], E4M3, x0_packed[0][:], 0, R // 2)
-        for k in (0, 2, 1, 3):
-            nc.vector.tensor_copy(w_planes[0][:, 3, P * k:P * (k + 1)], w_plane[3][:].indirect(offsets[:, 8 * k:8 * (k + 1)]))
-        nc.vector.tensor_copy(woven(x0_packed[1][:]), planes(x0_half[1][:]))
-        quantize(x_d[0], E4M3, x0_packed[1][:], R // 2, R)
-        w_d = [mx_operand("w_d0")]
-        for j, packed in enumerate((work[:, meet - 2 * N:meet], work[:, meet:meet + 2 * N])):
-            for half in range(2):
-                weave(packed[:, N * half:N * (half + 1)], w_planes[0], 2 * half + j)
-            quantize(w_d[0], E4M3, packed, 2 * P * j, 2 * P * (j + 1))
-        for half in range(2):
-            nc.vector.tensor_copy(w_planes[1][:, 3, 256 * half:256 * (half + 1)],
-                                  w_plane[3][:].indirect(offsets[:, 32 + 16 * half:48 + 16 * half]))
-
-        def turn_w(b, g, k_bank, out):
-            turn = bank(k_bank, "w_turn%d_%d" % (b, g))
+        def turn_words(source, g, k, name):
+            turn = bank(k, name)
             for c in range(4):
-                words = w_planes[b][:, 2 * g + c // 2, :].bitcast(F32)
-                nc.tensor.transpose(turn[:, P * c:P * (c + 1)], words[:, c % 2::2], ident[:])
-            nc.scalar.copy(out.bitcast(F32).rearrange("s (p c) -> s p c", c=4), turn[:].rearrange("s (c p) -> s p c", c=4))
+                t = 2 * g + c // 2
+                nc.tensor.transpose(turn[:, P * c:P * (c + 1)], source[:, N * t:N * (t + 1)].bitcast(F32)[:, c % 2::2], ident[:])
+            return turn
 
-        w0_turned = held([P, PACK * K], BF16, "w0_turned")
-        w1_turned = [held([P, 2 * K], BF16, "w1_turned_first", "x0_half0")]
-        turn_w(0, 0, 6, w0_turned[:, 0:2 * K])
-        turn_w(1, 0, 5, w1_turned[0][:])
-        turn_w(0, 1, 7, w0_turned[:, 2 * K:])
+        def turn_w(b, g, k, copy):
+            turn = turn_words(w_planes[b], g, k, "w_turn%d_%d" % (b, g))
+            copy(w_turned[b][:].bitcast(F32).rearrange("q (p g c) -> q g p c", g=2, c=4)[:, g], turn[:].rearrange("q (c p) -> q p c", c=4))
 
-        h_packed = [held([P, PACK * N], BF16, "h_packed%d" % b) for b in range(B)]
+        for t in range(PACK):
+            on_vector(w_planes[0][:, N * t:N * (t + 1)], w_plane[t][:].indirect(listed(0)))
+            (indirect_on_scalar if t >= 1 else on_vector)(w_planes[1][:, N * t:N * (t + 1)], w_plane[t][:].indirect(listed(1)))
+            if t == 1:
+                turn_w(0, 0, 2, on_scalar)
+                turn_w(1, 0, 3, on_scalar)
+
+        w_d = [mx_operand("w_d%d" % b) for b in range(B)]
+        x_d = [mx_operand("x_d%d" % b) for b in range(B)]
+        w_i = [mx_operand("w_i%d" % b) for b in range(B)]
+        xm_r = [mx_operand("xm_r%d" % b) for b in range(B)]
         h_r = [mx_operand("h_r%d" % b) for b in range(B)]
-
-        def scale_items(b, score, c):
-            out = held([P, R], F32, "scaled%d_%d" % (b, c))
-            k = 2 * b + c // 2
-            nc.scalar.activation(by_plane(out[:]), dealt(score[:]), COPY, scale=signed[c % 2][:, k:k + 1])
-            return out
-
-        score = [bank(c, "score0_%d" % c) for c in range(4)]
-        for c in range(4):
-            product(score[c], w_d[0], E4M3, c, x_d[0], E4M3)
-        diff = [held([P, R], F32, "diff%d" % j) for j in range(2)]
-        for j in range(2):
-            positive = scale_items(0, score[2 * j], 2 * j)
-            nc.vector.scalar_tensor_tensor(by_plane(diff[j][:]), dealt(score[2 * j + 1][:]), signed[1][:, j:j + 1],
-                                           by_plane(positive[:]), MULT, ADD)
-        turned = []
-        for j in range(2):
-            sig = held([P, R], F32, "sig0_%d" % j, "sig%d" % j)
-            nc.scalar.activation(sig[:], diff[j][:], SIGMOID)
-            turn = bank(4 + j, "sig_turned%d" % j)
-            for t in range(PACK):
-                nc.tensor.transpose(turn[:, P * t:P * (t + 1)], sig[:, P * t:P * (t + 1)], ident[:])
-            turned.append(turn)
-
-        for j in range(2):
-            for half in (1, 0):
-                s0 = 256 * half + P * j
-                nc.vector.tensor_tensor(woven(h_packed[0][:, PACK * s0:PACK * (s0 + P)], 2), planes(by_plane(turned[j][:]), 2),
-                                        planes(by_plane(factor[0][:])[:, :, s0:s0 + P], 2), MULT)
-
-        def weave_on_gpsimd(packed, source):
-            nc.gpsimd.tensor_scalar(packed.rearrange("p (c t) -> p c t", t=PACK), source.rearrange("p t c -> p c t"), 1.0, 0.0, MULT, ADD)
-
-        xm0_first = held([P, N], BF16, "xm0_first")
-        weave(xm0_first[:], xm_raw[0], 0, nc.vector.tensor_copy)
-        w_i = [mx_operand("w_i0", "scaled0_2")]
-        quantize(w_i[0], E4M3, w0_turned[:])
-        x1_half = [held([P, 2 * N], BF16, "x1_first", "w0_turned"), held([P, 2 * N], BF16, "x1_second", "diff1")]
-        weave_on_gpsimd(x1_half[0][:], x1_raw[:, :, 0:R // 2])
-        xm0_r = mx_operand("xm_r0", "factor0")
-        xm_blocks = [[(xm0_r, j) for j in range(4)]]
-        quantize(h_r[0], E5M2, h_packed[0][:, 2 * N:], 2 * P, N)
-        quantize(xm0_r, E4M3, xm0_first[:], 0, P)
-        quantize(h_r[0], E5M2, h_packed[0][:, 0:2 * N], 0, 2 * P)
-        xm0_second = held([P, N], BF16, "xm0_second", "xm0_first")
-        weave(xm0_second[:], xm_raw[0], 1, nc.vector.tensor_copy)
-        quantize(xm0_r, E4M3, xm0_second[:], P, 2 * P)
-
-        def table_gradient(b, j, k):
-            tile = bank(k, "dw%d_%d" % (b, j))
-            operand, block = xm_blocks[b][j]
-            product(tile, operand, E4M3, block, h_r[b], E5M2)
-            return tile
-
-        def stage(name, tag):
-            return held([P, N], F32, name, tag)
-
-        def place(b, j, dw, staged):
-            nc.scalar.copy(staged, dw[:])
-            nc.vector.tensor_copy(window[j][:].indirect(group_offsets[b]), staged)
-            if b == B - 1:
-                nc.sync.dma_start(out=out_0[P * j:P * (j + 1), :], in_=window[j][:])
-
-        def turn_h(b, banks):
-            words = h_packed[b][:].bitcast(F32)
-            out = held([P, PACK * K], BF16, "h_turned%d" % b, ("scaled1_0", "h_turned1")[b])
-            for u in range(2):
-                turn = bank(banks[u], "h_turn%d_%d" % (b, u))
-                for t in range(PACK):
-                    nc.tensor.transpose(turn[:, P * t:P * (t + 1)], words[:, 2 * t + u::2 * PACK], ident[:])
-                nc.scalar.copy(out[:].rearrange("s (p u e t) -> s u p e t", u=2, e=2, t=PACK)[:, u],
-                               turn[:].bitcast(BF16).rearrange("s (t p e) -> s p e t", t=PACK, e=2))
-            return out
-
-
-        def row_gradient(b, banks, tag):
-            staged = held([P, PACK * D], F32, "gx_staged%d" % b, tag)
-            for j in range(4):
-                gx = bank(banks[j], "gx%d_%d" % (b, j))
-                product(gx, h_i[b], E5M2, j, w_i[b], E4M3)
-                nc.scalar.copy(staged[:, D * j:D * (j + 1)].rearrange("m (p g a) -> m p g a", g=2, a=2),
-                               gx[:].rearrange("m (g p a) -> m p g a", g=2, a=2))
-                nc.scalar.dma_start(out=out_1[b, P * j:P * (j + 1), :], in_=staged[:, D * j:D * (j + 1)])
-
-        w1_packed = held([P, PACK * N], BF16, "w1_packed", "diff0")
-        for c in range(4):
-            weave(w1_packed[:, N * c:N * (c + 1)], w_planes[1], 2 * (c % 2) + c // 2)
-        for k in range(2):
-            weave(x1_half[1][:, N * k:N * (k + 1)], x1_raw, 2 + k)
-        w_d.append(mx_operand("w_d1", "sig1"))
-        x_d.append(mx_operand("x_d1", "sig0"))
-        quantize(w_d[1], E4M3, w1_packed[:])
-        for h in range(2):
-            quantize(x_d[1], E4M3, x1_half[h][:], h * R // 2, (h + 1) * R // 2)
-        place(0, 0, table_gradient(0, 0, 0), stage("dw_staged0_0", "x0_packed0")[:])
-        w1_turned.append(held([P, 2 * K], BF16, "w1_turned_second", "diff0"))
-        turn_w(1, 1, 6, w1_turned[1][:])
-        xm0_rest = held([P, 2 * N], BF16, "xm0_rest", "diff1")
-        weave_on_gpsimd(xm0_rest[:], xm_raw[0][:, :, 2 * P:D])
-        quantize(xm0_r, E4M3, xm0_rest[:], 2 * P, D)
-        scaled = []
-        for c in range(4):
-            score = bank(4 + c, "score1_%d" % c)
-            product(score, w_d[1], E4M3, c, x_d[1], E4M3)
-            scaled.append(scale_items(1, score, c))
-            if c == 1:
-                place(0, 1, table_gradient(0, 1, 1), stage("dw_staged0_1", "xm_raw0")[:])
-        weighted = []
-        for j in range(2):
-            summed = bank(4 + j, "summed%d" % j)
-            for t in range(PACK):
-                for half in range(2):
-                    nc.tensor.matmul(summed[:, P * t:P * (t + 1)], scaled[2 * j + half][:, P * t:P * (t + 1)], ident[:],
-                                     start=(half == 0), stop=(half == 1), is_transpose=True)
-            sig = held([P, R], F32, "sig1_%d" % j)
-            nc.scalar.activation(sig[:], summed[:], SIGMOID)
-            out = held([P, R], F32, "weighted%d" % j)
-            for t in range(PACK):
-                nc.gpsimd.tensor_scalar(out[:, P * t:P * (t + 1)], sig[:, P * t:P * (t + 1)], row_weight[:, 1, t:t + 1], 0.0, MULT, ADD)
-            weighted.append(out)
-            if j == 0:
-                place(0, 2, table_gradient(0, 2, 7), stage("dw_staged0_2", "x0_packed1")[:])
-        place(0, 3, table_gradient(0, 3, 7), stage("dw_staged0_3", "x0_half1")[:])
-        xm1_packed = held([P, PACK * D], BF16, "xm1_packed", "sig1_1")
-        weave_on_gpsimd(xm1_packed[:], xm_raw[1][:])
-        xm1_first = mx_operand("xm_r1_first", None, 2 * P)
-        quantize(xm1_first, E4M3, xm1_packed[:, 0:2 * N], 0, 2 * P)
-        h_slots = held([P, PACK, R], BF16, "h_slots")
-        for j in range(2):
-            back = bank((6, 4)[j], "weighted_turned%d" % j)
-            for t in range(PACK):
-                nc.tensor.transpose(back[:, P * t:P * (t + 1)], weighted[j][:, P * t:P * (t + 1)], ident[:])
-            for half in range(2):
-                nc.scalar.activation(h_slots[:, 2 * half + j, :].rearrange("s (u m e) -> s u m e", u=2, e=2),
-                                     back[:].rearrange("s (u e m) -> s u m e", u=2, e=2), COPY, scale=signed[half][:, 2 + j:3 + j])
-        for j in range(2):
-            turn = bank(2 + j, "h_rows%d" % j)
-            for half in range(2):
-                words = h_slots[:, 2 * half + j, :].bitcast(F32)
-                for u in range(2):
-                    c = 2 * half + u
-                    nc.tensor.transpose(turn[:, P * c:P * (c + 1)], words[:, P * u:P * (u + 1)], ident[:])
-            nc.scalar.copy(h_packed[1][:].bitcast(F32).rearrange("m (h j s u) -> m j h s u", h=2, j=2, u=2)[:, j],
-                           turn[:].rearrange("m (h u s) -> m h s u", h=2, u=2))
-        quantize(h_r[1], E5M2, h_packed[1][:])
-        h0_turned = turn_h(0, (6, 3))
-        late_codes = held([P, K + 2 * P], U32, "late_codes", "h_packed0")
-        xm1_rest = late_codes[:, K:], held([P, 2 * P], U8, "xm_r1_rest_scales")
-        quantize(xm1_rest, E4M3, xm1_packed[:, 2 * N:], 0, 2 * P)
-        w_i.append((late_codes[:, 0:K], held([P, K], U8, "w_i1_scales")))
-        for g in range(2):
-            quantize(w_i[1], E4M3, w1_turned[g][:], 2 * P * g, 2 * P * (g + 1))
-        xm_blocks.append([(xm1_first, 0), (xm1_first, 1), (xm1_rest, 0), (xm1_rest, 1)])
-        place(1, 0, table_gradient(1, 0, 1), stage("dw_staged1_0", "weighted0")[:])
         h_i = [mx_operand("h_i%d" % b) for b in range(B)]
+
+        def pack_w(b, j, copy, tag=None):
+            packed = held([P, 2 * N], BF16, "w_packed%d_%d" % (b, j), tag)
+            source = w_planes[b][:].rearrange("p (t h j c i) -> p j h c t i", t=PACK, h=2, j=2, i=4)[:, j]
+            copy(packed[:].rearrange("p (h c i t) -> p h c t i", h=2, i=4, t=PACK), source)
+            return packed
+
+        def quantize_w(b, j, packed):
+            quantize(w_d[b], E4M3, packed[:], 2 * P * j, 2 * P * (j + 1))
+
+        def dealt(rows):
+            return rows.rearrange("p (m t) -> p t m", t=PACK)
+
+        def scale_items(b, c, score, on_vector_too):
+            out = held([P, R], F32, "scaled%d_%d" % (b, c), "scaled%d" % c)
+            k = 2 * b + c // 2
+            if on_vector_too and c % 2 == 1:
+                nc.vector.tensor_scalar(by_plane(out[:]), dealt(score[:]), signed[c % 2][:, k:k + 1], None, MULT)
+            else:
+                nc.scalar.activation(by_plane(out[:]), dealt(score[:]), COPY, scale=signed[c % 2][:, k:k + 1])
+            return out
+
+        def scores_of(b, banks, row_runs):
+            scores = [bank(banks[c], "score%d_%d" % (b, c)) for c in range(4)]
+            for r0, r1 in row_runs:
+                for c in range(4):
+                    product(scores[c][:, r0:r1], w_d[b], E4M3, c, x_d[b], E4M3, r0, r1)
+            return scores
+
+        def sigmoids(b, scores, sum_banks, on_vector_too):
+            scaled = [scale_items(b, c, scores[c], on_vector_too) for c in range(4)]
+            sig = held([P, PACK * HALF], F32, "sig%d" % b)
+            for j in range(2):
+                summed = bank(sum_banks[j], "summed%d_%d" % (b, j))
+                for t in range(PACK):
+                    for half in range(2):
+                        nc.tensor.matmul(summed[:, P * t:P * (t + 1)], scaled[2 * j + half][:, P * t:P * (t + 1)], ident[:],
+                                         start=(half == 0), stop=(half == 1), is_transpose=True)
+                nc.scalar.activation(by_plane(sig[:])[:, :, P * j:P * (j + 1)], by_plane(summed[:]), SIGMOID)
+            return [sig[:, HALF * t:HALF * (t + 1)] for t in range(PACK)]
+
+        h_planes = [held([P, PACK * N], BF16, "h_planes%d" % b) for b in range(B)]
+        h_packed = [held([P, PACK * N], BF16, "h_packed%d" % b) for b in range(B)]
+
+        def form_h(b, half, sig):
+            s0 = HALF * half
+            for t in range(PACK):
+                nc.vector.scalar_tensor_tensor(h_planes[b][:, N * t + s0:N * t + s0 + HALF], sig[t],
+                                               row_weight[:, b, t:t + 1], ts_spread[b][:, s0:s0 + HALF], MULT, MULT)
+
+        def pack_h(b, half):
+            s0 = HALF * half
+            weave(on_vector, h_packed[b][:, PACK * s0:PACK * (s0 + HALF)], by_plane(h_planes[b][:])[:, :, s0:s0 + HALF])
+
+        def quantize_h(b, half):
+            s0 = HALF * half
+            quantize(h_r[b], E5M2, h_packed[b][:, PACK * s0:PACK * (s0 + HALF)], s0, s0 + HALF)
+
+        def table_gradient(b, j, k, copy, tag):
+            dw = bank(k, "dw%d_%d" % (b, j))
+            product(dw[:], xm_r[b], E4M3, j, h_r[b], E5M2)
+            staged = held([P, N], F32, "dw_staged%d_%d" % (b, j), tag)
+            copy(staged[:], dw[:])
+            return staged
+
+        def place_halves(b, j, staged):
+            for s0 in (0, HALF):
+                indirect_on_scalar(window[j][:].indirect(listed(b, s0, s0 + HALF)), staged[:, s0:s0 + HALF])
+
+        def store_window(j, queue):
+            queue.dma_start(out=out_0[P * j:P * (j + 1), :], in_=window[j][:])
+
+        def turn_h(b, banks, copy):
+            turned = held([P, PACK * R], BF16, "h_turned%d" % b)
+            for g in range(2):
+                turn = turn_words(h_planes[b], g, banks[g], "h_turn%d_%d" % (b, g))
+                copy(turned[:].bitcast(F32).rearrange("q (p g c) -> q g p c", g=2, c=4)[:, g], turn[:].rearrange("q (c p) -> q p c", c=4))
+            return turned
+
+        def row_gradient(b, banks, copy, tag, queue):
+            staged = held([P, PACK * D], F32, "gx_staged%d" % b, tag)
+            rows = out_1[b].rearrange("(j p) d -> p j d", p=P)
+            for t in range(PACK):
+                gx = bank(banks[t], "gx%d_%d" % (b, t))
+                product(gx[:], h_i[b], E5M2, t, w_i[b], E4M3)
+                copy[t // 2](staged[:, D * t:D * (t + 1)], gx[:])
+                if t % 2 == 1:
+                    queue[t // 2].dma_start(out=rows[:, t - 1:t + 1, :], in_=by_plane(staged[:])[:, t - 1:t + 1, :])
+
+        def pack_rows(name, raw, tag=None):
+            packed = held([P, PACK * K], BF16, name, tag)
+            for h in range(2):
+                weave(on_vector, packed[:, 2 * K * h:2 * K * (h + 1)], raw[:, :, HALF * h:HALF * (h + 1)])
+            return packed
+
+        x0_packed = [held([P, 2 * R], BF16, "x0_packed%d" % h) for h in range(2)]
+        for h in range(2):
+            for k in range(2):
+                weave(on_scalar, x0_packed[h][:, N * k:N * (k + 1)], x0_half[h][:, :, P * k:P * (k + 1)])
+        packed = [pack_w(0, j, on_vector) for j in range(2)]
+        for j in range(2):
+            quantize_w(0, j, packed[j])
+        for h in range(2):
+            quantize(x_d[0], E4M3, x0_packed[h][:], h * R // 2, (h + 1) * R // 2)
+        turn_w(0, 1, 4, on_scalar)
+        turn_w(1, 1, 5, on_scalar)
+        scores0 = scores_of(0, (0, 1, 2, 3), ((0, R // 2), (R // 2, R)))
+        sig0 = sigmoids(0, scores0, (0, 1), True)
+        packed = [pack_w(1, 0, on_vector, "x0_packed0"), pack_w(1, 1, on_scalar, "x0_packed1")]
+        x1_packed = pack_rows("x1_packed", x1_raw)
+        for j in range(2):
+            quantize_w(1, j, packed[j])
+        quantize(x_d[1], E4M3, x1_packed[:])
+        scores1 = scores_of(1, (4, 5, 6, 7), ((0, R),))
+        xm0_packed = [held([P, 2 * D], BF16, "xm0_packed%d" % h) for h in range(2)]
+        weave(on_vector, xm0_packed[0][:], xm_raw[0][:, :, 0:HALF])
+        for k in range(2):
+            weave(on_scalar, xm0_packed[1][:, N * k:N * (k + 1)], xm_raw[0][:, :, HALF + P * k:HALF + P * (k + 1)])
+        quantize(xm_r[0], E4M3, xm0_packed[0][:], 0, HALF)
+        for half in range(2):
+            form_h(0, half, sig0)
+            pack_h(0, half)
+            quantize_h(0, half)
+        sig1 = sigmoids(1, scores1, (2, 3), False)
+        staged = held([P, N], F32, "dw_staged0_0", "w_plane0")
+        for half in range(2):
+            s0 = HALF * half
+            dw = bank(4 + half, "dw0_0_%d" % half)
+            product(dw[:, 0:HALF], xm_r[0], E4M3, 0, h_r[0], E5M2, s0, s0 + HALF)
+            on_scalar(staged[:, s0:s0 + HALF], dw[:, 0:HALF])
+        place_halves(0, 0, staged)
+        quantize(xm_r[0], E4M3, xm0_packed[1][:], HALF, D)
+        staged = table_gradient(0, 2, 6, on_scalar, "w_plane1")
+        place_halves(0, 2, staged)
+        for half in range(2):
+            form_h(1, half, sig1)
+        xm1_packed = pack_rows("xm1_packed", xm_raw[1], "h_packed0")
+        for half in range(2):
+            pack_h(1, half)
+        quantize(xm_r[1], E4M3, xm1_packed[:])
+        for half in range(2):
+            quantize_h(1, half)
+        place_halves(1, 0, table_gradient(1, 0, 4, on_scalar, "w_plane2"))
+        store_window(0, nc.scalar)
+        h0_turned = turn_h(0, (0, 1), on_vector)
+        h1_turned = turn_h(1, (2, 3), on_vector)
+        quantize(w_i[0], E4M3, w_turned[0][:])
         quantize(h_i[0], E5M2, h0_turned[:])
-        place(1, 1, table_gradient(1, 1, 0), stage("dw_staged1_1", "scaled1_1")[:])
-        row_gradient(0, (4, 5, 7, 2), "x1_raw")
-        quantize(h_i[1], E5M2, turn_h(1, (4, 5))[:])
-        place(1, 2, table_gradient(1, 2, 6), stage("dw_staged1_2", "h_packed1")[:])
-        place(1, 3, table_gradient(1, 3, 3), stage("dw_staged1_3", "h_turned1")[:])
-        row_gradient(1, (0, 1, 7, 2), "xm_raw1")
+        quantize(w_i[1], E4M3, w_turned[1][:])
+        quantize(h_i[1], E5M2, h1_turned[:])
+        staged = table_gradient(1, 2, 7, on_vector, "h_turned1")
+        row_gradient(0, (0, 1, 2, 3), (on_scalar, on_scalar), "w_plane0", (nc.scalar, nc.scalar))
+        on_vector(window[2][:].indirect(listed(1)), staged[:])
+        store_window(2, nc.sync)
+        place_halves(0, 1, table_gradient(0, 1, 5, on_scalar, "w_plane2"))
+        staged = [table_gradient(b, 3, 6 + b, on_vector, ("x0_half1", "scaled0")[b]) for b in range(B)]
+        row_gradient(1, (0, 1, 2, 3), (on_scalar, on_vector), "x1_raw", (nc.scalar, nc.sync))
+        place_halves(1, 1, table_gradient(1, 1, 4, on_scalar, "w_plane1"))
+        store_window(1, nc.scalar)
+        for b in range(B):
+            on_vector(window[3][:].indirect(listed(b)), staged[b][:])
+        store_window(3, nc.sync)

@@ -71,6 +71,10 @@ def tile_attend_gbpr_wx_ts_kernel(tc, xT, wT, wt, ts, xm, offs, out_0, out_1):
         def weave_on_gpsimd(packed, source):
             nc.gpsimd.tensor_scalar(packed.rearrange("p (c t) -> p c t", t=PACK), source.rearrange("p t c -> p c t"), 1.0, 0.0, MULT, ADD)
 
+        warm = held([P, 2], F32, "warm")
+        nc.vector.memset(warm[:, 0:1], 0.0)
+        nc.scalar.activation(warm[:, 1:2], warm[:, 0:1], SIGMOID)
+
         offsets = lists.tile([P, B * N // 16], U16, name="offsets")
         nc.sync.dma_start(offsets[:], offs)
 
@@ -99,8 +103,6 @@ def tile_attend_gbpr_wx_ts_kernel(tc, xT, wT, wt, ts, xm, offs, out_0, out_1):
 
         ident = held([P, P], F32, "ident")
         make_identity(nc, ident[:])
-        warm = held([P, 1], F32, "warm")
-        nc.scalar.activation(warm[:], ident[:, 0:1], SIGMOID)
         window = [held([P, T], F32, "window%d" % j) for j in range(PACK)]
         for j in range(PACK):
             nc.gpsimd.memset(window[j][:], 0.0)
@@ -121,13 +123,16 @@ def tile_attend_gbpr_wx_ts_kernel(tc, xT, wT, wt, ts, xm, offs, out_0, out_1):
         ts_spread = []
         for b in range(B):
             spread = bank(6 + b, "ts_spread_bank%d" % b)
+            if b == 0:
+                spread0 = spread
             for half in range(2):
                 for j in range(2):
                     k = 2 * half + j
                     nc.tensor.transpose(spread[:, P * k:P * (k + 1)],
                                         signed[half][:, 2 * b + j:2 * b + j + 1].to_broadcast([P, P]), ident[:])
-            ts_spread.append(held([P, N], F32, "ts_spread%d" % b))
-            on_scalar(ts_spread[b][:], spread[:])
+            ts_spread.append(spread)
+        ts_spread[0] = held([P, N], F32, "ts_spread0")
+        on_scalar(ts_spread[0][:], spread0[:])
 
         w_planes = [held([P, PACK * N], BF16, "w_planes%d" % b) for b in range(B)]
         w_turned = [held([P, PACK * D], BF16, "w_turned%d" % b) for b in range(B)]
@@ -221,6 +226,17 @@ def tile_attend_gbpr_wx_ts_kernel(tc, xT, wT, wt, ts, xm, offs, out_0, out_1):
             copy(staged[:], dw[:])
             return staged
 
+        def table_gradient_half(b, half, tiles, k, tag):
+            dw = bank(k, "dw_half%d_%d" % (b, half))
+            for n, j in enumerate(tiles):
+                product(dw[:, HALF * n:HALF * (n + 1)], xm_r[b], E4M3, j, h_r[b], E5M2, HALF * half, HALF * (half + 1))
+            staged = held([P, N], F32, "dw_half_staged%d_%d" % (b, half), tag)
+            on_scalar(staged[:], dw[:])
+            return staged
+
+        def place_half(b, j, half, source):
+            indirect_on_scalar(window[j][:].indirect(listed(b, HALF * half, HALF * (half + 1))), source)
+
         def place_halves(b, j, staged):
             for s0 in (0, HALF):
                 indirect_on_scalar(window[j][:].indirect(listed(b, s0, s0 + HALF)), staged[:, s0:s0 + HALF])
@@ -235,15 +251,16 @@ def tile_attend_gbpr_wx_ts_kernel(tc, xT, wT, wt, ts, xm, offs, out_0, out_1):
                 copy(turned[:].bitcast(F32).rearrange("q (p g c) -> q g p c", g=2, c=4)[:, g], turn[:].rearrange("q (c p) -> q p c", c=4))
             return turned
 
-        def row_gradient(b, banks, copy, tag, queue):
+        def row_gradient(b, banks, copy, tag, stores):
             staged = held([P, PACK * D], F32, "gx_staged%d" % b, tag)
             rows = out_1[b].rearrange("(j p) d -> p j d", p=P)
             for t in range(PACK):
                 gx = bank(banks[t], "gx%d_%d" % (b, t))
                 product(gx[:], h_i[b], E5M2, t, w_i[b], E4M3)
-                copy[t // 2](staged[:, D * t:D * (t + 1)], gx[:])
-                if t % 2 == 1:
-                    queue[t // 2].dma_start(out=rows[:, t - 1:t + 1, :], in_=by_plane(staged[:])[:, t - 1:t + 1, :])
+                copy[t](staged[:, D * t:D * (t + 1)], gx[:])
+                if t + 1 in stores:
+                    t0, queue = stores[t + 1]
+                    queue.dma_start(out=rows[:, t0:t + 1, :], in_=by_plane(staged[:])[:, t0:t + 1, :])
 
         def pack_rows(name, raw, tag=None):
             packed = held([P, PACK * K], BF16, name, tag)
@@ -269,52 +286,54 @@ def tile_attend_gbpr_wx_ts_kernel(tc, xT, wT, wt, ts, xm, offs, out_0, out_1):
         for j in range(2):
             quantize_w(1, j, packed[j])
         quantize(x_d[1], E4M3, x1_packed[:])
-        scores1 = scores_of(1, (4, 5, 6, 7), ((0, R),))
+        scores1 = scores_of(1, (4, 5, 6, 2), ((0, R),))
         xm0_packed = [held([P, 2 * D], BF16, "xm0_packed%d" % h) for h in range(2)]
         weave(on_vector, xm0_packed[0][:], xm_raw[0][:, :, 0:HALF])
         for k in range(2):
             weave(on_scalar, xm0_packed[1][:, N * k:N * (k + 1)], xm_raw[0][:, :, HALF + P * k:HALF + P * (k + 1)])
-        quantize(xm_r[0], E4M3, xm0_packed[0][:], 0, HALF)
+        for h in range(2):
+            quantize(xm_r[0], E4M3, xm0_packed[h][:], HALF * h, HALF * (h + 1))
         for half in range(2):
             form_h(0, half, sig0)
             pack_h(0, half)
             quantize_h(0, half)
-        sig1 = sigmoids(1, scores1, (2, 3), False)
-        staged = held([P, N], F32, "dw_staged0_0", "w_plane0")
+        sig1 = sigmoids(1, scores1, (3, 0), False)
         for half in range(2):
-            s0 = HALF * half
-            dw = bank(4 + half, "dw0_0_%d" % half)
-            product(dw[:, 0:HALF], xm_r[0], E4M3, 0, h_r[0], E5M2, s0, s0 + HALF)
-            on_scalar(staged[:, s0:s0 + HALF], dw[:, 0:HALF])
-        place_halves(0, 0, staged)
-        quantize(xm_r[0], E4M3, xm0_packed[1][:], HALF, D)
-        staged = table_gradient(0, 2, 6, on_scalar, "w_plane1")
-        place_halves(0, 2, staged)
+            staged = table_gradient_half(0, half, (0, 2), 4 + half, "w_plane%d" % half)
+            for n, j in enumerate((0, 2)):
+                place_half(0, j, half, staged[:, HALF * n:HALF * (n + 1)])
         for half in range(2):
             form_h(1, half, sig1)
-        xm1_packed = pack_rows("xm1_packed", xm_raw[1], "h_packed0")
+        xm1_packed = held([P, PACK * D], BF16, "xm1_packed", "h_packed0")
+        weave_on_gpsimd(xm1_packed[:], xm_raw[1][:])
+        h0_turned = turn_h(0, (0, 1), on_vector)
         for half in range(2):
             pack_h(1, half)
         quantize(xm_r[1], E4M3, xm1_packed[:])
         for half in range(2):
             quantize_h(1, half)
-        place_halves(1, 0, table_gradient(1, 0, 4, on_scalar, "w_plane2"))
-        store_window(0, nc.scalar)
-        h0_turned = turn_h(0, (0, 1), on_vector)
-        h1_turned = turn_h(1, (2, 3), on_vector)
         quantize(w_i[0], E4M3, w_turned[0][:])
         quantize(h_i[0], E5M2, h0_turned[:])
+        staged = [table_gradient(1, 0, 5, on_scalar, "w_plane2"), table_gradient(0, 1, 4, on_scalar, "h_turned0")]
+        for half in range(2):
+            place_half(1, 0, half, staged[0][:, HALF * half:HALF * (half + 1)])
+            if half == 1:
+                store_window(0, nc.scalar)
+            place_half(0, 1, half, staged[1][:, HALF * half:HALF * (half + 1)])
+        h1_turned = turn_h(1, (2, 3), on_vector)
         quantize(w_i[1], E4M3, w_turned[1][:])
         quantize(h_i[1], E5M2, h1_turned[:])
-        staged = table_gradient(1, 2, 7, on_vector, "h_turned1")
-        row_gradient(0, (0, 1, 2, 3), (on_scalar, on_scalar), "w_plane0", (nc.scalar, nc.scalar))
+        row_gradient(0, (6, 0, 1, 2), [on_vector] * 4, "w_plane3", {2: (0, nc.sync), 4: (2, nc.sync)})
+        staged = table_gradient(1, 2, 3, on_vector, "h_turned1")
         on_vector(window[2][:].indirect(listed(1)), staged[:])
         store_window(2, nc.sync)
-        place_halves(0, 1, table_gradient(0, 1, 5, on_scalar, "w_plane2"))
-        staged = [table_gradient(b, 3, 6 + b, on_vector, ("x0_half1", "scaled0")[b]) for b in range(B)]
-        row_gradient(1, (0, 1, 2, 3), (on_scalar, on_vector), "x1_raw", (nc.scalar, nc.sync))
-        place_halves(1, 1, table_gradient(1, 1, 4, on_scalar, "w_plane1"))
-        store_window(1, nc.scalar)
+        staged = held([P, B * N], F32, "dw_staged_last", "xm_raw0")
         for b in range(B):
-            on_vector(window[3][:].indirect(listed(b)), staged[b][:])
+            dw = bank((6, 0)[b], "dw%d_3" % b)
+            product(dw[:], xm_r[b], E4M3, 3, h_r[b], E5M2)
+            on_vector(staged[:, N * b:N * (b + 1)], dw[:])
+        row_gradient(1, (1, 2, 3, 7), [on_vector] + [on_scalar] * 3, "x1_raw", {1: (0, nc.sync), 4: (1, nc.scalar)})
+        place_halves(1, 1, table_gradient(1, 1, 2, on_scalar, "w_plane2"))
+        store_window(1, nc.scalar)
+        on_vector(window[3][:].indirect(offsets[:]), staged[:])
         store_window(3, nc.sync)

@@ -9,7 +9,6 @@ FLOPS = 3 * 2 * B * N * D * R
 F32 = mybir.dt.float32
 BF16 = mybir.dt.bfloat16
 U32 = mybir.dt.uint32
-I32 = mybir.dt.int32
 U16 = mybir.dt.uint16
 U8 = mybir.dt.uint8
 E4M3 = mybir.dt.float8_e4m3fn_x4
@@ -72,8 +71,11 @@ def tile_attend_gbpr_wx_ts_kernel(tc, xT, wT, wt, ts, xm, offs, out_0, out_1):
             nc.gpsimd.tensor_scalar(packed.rearrange("p (c t) -> p c t", t=PACK), source.rearrange("p t c -> p c t"), 1.0, 0.0, MULT, ADD)
 
         warm = held([P, 2], F32, "warm")
-        nc.vector.memset(warm[:, 0:1], 0.0)
+        nc.gpsimd.memset(warm[:, 0:1], 0.0)
         nc.scalar.activation(warm[:, 1:2], warm[:, 0:1], SIGMOID)
+
+        ident = held([P, P], F32, "ident")
+        make_identity(nc, ident[:])
 
         offsets = lists.tile([P, B * N // 16], U16, name="offsets")
         nc.sync.dma_start(offsets[:], offs)
@@ -85,7 +87,7 @@ def tile_attend_gbpr_wx_ts_kernel(tc, xT, wT, wt, ts, xm, offs, out_0, out_1):
         nc.scalar.dma_start(out=row_weight[:], in_=wt.rearrange("b (p t) o -> p b (t o)", t=PACK))
         ts_row = held([P, T], F32, "ts_row")
         nc.sync.dma_start(out=ts_row[P - 1:P, :], in_=ts[0:1, :])
-        nc.vector.memset(ts_row[0:P - 1, :].bitcast(I32), 0)
+        nc.gpsimd.memset(ts_row[0:P - 1, :], 0.0)
 
         w_rows = wT.rearrange("(p t) c -> t p c", t=PACK)
         w_plane = [held([P, T], F32, "w_plane%d" % t) for t in range(PACK)]
@@ -101,10 +103,8 @@ def tile_attend_gbpr_wx_ts_kernel(tc, xT, wT, wt, ts, xm, offs, out_0, out_1):
         for b in range(B):
             nc.sync.dma_start(out=xm_raw[b][:], in_=xm[b].rearrange("(p t) d -> p t d", t=PACK))
 
-        ident = held([P, P], F32, "ident")
-        make_identity(nc, ident[:])
-        window = [held([P, T], F32, "window%d" % j) for j in range(PACK)]
-        for j in range(PACK):
+        window = [held([P, T], F32, "window%d" % j) for j in range(PACK - 1)]
+        for j in range(PACK - 1):
             nc.gpsimd.memset(window[j][:], 0.0)
 
         ts_listed = held([P, B * N], F32, "ts_listed")
@@ -323,8 +323,10 @@ def tile_attend_gbpr_wx_ts_kernel(tc, xT, wT, wt, ts, xm, offs, out_0, out_1):
         h1_turned = turn_h(1, (2, 3), on_vector)
         quantize(w_i[1], E4M3, w_turned[1][:])
         quantize(h_i[1], E5M2, h1_turned[:])
+        window.append(held([P, T], F32, "window3", "h_turned1"))
+        nc.gpsimd.memset(window[3][:], 0.0)
         row_gradient(0, (6, 0, 1, 2), [on_vector] * 4, "w_plane3", {2: (0, nc.sync), 4: (2, nc.sync)})
-        staged = table_gradient(1, 2, 3, on_vector, "h_turned1")
+        staged = table_gradient(1, 2, 3, on_vector, "h_planes1")
         on_vector(window[2][:].indirect(listed(1)), staged[:])
         store_window(2, nc.sync)
         staged = held([P, B * N], F32, "dw_staged_last", "xm_raw0")
@@ -332,8 +334,8 @@ def tile_attend_gbpr_wx_ts_kernel(tc, xT, wT, wt, ts, xm, offs, out_0, out_1):
             dw = bank((6, 0)[b], "dw%d_3" % b)
             product(dw[:], xm_r[b], E4M3, 3, h_r[b], E5M2)
             on_vector(staged[:, N * b:N * (b + 1)], dw[:])
-        row_gradient(1, (1, 2, 3, 7), [on_vector] + [on_scalar] * 3, "x1_raw", {1: (0, nc.sync), 4: (1, nc.scalar)})
-        place_halves(1, 1, table_gradient(1, 1, 2, on_scalar, "w_plane2"))
+        row_gradient(1, (1, 2, 3, 6), [on_vector] + [on_scalar] * 3, "x1_raw", {1: (0, nc.sync), 4: (1, nc.scalar)})
+        place_halves(1, 1, table_gradient(1, 1, 7, on_scalar, "h_planes1"))
         store_window(1, nc.scalar)
         on_vector(window[3][:].indirect(offsets[:]), staged[:])
         store_window(3, nc.sync)

@@ -103,8 +103,8 @@ def tile_attend_gbpr_wx_ts_kernel(tc, xT, wT, wt, ts, xm, offs, out_0, out_1):
         for b in range(B):
             nc.sync.dma_start(out=xm_raw[b][:], in_=xm[b].rearrange("(p t) d -> p t d", t=PACK))
 
-        window = [held([P, T], F32, "window%d" % j) for j in range(PACK - 1)]
-        for j in range(PACK - 1):
+        window = [held([P, T], F32, "window%d" % j) for j in range(PACK)]
+        for j in range(PACK):
             nc.gpsimd.memset(window[j][:], 0.0)
 
         ts_listed = held([P, B * N], F32, "ts_listed")
@@ -186,20 +186,23 @@ def tile_attend_gbpr_wx_ts_kernel(tc, xT, wT, wt, ts, xm, offs, out_0, out_1):
         def scores_of(b, banks, row_runs):
             scores = [bank(banks[c], "score%d_%d" % (b, c)) for c in range(4)]
             for r0, r1 in row_runs:
-                for c in range(4):
+                for c in (0, 2, 1, 3):
                     product(scores[c][:, r0:r1], w_d[b], E4M3, c, x_d[b], E4M3, r0, r1)
             return scores
 
         def sigmoids(b, scores, sum_banks, on_vector_too):
-            scaled = [scale_items(b, c, scores[c], on_vector_too) for c in range(4)]
             sig = held([P, PACK * HALF], F32, "sig%d" % b)
+            summed = [None, None]
+            for half in range(2):
+                for j in range(2):
+                    scaled = scale_items(b, 2 * j + half, scores[2 * j + half], on_vector_too)
+                    if half == 0:
+                        summed[j] = bank(sum_banks[j], "summed%d_%d" % (b, j))
+                    for t in range(PACK):
+                        nc.tensor.matmul(summed[j][:, P * t:P * (t + 1)], scaled[:, P * t:P * (t + 1)], ident[:],
+                                         start=(half == 0 and t == 0), stop=(half == 1 and t == PACK - 1), is_transpose=True)
             for j in range(2):
-                summed = bank(sum_banks[j], "summed%d_%d" % (b, j))
-                for t in range(PACK):
-                    for half in range(2):
-                        nc.tensor.matmul(summed[:, P * t:P * (t + 1)], scaled[2 * j + half][:, P * t:P * (t + 1)], ident[:],
-                                         start=(half == 0), stop=(half == 1), is_transpose=True)
-                nc.scalar.activation(by_plane(sig[:])[:, :, P * j:P * (j + 1)], by_plane(summed[:]), SIGMOID)
+                nc.scalar.activation(by_plane(sig[:])[:, :, P * j:P * (j + 1)], by_plane(summed[j][:]), SIGMOID)
             return [sig[:, HALF * t:HALF * (t + 1)] for t in range(PACK)]
 
         h_planes = [held([P, PACK * N], BF16, "h_planes%d" % b) for b in range(B)]
@@ -262,6 +265,14 @@ def tile_attend_gbpr_wx_ts_kernel(tc, xT, wT, wt, ts, xm, offs, out_0, out_1):
                     t0, queue = stores[t + 1]
                     queue.dma_start(out=rows[:, t0:t + 1, :], in_=by_plane(staged[:])[:, t0:t + 1, :])
 
+        def row_tile(b, t, k, copy, staged):
+            gx = bank(k, "gx%d_%d" % (b, t))
+            product(gx[:], h_i[b], E5M2, t, w_i[b], E4M3)
+            copy(staged[:, D * t:D * (t + 1)], gx[:])
+
+        def store_rows(b, t0, t1, queue, staged):
+            queue.dma_start(out=out_1[b].rearrange("(j p) d -> p j d", p=P)[:, t0:t1, :], in_=by_plane(staged[:])[:, t0:t1, :])
+
         def pack_rows(name, raw, tag=None):
             packed = held([P, PACK * K], BF16, name, tag)
             for h in range(2):
@@ -280,28 +291,28 @@ def tile_attend_gbpr_wx_ts_kernel(tc, xT, wT, wt, ts, xm, offs, out_0, out_1):
         turn_w(0, 1, 4, on_scalar)
         turn_w(1, 1, 5, on_scalar)
         scores0 = scores_of(0, (0, 1, 2, 3), ((0, R // 2), (R // 2, R)))
-        sig0 = sigmoids(0, scores0, (0, 1), True)
-        packed = [pack_w(1, 0, on_vector, "x0_packed0"), pack_w(1, 1, on_scalar, "x0_packed1")]
+        sig0 = sigmoids(0, scores0, (0, 2), False)
+        packed = [pack_w(1, 0, on_vector, "x0_packed0"), pack_w(1, 1, on_vector, "x0_packed1")]
         x1_packed = pack_rows("x1_packed", x1_raw)
         for j in range(2):
             quantize_w(1, j, packed[j])
         quantize(x_d[1], E4M3, x1_packed[:])
-        scores1 = scores_of(1, (4, 5, 6, 2), ((0, R),))
-        xm0_packed = [held([P, 2 * D], BF16, "xm0_packed%d" % h) for h in range(2)]
-        weave(on_vector, xm0_packed[0][:], xm_raw[0][:, :, 0:HALF])
-        for k in range(2):
-            weave(on_scalar, xm0_packed[1][:, N * k:N * (k + 1)], xm_raw[0][:, :, HALF + P * k:HALF + P * (k + 1)])
-        for h in range(2):
-            quantize(xm_r[0], E4M3, xm0_packed[h][:], HALF * h, HALF * (h + 1))
+        scores1 = scores_of(1, (4, 1, 5, 6), ((0, R),))
+        xm0_packed = held([P, 2 * D], BF16, "xm0_packed")
+        weave(on_vector, xm0_packed[:], xm_raw[0][:, :, 0:HALF])
+        quantize(xm_r[0], E4M3, xm0_packed[:], 0, HALF)
         for half in range(2):
             form_h(0, half, sig0)
             pack_h(0, half)
             quantize_h(0, half)
         sig1 = sigmoids(1, scores1, (3, 0), False)
         for half in range(2):
-            staged = table_gradient_half(0, half, (0, 2), 4 + half, "w_plane%d" % half)
-            for n, j in enumerate((0, 2)):
+            staged = table_gradient_half(0, half, (0, 1), 4 + half, "w_plane%d" % half)
+            for n, j in enumerate((0, 1)):
                 place_half(0, j, half, staged[:, HALF * n:HALF * (n + 1)])
+        xm0_late = held([P, 2 * D], BF16, "xm0_late")
+        weave(on_vector, xm0_late[:], xm_raw[0][:, :, HALF:D])
+        quantize(xm_r[0], E4M3, xm0_late[:], HALF, D)
         for half in range(2):
             form_h(1, half, sig1)
         xm1_packed = held([P, PACK * D], BF16, "xm1_packed", "h_packed0")
@@ -314,28 +325,42 @@ def tile_attend_gbpr_wx_ts_kernel(tc, xT, wT, wt, ts, xm, offs, out_0, out_1):
             quantize_h(1, half)
         quantize(w_i[0], E4M3, w_turned[0][:])
         quantize(h_i[0], E5M2, h0_turned[:])
-        staged = [table_gradient(1, 0, 5, on_scalar, "w_plane2"), table_gradient(0, 1, 4, on_scalar, "h_turned0")]
-        for half in range(2):
-            place_half(1, 0, half, staged[0][:, HALF * half:HALF * (half + 1)])
-            if half == 1:
-                store_window(0, nc.scalar)
-            place_half(0, 1, half, staged[1][:, HALF * half:HALF * (half + 1)])
+        staged = table_gradient(1, 0, 7, on_vector, "w_plane2")
         h1_turned = turn_h(1, (2, 3), on_vector)
-        quantize(w_i[1], E4M3, w_turned[1][:])
-        quantize(h_i[1], E5M2, h1_turned[:])
-        window.append(held([P, T], F32, "window3", "h_turned1"))
-        nc.gpsimd.memset(window[3][:], 0.0)
-        row_gradient(0, (6, 0, 1, 2), [on_vector] * 4, "w_plane3", {2: (0, nc.sync), 4: (2, nc.sync)})
-        staged = table_gradient(1, 2, 3, on_vector, "h_planes1")
-        on_vector(window[2][:].indirect(listed(1)), staged[:])
-        store_window(2, nc.sync)
-        staged = held([P, B * N], F32, "dw_staged_last", "xm_raw0")
-        for b in range(B):
-            dw = bank((6, 0)[b], "dw%d_3" % b)
-            product(dw[:], xm_r[b], E4M3, 3, h_r[b], E5M2)
-            on_vector(staged[:, N * b:N * (b + 1)], dw[:])
-        row_gradient(1, (1, 2, 3, 6), [on_vector] + [on_scalar] * 3, "x1_raw", {1: (0, nc.sync), 4: (1, nc.scalar)})
-        place_halves(1, 1, table_gradient(1, 1, 7, on_scalar, "h_planes1"))
+        gx0 = held([P, PACK * D], F32, "gx_staged0", "w_plane3")
+        row_tile(0, 0, 1, on_vector, gx0)
+        row_tile(0, 1, 6, on_vector, gx0)
+        store_rows(0, 0, 2, nc.sync, gx0)
+        on_vector(window[0][:].indirect(listed(1)), staged[:])
+        store_window(0, nc.sync)
+        staged = [table_gradient(0, 2, 4, on_scalar, "h_turned0"), table_gradient(1, 1, 5, on_scalar, "h_planes1")]
+        for half in range(2):
+            place_half(0, 2, half, staged[0][:, HALF * half:HALF * (half + 1)])
+            place_half(1, 1, half, staged[1][:, HALF * half:HALF * (half + 1)])
         store_window(1, nc.scalar)
-        on_vector(window[3][:].indirect(offsets[:]), staged[:])
+        quantize(w_i[1], E4M3, w_turned[1][:])
+        last = held([P, B * N], F32, "dw_staged_last", "h_packed1")
+
+        def stage_last(b, k):
+            dw = bank(k, "dw%d_3" % b)
+            product(dw[:], xm_r[b], E4M3, 3, h_r[b], E5M2)
+            on_vector(last[:, N * b:N * (b + 1)], dw[:])
+
+        stage_last(0, 0)
+        quantize(h_i[1], E5M2, h1_turned[:])
+        gx1 = held([P, PACK * D], F32, "gx_staged1", "x1_raw")
+        staged = table_gradient(1, 2, 0, on_scalar, None)
+        for half in range(2):
+            row_tile(1, 2 + half, 4 + half, on_scalar, gx1)
+            place_half(1, 2, half, staged[:, HALF * half:HALF * (half + 1)])
+        store_rows(1, 2, 4, nc.sync, gx1)
+        store_window(2, nc.scalar)
+        row_tile(0, 2, 7, on_vector, gx0)
+        row_tile(0, 3, 2, on_vector, gx0)
+        store_rows(0, 2, 4, nc.sync, gx0)
+        stage_last(1, 3)
+        row_tile(1, 0, 1, on_vector, gx1)
+        row_tile(1, 1, 6, on_vector, gx1)
+        store_rows(1, 0, 2, nc.sync, gx1)
+        on_vector(window[3][:].indirect(offsets[:]), last[:])
         store_window(3, nc.sync)

@@ -160,7 +160,7 @@ def tile_attend_gbpr_wx_ts_kernel(tc, xT, wT, wt, ts, xm, offs, out_0, out_1):
         w_i = [mx_operand("w_i%d" % b) for b in range(B)]
         xm_r = [mx_operand("xm_r%d" % b) for b in range(B)]
         h_r = [mx_operand("h_r%d" % b) for b in range(B)]
-        h_i = [mx_operand("h_i%d" % b) for b in range(B)]
+        h_i = [mx_operand("h_i0"), None]
 
         def pack_w(b, j, copy, tag=None):
             packed = held([P, 2 * N], BF16, "w_packed%d_%d" % (b, j), tag)
@@ -206,7 +206,7 @@ def tile_attend_gbpr_wx_ts_kernel(tc, xT, wT, wt, ts, xm, offs, out_0, out_1):
             return [sig[:, HALF * t:HALF * (t + 1)] for t in range(PACK)]
 
         h_planes = [held([P, PACK * N], BF16, "h_planes%d" % b) for b in range(B)]
-        h_packed = [held([P, PACK * N], BF16, "h_packed%d" % b) for b in range(B)]
+        h_packed = [held([P, PACK * N], BF16, "h_packed0")]
 
         def form_h(b, half, sig):
             s0 = HALF * half
@@ -305,62 +305,63 @@ def tile_attend_gbpr_wx_ts_kernel(tc, xT, wT, wt, ts, xm, offs, out_0, out_1):
             form_h(0, half, sig0)
             pack_h(0, half)
             quantize_h(0, half)
+            if half == 0:
+                for b in range(B):
+                    quantize(w_i[b], E4M3, w_turned[b][:])
         sig1 = sigmoids(1, scores1, (3, 0), False)
-        for half in range(2):
-            staged = table_gradient_half(0, half, (0, 1), 4 + half, "w_plane%d" % half)
-            for n, j in enumerate((0, 1)):
-                place_half(0, j, half, staged[:, HALF * n:HALF * (n + 1)])
+        staged = table_gradient_half(0, 0, (0, 1), 4, "w_plane0")
+        for j in range(2):
+            place_half(0, j, 0, staged[:, HALF * j:HALF * (j + 1)])
+        staged = table_gradient_half(0, 1, (0, 1), 5, "w_plane1")
         xm0_late = held([P, 2 * D], BF16, "xm0_late")
         weave(on_vector, xm0_late[:], xm_raw[0][:, :, HALF:D])
         quantize(xm_r[0], E4M3, xm0_late[:], HALF, D)
+        staged02 = table_gradient(0, 2, 6, on_scalar, None)
+        for j in range(2):
+            place_half(0, j, 1, staged[:, HALF * j:HALF * (j + 1)])
+            place_half(0, 2, j, staged02[:, HALF * j:HALF * (j + 1)])
         for half in range(2):
             form_h(1, half, sig1)
         xm1_packed = held([P, PACK * D], BF16, "xm1_packed", "h_packed0")
         weave_on_gpsimd(xm1_packed[:], xm_raw[1][:])
         h0_turned = turn_h(0, (0, 1), on_vector)
-        for half in range(2):
-            pack_h(1, half)
         quantize(xm_r[1], E4M3, xm1_packed[:])
-        for half in range(2):
-            quantize_h(1, half)
-        quantize(w_i[0], E4M3, w_turned[0][:])
         quantize(h_i[0], E5M2, h0_turned[:])
-        staged = table_gradient(1, 0, 7, on_vector, "w_plane2")
+        h1_packed = held([P, PACK * N], BF16, "h_packed1", "h_packed0")
+        weave_on_gpsimd(h1_packed[:], by_plane(h_planes[1][:]))
+        quantize(h_r[1], E5M2, h1_packed[:])
         h1_turned = turn_h(1, (2, 3), on_vector)
-        gx0 = held([P, PACK * D], F32, "gx_staged0", "w_plane3")
-        row_tile(0, 0, 1, on_vector, gx0)
-        row_tile(0, 1, 6, on_vector, gx0)
-        store_rows(0, 0, 2, nc.sync, gx0)
-        on_vector(window[0][:].indirect(listed(1)), staged[:])
-        store_window(0, nc.sync)
-        staged = [table_gradient(0, 2, 4, on_scalar, "h_turned0"), table_gradient(1, 1, 5, on_scalar, "h_planes1")]
-        for half in range(2):
-            place_half(0, 2, half, staged[0][:, HALF * half:HALF * (half + 1)])
-            place_half(1, 1, half, staged[1][:, HALF * half:HALF * (half + 1)])
-        store_window(1, nc.scalar)
-        quantize(w_i[1], E4M3, w_turned[1][:])
-        last = held([P, B * N], F32, "dw_staged_last", "h_packed1")
+        h_i[1] = mx_operand("h_i1", "h_planes1")
+        quantize(h_i[1], E5M2, h1_turned[:])
+        staged = table_gradient(1, 0, 2, on_vector, "w_plane2")
+        last = held([P, B * N], F32, "dw_staged_last")
 
         def stage_last(b, k):
             dw = bank(k, "dw%d_3" % b)
             product(dw[:], xm_r[b], E4M3, 3, h_r[b], E5M2)
             on_vector(last[:, N * b:N * (b + 1)], dw[:])
 
-        stage_last(0, 0)
-        quantize(h_i[1], E5M2, h1_turned[:])
+        gx0 = held([P, PACK * D], F32, "gx_staged0", "w_plane3")
+        stage_last(0, 7)
+        for t, k in enumerate((4, 0, 1, 7)):
+            row_tile(0, t, k, on_vector, gx0)
+            if t % 2 == 1:
+                store_rows(0, t - 1, t + 1, nc.sync, gx0)
+        on_vector(window[0][:].indirect(listed(1)), staged[:])
+        store_window(0, nc.sync)
+        staged = [table_gradient(1, 1, 5, on_scalar, None), table_gradient(1, 2, 6, on_scalar, None)]
         gx1 = held([P, PACK * D], F32, "gx_staged1", "x1_raw")
-        staged = table_gradient(1, 2, 0, on_scalar, None)
-        for half in range(2):
-            row_tile(1, 2 + half, 4 + half, on_scalar, gx1)
-            place_half(1, 2, half, staged[:, HALF * half:HALF * (half + 1)])
+        row_tile(1, 2, 3, on_scalar, gx1)
+        row_tile(1, 3, 4, on_scalar, gx1)
         store_rows(1, 2, 4, nc.sync, gx1)
+        for half in range(2):
+            for j in (1, 2):
+                place_half(1, j, half, staged[j - 1][:, HALF * half:HALF * (half + 1)])
+        store_window(1, nc.sync)
         store_window(2, nc.scalar)
-        row_tile(0, 2, 7, on_vector, gx0)
-        row_tile(0, 3, 2, on_vector, gx0)
-        store_rows(0, 2, 4, nc.sync, gx0)
-        stage_last(1, 3)
-        row_tile(1, 0, 1, on_vector, gx1)
-        row_tile(1, 1, 6, on_vector, gx1)
-        store_rows(1, 0, 2, nc.sync, gx1)
+        stage_last(1, 7)
+        row_tile(1, 0, 0, on_vector, gx1)
+        row_tile(1, 1, 2, on_vector, gx1)
+        store_rows(1, 0, 2, nc.gpsimd, gx1)
         on_vector(window[3][:].indirect(offsets[:]), last[:])
         store_window(3, nc.sync)

@@ -247,12 +247,10 @@ def tile_attend_gbpr_wx_ts_kernel(tc, xT, wT, wt, ts, xm, offs, out_0, out_1):
         def store_window(j, queue):
             queue.dma_start(out=out_0[P * j:P * (j + 1), :], in_=window[j][:])
 
-        def turn_h(b, banks, copy):
-            turned = held([P, PACK * R], BF16, "h_turned%d" % b)
+        def turn_h(b, banks, copy, turned):
             for g in range(2):
                 turn = turn_words(h_planes[b], g, banks[g], "h_turn%d_%d" % (b, g))
-                copy(turned[:].bitcast(F32).rearrange("q (p g c) -> q g p c", g=2, c=4)[:, g], turn[:].rearrange("q (c p) -> q p c", c=4))
-            return turned
+                copy(turned.bitcast(F32).rearrange("q (p g c) -> q g p c", g=2, c=4)[:, g], turn[:].rearrange("q (c p) -> q p c", c=4))
 
         def row_gradient(b, banks, copy, tag, stores):
             staged = held([P, PACK * D], F32, "gx_staged%d" % b, tag)
@@ -322,18 +320,16 @@ def tile_attend_gbpr_wx_ts_kernel(tc, xT, wT, wt, ts, xm, offs, out_0, out_1):
             place_half(0, 2, j, staged02[:, HALF * j:HALF * (j + 1)])
         for half in range(2):
             form_h(1, half, sig1)
-        xm1_packed = held([P, PACK * D], BF16, "xm1_packed", "h_packed0")
-        weave_on_gpsimd(xm1_packed[:], xm_raw[1][:])
-        h0_turned = turn_h(0, (0, 1), on_vector)
-        quantize(xm_r[1], E4M3, xm1_packed[:])
-        quantize(h_i[0], E5M2, h0_turned[:])
+        both = held([P, PACK * (D + R)], BF16, "xm1_packed_h0_turned", "h_packed0")
+        xm1_packed, h0_turned = both[:, 0:PACK * D], both[:, PACK * D:PACK * (D + R)]
+        weave_on_gpsimd(xm1_packed, xm_raw[1][:])
+        turn_h(0, (0, 1), on_vector, h0_turned)
+        quantize(xm_r[1], E4M3, xm1_packed)
+        quantize(h_i[0], E5M2, h0_turned)
         h1_packed = held([P, PACK * N], BF16, "h_packed1", "h_packed0")
         weave_on_gpsimd(h1_packed[:], by_plane(h_planes[1][:]))
-        quantize(h_r[1], E5M2, h1_packed[:])
-        h1_turned = turn_h(1, (2, 3), on_vector)
-        h_i[1] = mx_operand("h_i1", "h_planes1")
-        quantize(h_i[1], E5M2, h1_turned[:])
-        staged = table_gradient(1, 0, 2, on_vector, "w_plane2")
+        h1_turned = held([P, PACK * R], BF16, "h_turned1")
+        turn_h(1, (2, 3), on_vector, h1_turned[:])
         last = held([P, B * N], F32, "dw_staged_last")
 
         def stage_last(b, k):
@@ -343,10 +339,15 @@ def tile_attend_gbpr_wx_ts_kernel(tc, xT, wT, wt, ts, xm, offs, out_0, out_1):
 
         gx0 = held([P, PACK * D], F32, "gx_staged0", "w_plane3")
         stage_last(0, 7)
-        for t, k in enumerate((4, 0, 1, 7)):
+        for t, k in enumerate((4, 0, 1)):
             row_tile(0, t, k, on_vector, gx0)
-            if t % 2 == 1:
-                store_rows(0, t - 1, t + 1, nc.sync, gx0)
+        store_rows(0, 0, 3, nc.sync, gx0)
+        quantize(h_r[1], E5M2, h1_packed[:])
+        h_i[1] = mx_operand("h_i1", "h_planes1")
+        quantize(h_i[1], E5M2, h1_turned[:])
+        staged = table_gradient(1, 0, 2, on_vector, "w_plane2")
+        row_tile(0, 3, 7, on_vector, gx0)
+        store_rows(0, 3, 4, nc.sync, gx0)
         on_vector(window[0][:].indirect(listed(1)), staged[:])
         store_window(0, nc.sync)
         staged = [table_gradient(1, 1, 5, on_scalar, None), table_gradient(1, 2, 6, on_scalar, None)]
@@ -362,6 +363,6 @@ def tile_attend_gbpr_wx_ts_kernel(tc, xT, wT, wt, ts, xm, offs, out_0, out_1):
         stage_last(1, 7)
         row_tile(1, 0, 0, on_vector, gx1)
         row_tile(1, 1, 2, on_vector, gx1)
-        store_rows(1, 0, 2, nc.gpsimd, gx1)
+        store_rows(1, 0, 2, nc.scalar, gx1)
         on_vector(window[3][:].indirect(offsets[:]), last[:])
         store_window(3, nc.sync)

@@ -93,10 +93,8 @@ def tile_attend_gbpr_wx_ts_kernel(tc, xT, wT, wt, ts, xm, offs, out_0, out_1):
         w_plane = [held([P, T], F32, "w_plane%d" % t) for t in range(PACK)]
         for t in range(PACK):
             nc.sync.dma_start(out=w_plane[t][:], in_=w_rows[t])
-        x0_half = [held([P, PACK, R // 2], F32, "x0_half%d" % h) for h in range(2)]
-        x0_rows = xT[0].rearrange("(p j) (h r) -> h p j r", j=PACK, h=2)
-        for h in range(2):
-            nc.sync.dma_start(out=x0_half[h][:], in_=x0_rows[h])
+        x0_raw = held([P, PACK, R], F32, "x0_raw")
+        nc.sync.dma_start(out=x0_raw[:], in_=xT[0].rearrange("(p j) r -> p j r", j=PACK))
         x1_raw = held([P, PACK, R], F32, "x1_raw")
         xm_raw = [held([P, PACK, D], F32, "xm_raw%d" % b) for b in range(B)]
         nc.sync.dma_start(out=x1_raw[:], in_=xT[1].rearrange("(p j) r -> p j r", j=PACK))
@@ -135,22 +133,32 @@ def tile_attend_gbpr_wx_ts_kernel(tc, xT, wT, wt, ts, xm, offs, out_0, out_1):
         on_scalar(ts_spread[0][:], spread0[:])
 
         w_planes = [held([P, PACK * N], BF16, "w_planes%d" % b) for b in range(B)]
-        w_turned = [held([P, PACK * D], BF16, "w_turned%d" % b) for b in range(B)]
+        woven_early = held([P, B * PACK * D + PACK * N + 2 * D], BF16, "woven_early")
+        w_turned = [woven_early[:, PACK * D * b:PACK * D * (b + 1)] for b in range(B)]
+        h_packed = [woven_early[:, B * PACK * D:B * PACK * D + PACK * N]]
+        xm0_late = woven_early[:, B * PACK * D + PACK * N:B * PACK * D + PACK * N + 2 * D]
 
         def turn_words(source, g, k, name):
             turn = bank(k, name)
             for c in range(4):
                 t = 2 * g + c // 2
                 nc.tensor.transpose(turn[:, P * c:P * (c + 1)], source[:, N * t:N * (t + 1)].bitcast(F32)[:, c % 2::2], ident[:])
-            return turn
+            return turn[:].rearrange("q (t e p) -> q t p e", t=2, e=2)
+
+        def as_words(turned):
+            return turned.bitcast(F32).rearrange("q (t p e) -> q t p e", t=2, e=2)
 
         def turn_w(b, g, k, copy):
-            turn = turn_words(w_planes[b], g, k, "w_turn%d_%d" % (b, g))
-            copy(w_turned[b][:].bitcast(F32).rearrange("q (p g c) -> q g p c", g=2, c=4)[:, g], turn[:].rearrange("q (c p) -> q p c", c=4))
+            copy(as_words(w_turned[b][:, 2 * D * g:2 * D * (g + 1)]), turn_words(w_planes[b], g, k, "w_turn%d_%d" % (b, g)))
 
         for t in range(PACK):
-            on_vector(w_planes[0][:, N * t:N * (t + 1)], w_plane[t][:].indirect(listed(0)))
-            (indirect_on_scalar if t >= 1 else on_vector)(w_planes[1][:, N * t:N * (t + 1)], w_plane[t][:].indirect(listed(1)))
+            if t < PACK - 1:
+                on_vector(w_planes[0][:, N * t:N * (t + 1)], w_plane[t][:].indirect(listed(0)))
+                (indirect_on_scalar if t >= 1 else on_vector)(w_planes[1][:, N * t:N * (t + 1)], w_plane[t][:].indirect(listed(1)))
+            else:
+                for b in range(B):
+                    for s0, gather in ((0, on_vector), (HALF, indirect_on_scalar)):
+                        gather(w_planes[b][:, N * t + s0:N * t + s0 + HALF], w_plane[t][:].indirect(listed(b, s0, s0 + HALF)))
             if t == 1:
                 turn_w(0, 0, 2, on_scalar)
                 turn_w(1, 0, 3, on_scalar)
@@ -162,40 +170,30 @@ def tile_attend_gbpr_wx_ts_kernel(tc, xT, wT, wt, ts, xm, offs, out_0, out_1):
         h_r = [mx_operand("h_r%d" % b) for b in range(B)]
         h_i = [mx_operand("h_i0"), None]
 
-        def pack_w(b, j, copy, tag=None):
-            packed = held([P, 2 * N], BF16, "w_packed%d_%d" % (b, j), tag)
-            source = w_planes[b][:].rearrange("p (t h j c i) -> p j h c t i", t=PACK, h=2, j=2, i=4)[:, j]
-            copy(packed[:].rearrange("p (h c i t) -> p h c t i", h=2, i=4, t=PACK), source)
-            return packed
-
-        def quantize_w(b, j, packed):
-            quantize(w_d[b], E4M3, packed[:], 2 * P * j, 2 * P * (j + 1))
+        def pack_w(b, half, packed):
+            weave(on_vector, packed, by_plane(w_planes[b][:])[:, :, HALF * half:HALF * (half + 1)])
 
         def dealt(rows):
             return rows.rearrange("p (m t) -> p t m", t=PACK)
 
-        def scale_items(b, c, score, on_vector_too):
-            out = held([P, R], F32, "scaled%d_%d" % (b, c), "scaled%d" % c)
-            k = 2 * b + c // 2
-            if on_vector_too and c % 2 == 1:
-                nc.vector.tensor_scalar(by_plane(out[:]), dealt(score[:]), signed[c % 2][:, k:k + 1], None, MULT)
-            else:
-                nc.scalar.activation(by_plane(out[:]), dealt(score[:]), COPY, scale=signed[c % 2][:, k:k + 1])
+        def scale_items(b, half, j, score):
+            out = held([P, R], F32, "scaled%d_%d_%d" % (b, half, j), "scaled%d_%d" % (half, j))
+            nc.scalar.activation(by_plane(out[:]), dealt(score[:]), COPY, scale=signed[half][:, 2 * b + j:2 * b + j + 1])
             return out
 
         def scores_of(b, banks, row_runs):
             scores = [bank(banks[c], "score%d_%d" % (b, c)) for c in range(4)]
-            for r0, r1 in row_runs:
-                for c in (0, 2, 1, 3):
+            for c in range(4):
+                for r0, r1 in row_runs:
                     product(scores[c][:, r0:r1], w_d[b], E4M3, c, x_d[b], E4M3, r0, r1)
             return scores
 
-        def sigmoids(b, scores, sum_banks, on_vector_too):
+        def sigmoids(b, scores, sum_banks):
             sig = held([P, PACK * HALF], F32, "sig%d" % b)
             summed = [None, None]
             for half in range(2):
                 for j in range(2):
-                    scaled = scale_items(b, 2 * j + half, scores[2 * j + half], on_vector_too)
+                    scaled = scale_items(b, half, j, scores[2 * half + j])
                     if half == 0:
                         summed[j] = bank(sum_banks[j], "summed%d_%d" % (b, j))
                     for t in range(PACK):
@@ -206,7 +204,6 @@ def tile_attend_gbpr_wx_ts_kernel(tc, xT, wT, wt, ts, xm, offs, out_0, out_1):
             return [sig[:, HALF * t:HALF * (t + 1)] for t in range(PACK)]
 
         h_planes = [held([P, PACK * N], BF16, "h_planes%d" % b) for b in range(B)]
-        h_packed = [held([P, PACK * N], BF16, "h_packed0")]
 
         def form_h(b, half, sig):
             s0 = HALF * half
@@ -249,8 +246,7 @@ def tile_attend_gbpr_wx_ts_kernel(tc, xT, wT, wt, ts, xm, offs, out_0, out_1):
 
         def turn_h(b, banks, copy, turned):
             for g in range(2):
-                turn = turn_words(h_planes[b], g, banks[g], "h_turn%d_%d" % (b, g))
-                copy(turned.bitcast(F32).rearrange("q (p g c) -> q g p c", g=2, c=4)[:, g], turn[:].rearrange("q (c p) -> q p c", c=4))
+                copy(as_words(turned[:, 2 * R * g:2 * R * (g + 1)]), turn_words(h_planes[b], g, banks[g], "h_turn%d_%d" % (b, g)))
 
         def row_gradient(b, banks, copy, tag, stores):
             staged = held([P, PACK * D], F32, "gx_staged%d" % b, tag)
@@ -266,10 +262,10 @@ def tile_attend_gbpr_wx_ts_kernel(tc, xT, wT, wt, ts, xm, offs, out_0, out_1):
         def row_tile(b, t, k, copy, staged):
             gx = bank(k, "gx%d_%d" % (b, t))
             product(gx[:], h_i[b], E5M2, t, w_i[b], E4M3)
-            copy(staged[:, D * t:D * (t + 1)], gx[:])
+            copy(staged[:, D * t:D * (t + 1)].rearrange("r (p u) -> r p u", u=PACK), gx[:].rearrange("r (u p) -> r p u", u=PACK))
 
         def store_rows(b, t0, t1, queue, staged):
-            queue.dma_start(out=out_1[b].rearrange("(j p) d -> p j d", p=P)[:, t0:t1, :], in_=by_plane(staged[:])[:, t0:t1, :])
+            queue.dma_start(out=out_1[b].rearrange("(p t) d -> p (t d)", t=PACK)[:, D * t0:D * t1], in_=staged[:, D * t0:D * t1])
 
         def pack_rows(name, raw, tag=None):
             packed = held([P, PACK * K], BF16, name, tag)
@@ -277,25 +273,29 @@ def tile_attend_gbpr_wx_ts_kernel(tc, xT, wT, wt, ts, xm, offs, out_0, out_1):
                 weave(on_vector, packed[:, 2 * K * h:2 * K * (h + 1)], raw[:, :, HALF * h:HALF * (h + 1)])
             return packed
 
-        x0_packed = [held([P, 2 * R], BF16, "x0_packed%d" % h) for h in range(2)]
-        for h in range(2):
-            for k in range(2):
-                weave(on_scalar, x0_packed[h][:, N * k:N * (k + 1)], x0_half[h][:, :, P * k:P * (k + 1)])
-        packed = [pack_w(0, j, on_vector) for j in range(2)]
-        for j in range(2):
-            quantize_w(0, j, packed[j])
-        for h in range(2):
-            quantize(x_d[0], E4M3, x0_packed[h][:], h * R // 2, (h + 1) * R // 2)
+        x0_packed = held([P, PACK * R], BF16, "x0_packed")
+        weave(on_scalar, x0_packed[:, 0:2 * K], x0_raw[:, :, 0:HALF])
+        w0_packed = [held([P, 2 * N], BF16, "w0_packed%d" % half) for half in range(2)]
+        for half in range(2):
+            pack_w(0, half, w0_packed[half][:])
+        weave(on_vector, x0_packed[:, 2 * K:4 * K], x0_raw[:, :, HALF:R])
+        for half in range(2):
+            quantize(w_d[0], E4M3, w0_packed[half][:], HALF * half, HALF * (half + 1))
+        quantize(x_d[0], E4M3, x0_packed[:])
         turn_w(0, 1, 4, on_scalar)
         turn_w(1, 1, 5, on_scalar)
-        scores0 = scores_of(0, (0, 1, 2, 3), ((0, R // 2), (R // 2, R)))
-        sig0 = sigmoids(0, scores0, (0, 2), False)
-        packed = [pack_w(1, 0, on_vector, "x0_packed0"), pack_w(1, 1, on_vector, "x0_packed1")]
-        x1_packed = pack_rows("x1_packed", x1_raw)
-        for j in range(2):
-            quantize_w(1, j, packed[j])
+        scores0 = scores_of(0, (0, 2, 1, 3), ((0, R),))
+        sig0 = sigmoids(0, scores0, (0, 2))
+        w1_packed = held([P, PACK * (N - P)], BF16, "w1_packed", "x0_packed")
+        w1_first = held([P, K], BF16, "w1_first")
+        weave(on_scalar, w1_first[:], by_plane(w_planes[1][:])[:, :, 0:P])
+        weave(on_vector, w1_packed[:], by_plane(w_planes[1][:])[:, :, P:N])
+        x1_packed = held([P, PACK * R], BF16, "x1_packed")
+        weave(on_vector, x1_packed[:], x1_raw[:])
+        quantize(w_d[1], E4M3, w1_first[:], 0, P)
+        quantize(w_d[1], E4M3, w1_packed[:], P, N)
         quantize(x_d[1], E4M3, x1_packed[:])
-        scores1 = scores_of(1, (4, 1, 5, 6), ((0, R),))
+        scores1 = scores_of(1, (4, 5, 1, 6), ((0, R),))
         xm0_packed = held([P, 2 * D], BF16, "xm0_packed")
         weave(on_vector, xm0_packed[:], xm_raw[0][:, :, 0:HALF])
         quantize(xm_r[0], E4M3, xm0_packed[:], 0, HALF)
@@ -303,30 +303,30 @@ def tile_attend_gbpr_wx_ts_kernel(tc, xT, wT, wt, ts, xm, offs, out_0, out_1):
             form_h(0, half, sig0)
             pack_h(0, half)
             quantize_h(0, half)
-            if half == 0:
-                for b in range(B):
-                    quantize(w_i[b], E4M3, w_turned[b][:])
-        sig1 = sigmoids(1, scores1, (3, 0), False)
+        sig1 = sigmoids(1, scores1, (3, 0))
         staged = table_gradient_half(0, 0, (0, 1), 4, "w_plane0")
         for j in range(2):
             place_half(0, j, 0, staged[:, HALF * j:HALF * (j + 1)])
         staged = table_gradient_half(0, 1, (0, 1), 5, "w_plane1")
-        xm0_late = held([P, 2 * D], BF16, "xm0_late")
-        weave(on_vector, xm0_late[:], xm_raw[0][:, :, HALF:D])
-        quantize(xm_r[0], E4M3, xm0_late[:], HALF, D)
+        weave(on_vector, xm0_late, xm_raw[0][:, :, HALF:D])
+        quantize(xm_r[0], E4M3, xm0_late, HALF, D)
+        for b in range(B):
+            quantize(w_i[b], E4M3, w_turned[b])
         staged02 = table_gradient(0, 2, 6, on_scalar, None)
         for j in range(2):
             place_half(0, j, 1, staged[:, HALF * j:HALF * (j + 1)])
             place_half(0, 2, j, staged02[:, HALF * j:HALF * (j + 1)])
-        for half in range(2):
-            form_h(1, half, sig1)
-        both = held([P, PACK * (D + R)], BF16, "xm1_packed_h0_turned", "h_packed0")
+        for t in range(PACK):
+            nc.vector.scalar_tensor_tensor(h_planes[1][:, N * t:N * (t + 1)].rearrange("p (h c) -> p h c", h=2),
+                                           sig1[t].rearrange("p (o c) -> p o c", o=1).to_broadcast([P, 2, HALF]),
+                                           row_weight[:, 1, t:t + 1], ts_spread[1][:].rearrange("p (h c) -> p h c", h=2), MULT, MULT)
+        both = held([P, PACK * (D + R)], BF16, "xm1_packed_h0_turned", "woven_early")
         xm1_packed, h0_turned = both[:, 0:PACK * D], both[:, PACK * D:PACK * (D + R)]
         weave_on_gpsimd(xm1_packed, xm_raw[1][:])
         turn_h(0, (0, 1), on_vector, h0_turned)
         quantize(xm_r[1], E4M3, xm1_packed)
         quantize(h_i[0], E5M2, h0_turned)
-        h1_packed = held([P, PACK * N], BF16, "h_packed1", "h_packed0")
+        h1_packed = held([P, PACK * N], BF16, "h_packed1", "woven_early")
         weave_on_gpsimd(h1_packed[:], by_plane(h_planes[1][:]))
         h1_turned = held([P, PACK * R], BF16, "h_turned1")
         turn_h(1, (2, 3), on_vector, h1_turned[:])

@@ -84,7 +84,6 @@ def tile_attend_gbpr_wx_ts_kernel(tc, xT, wT, wt, ts, xm, offs, out_0, out_1):
             return offsets[:, (N * b + s0) // 16:(N * b + s1) // 16]
 
         row_weight = held([P, B, PACK], F32, "row_weight")
-        nc.scalar.dma_start(out=row_weight[:], in_=wt.rearrange("b (p t) o -> p b (t o)", t=PACK))
         ts_row = held([P, T], F32, "ts_row")
         nc.sync.dma_start(out=ts_row[P - 1:P, :], in_=ts[0:1, :])
         nc.gpsimd.memset(ts_row[0:P - 1, :], 0.0)
@@ -98,11 +97,12 @@ def tile_attend_gbpr_wx_ts_kernel(tc, xT, wT, wt, ts, xm, offs, out_0, out_1):
         x1_raw = held([P, PACK, R], F32, "x1_raw")
         xm_raw = [held([P, PACK, D], F32, "xm_raw%d" % b) for b in range(B)]
         nc.sync.dma_start(out=x1_raw[:], in_=xT[1].rearrange("(p j) r -> p j r", j=PACK))
+        nc.sync.dma_start(out=row_weight[:], in_=wt.rearrange("b (p t) o -> p b (t o)", t=PACK))
         for b in range(B):
             nc.sync.dma_start(out=xm_raw[b][:], in_=xm[b].rearrange("(p t) d -> p t d", t=PACK))
 
-        window = [held([P, T], F32, "window%d" % j) for j in range(PACK)]
-        for j in range(PACK):
+        window = [held([P, T], F32, "window%d" % j) for j in range(PACK - 1)]
+        for j in range(PACK - 1):
             nc.gpsimd.memset(window[j][:], 0.0)
 
         ts_listed = held([P, B * N], F32, "ts_listed")
@@ -328,8 +328,6 @@ def tile_attend_gbpr_wx_ts_kernel(tc, xT, wT, wt, ts, xm, offs, out_0, out_1):
         quantize(h_i[0], E5M2, h0_turned)
         h1_packed = held([P, PACK * N], BF16, "h_packed1", "woven_early")
         weave_on_gpsimd(h1_packed[:], by_plane(h_planes[1][:]))
-        h1_turned = held([P, PACK * R], BF16, "h_turned1")
-        turn_h(1, (2, 3), on_vector, h1_turned[:])
         last = held([P, B * N], F32, "dw_staged_last")
 
         def stage_last(b, k):
@@ -338,29 +336,33 @@ def tile_attend_gbpr_wx_ts_kernel(tc, xT, wT, wt, ts, xm, offs, out_0, out_1):
             on_vector(last[:, N * b:N * (b + 1)], dw[:])
 
         gx0 = held([P, PACK * D], F32, "gx_staged0", "w_plane3")
-        stage_last(0, 7)
-        for t, k in enumerate((4, 0, 1)):
+        stage_last(0, 4)
+        h1_turned = held([P, PACK * R], BF16, "h_turned1")
+        turn_h(1, (2, 3), on_vector, h1_turned[:])
+        for t, k in enumerate((7, 0, 1)):
             row_tile(0, t, k, on_vector, gx0)
         store_rows(0, 0, 3, nc.sync, gx0)
         quantize(h_r[1], E5M2, h1_packed[:])
         h_i[1] = mx_operand("h_i1", "h_planes1")
         quantize(h_i[1], E5M2, h1_turned[:])
+        window.append(held([P, T], F32, "window3", "h_turned1"))
+        nc.gpsimd.memset(window[3][:], 0.0)
         staged = table_gradient(1, 0, 2, on_vector, "w_plane2")
-        row_tile(0, 3, 7, on_vector, gx0)
+        row_tile(0, 3, 4, on_vector, gx0)
         store_rows(0, 3, 4, nc.sync, gx0)
         on_vector(window[0][:].indirect(listed(1)), staged[:])
         store_window(0, nc.sync)
         staged = [table_gradient(1, 1, 5, on_scalar, None), table_gradient(1, 2, 6, on_scalar, None)]
         gx1 = held([P, PACK * D], F32, "gx_staged1", "x1_raw")
         row_tile(1, 2, 3, on_scalar, gx1)
-        row_tile(1, 3, 4, on_scalar, gx1)
+        row_tile(1, 3, 7, on_scalar, gx1)
         store_rows(1, 2, 4, nc.sync, gx1)
         for half in range(2):
             for j in (1, 2):
                 place_half(1, j, half, staged[j - 1][:, HALF * half:HALF * (half + 1)])
         store_window(1, nc.sync)
         store_window(2, nc.scalar)
-        stage_last(1, 7)
+        stage_last(1, 4)
         row_tile(1, 0, 0, on_vector, gx1)
         row_tile(1, 1, 2, on_vector, gx1)
         store_rows(1, 0, 2, nc.scalar, gx1)

@@ -312,10 +312,20 @@ def tile_attend_gbpr_wx_ts_kernel(tc, xT, wT, wt, ts, xm, offs, out_0, out_1):
         quantize(xm_r[0], E4M3, xm0_late, HALF, D)
         for b in range(B):
             quantize(w_i[b], E4M3, w_turned[b])
-        staged02 = table_gradient(0, 2, 6, on_scalar, None)
-        for j in range(2):
-            place_half(0, j, 1, staged[:, HALF * j:HALF * (j + 1)])
-            place_half(0, 2, j, staged02[:, HALF * j:HALF * (j + 1)])
+        staged2 = held([P, B * N], F32, "dw_staged2")
+
+        def stage_both(b, j, k, copy, staged):
+            dw = bank(k, "dw%d_%d" % (b, j))
+            product(dw[:], xm_r[b], E4M3, j, h_r[b], E5M2)
+            copy(staged[:, N * b:N * (b + 1)], dw[:])
+
+        def place_piece(s0, s1):
+            indirect_on_scalar(window[2][:].indirect(offsets[:, s0 // 16:s1 // 16]), staged2[:, s0:s1])
+
+        stage_both(0, 2, 6, on_scalar, staged2)
+        place_half(0, 0, 1, staged[:, 0:HALF])
+        place_piece(0, 3 * P)
+        place_half(0, 1, 1, staged[:, HALF:N])
         for t in range(PACK):
             nc.vector.scalar_tensor_tensor(h_planes[1][:, N * t:N * (t + 1)].rearrange("p (h c) -> p h c", h=2),
                                            sig1[t].rearrange("p (o c) -> p o c", o=1).to_broadcast([P, 2, HALF]),
@@ -335,6 +345,11 @@ def tile_attend_gbpr_wx_ts_kernel(tc, xT, wT, wt, ts, xm, offs, out_0, out_1):
             product(dw[:], xm_r[b], E4M3, 3, h_r[b], E5M2)
             on_vector(last[:, N * b:N * (b + 1)], dw[:])
 
+        def stage_last_half(half, k, copy):
+            dw = bank(k, "dw1_3_%d" % half)
+            product(dw[:, 0:HALF], xm_r[1], E4M3, 3, h_r[1], E5M2, HALF * half, HALF * (half + 1))
+            copy(last[:, N + HALF * half:N + HALF * (half + 1)], dw[:, 0:HALF])
+
         gx0 = held([P, PACK * D], F32, "gx_staged0", "w_plane3")
         stage_last(0, 4)
         h1_turned = held([P, PACK * R], BF16, "h_turned1")
@@ -350,21 +365,25 @@ def tile_attend_gbpr_wx_ts_kernel(tc, xT, wT, wt, ts, xm, offs, out_0, out_1):
         staged = table_gradient(1, 0, 2, on_vector, "w_plane2")
         row_tile(0, 3, 4, on_vector, gx0)
         store_rows(0, 3, 4, nc.sync, gx0)
-        on_vector(window[0][:].indirect(listed(1)), staged[:])
-        store_window(0, nc.sync)
-        staged = [table_gradient(1, 1, 5, on_scalar, None), table_gradient(1, 2, 6, on_scalar, None)]
         gx1 = held([P, PACK * D], F32, "gx_staged1", "x1_raw")
         row_tile(1, 2, 3, on_scalar, gx1)
         row_tile(1, 3, 7, on_scalar, gx1)
-        store_rows(1, 2, 4, nc.sync, gx1)
-        for half in range(2):
-            for j in (1, 2):
-                place_half(1, j, half, staged[j - 1][:, HALF * half:HALF * (half + 1)])
+        store_rows(1, 2, 4, nc.scalar, gx1)
+        row_tile(1, 0, 0, on_vector, gx1)
+        store_rows(1, 0, 1, nc.sync, gx1)
+        on_vector(window[0][:].indirect(listed(1)), staged[:])
+        store_window(0, nc.sync)
+        staged = table_gradient(1, 1, 5, on_scalar, None)
+        stage_both(1, 2, 6, on_scalar, staged2)
+        stage_last_half(0, 1, on_vector)
+        place_half(1, 1, 0, staged[:, 0:HALF])
+        place_piece(3 * P, 5 * P)
+        place_half(1, 1, 1, staged[:, HALF:N])
+        place_piece(5 * P, 8 * P)
         store_window(1, nc.sync)
         store_window(2, nc.scalar)
-        stage_last(1, 4)
-        row_tile(1, 0, 0, on_vector, gx1)
+        stage_last_half(1, 4, on_vector)
         row_tile(1, 1, 2, on_vector, gx1)
-        store_rows(1, 0, 2, nc.scalar, gx1)
+        store_rows(1, 1, 2, nc.scalar, gx1)
         on_vector(window[3][:].indirect(offsets[:]), last[:])
         store_window(3, nc.sync)

@@ -205,15 +205,13 @@ def tile_attend_gbpr_wx_ts_kernel(tc, xT, wT, wt, ts, xm, offs, out_0, out_1):
 
         h_planes = [held([P, PACK * N], BF16, "h_planes%d" % b) for b in range(B)]
 
-        def form_h(b, half, sig):
-            s0 = HALF * half
+        def form_h(b, s0, s1, sig):
             for t in range(PACK):
-                nc.vector.scalar_tensor_tensor(h_planes[b][:, N * t + s0:N * t + s0 + HALF], sig[t],
-                                               row_weight[:, b, t:t + 1], ts_spread[b][:, s0:s0 + HALF], MULT, MULT)
+                nc.vector.scalar_tensor_tensor(h_planes[b][:, N * t + s0:N * t + s1], sig[t][:, s0 % HALF:s0 % HALF + s1 - s0],
+                                               row_weight[:, b, t:t + 1], ts_spread[b][:, s0:s1], MULT, MULT)
 
-        def pack_h(b, half):
-            s0 = HALF * half
-            weave(on_vector, h_packed[b][:, PACK * s0:PACK * (s0 + HALF)], by_plane(h_planes[b][:])[:, :, s0:s0 + HALF])
+        def pack_h(b, s0, s1):
+            weave(on_vector, h_packed[b][:, PACK * s0:PACK * s1], by_plane(h_planes[b][:])[:, :, s0:s1])
 
         def quantize_h(b, half):
             s0 = HALF * half
@@ -227,11 +225,11 @@ def tile_attend_gbpr_wx_ts_kernel(tc, xT, wT, wt, ts, xm, offs, out_0, out_1):
             return staged
 
         def table_gradient_half(b, half, tiles, k, tag):
-            dw = bank(k, "dw_half%d_%d" % (b, half))
+            dw = bank(k, "dw_half%d_%d_%d" % (b, half, tiles[0]))
             for n, j in enumerate(tiles):
                 product(dw[:, HALF * n:HALF * (n + 1)], xm_r[b], E4M3, j, h_r[b], E5M2, HALF * half, HALF * (half + 1))
-            staged = held([P, N], F32, "dw_half_staged%d_%d" % (b, half), tag)
-            on_scalar(staged[:], dw[:])
+            staged = held([P, HALF * len(tiles)], F32, "dw_half_staged%d_%d_%d" % (b, half, tiles[0]), tag)
+            on_scalar(staged[:], dw[:, 0:HALF * len(tiles)])
             return staged
 
         def place_half(b, j, half, source):
@@ -289,7 +287,8 @@ def tile_attend_gbpr_wx_ts_kernel(tc, xT, wT, wt, ts, xm, offs, out_0, out_1):
         w1_packed = held([P, PACK * (N - P)], BF16, "w1_packed", "x0_packed")
         w1_first = held([P, K], BF16, "w1_first")
         weave(on_scalar, w1_first[:], by_plane(w_planes[1][:])[:, :, 0:P])
-        weave(on_vector, w1_packed[:], by_plane(w_planes[1][:])[:, :, P:N])
+        weave(on_scalar, w1_packed[:, 0:K], by_plane(w_planes[1][:])[:, :, P:HALF])
+        weave(on_vector, w1_packed[:, K:3 * K], by_plane(w_planes[1][:])[:, :, HALF:N])
         x1_packed = held([P, PACK * R], BF16, "x1_packed")
         weave(on_vector, x1_packed[:], x1_raw[:])
         quantize(w_d[1], E4M3, w1_first[:], 0, P)
@@ -299,14 +298,15 @@ def tile_attend_gbpr_wx_ts_kernel(tc, xT, wT, wt, ts, xm, offs, out_0, out_1):
         xm0_packed = held([P, 2 * D], BF16, "xm0_packed")
         weave(on_vector, xm0_packed[:], xm_raw[0][:, :, 0:HALF])
         quantize(xm_r[0], E4M3, xm0_packed[:], 0, HALF)
-        for half in range(2):
-            form_h(0, half, sig0)
-            pack_h(0, half)
-            quantize_h(0, half)
+        for s0, s1 in ((0, P), (P, HALF), (HALF, N)):
+            form_h(0, s0, s1, sig0)
+            pack_h(0, s0, s1)
+            if s1 % HALF == 0:
+                quantize_h(0, s0 // HALF)
         sig1 = sigmoids(1, scores1, (3, 0))
-        staged = table_gradient_half(0, 0, (0, 1), 4, "w_plane0")
+        first = [table_gradient_half(0, 0, (j,), (4, 1)[j], None) for j in range(2)]
         for j in range(2):
-            place_half(0, j, 0, staged[:, HALF * j:HALF * (j + 1)])
+            place_half(0, j, 0, first[j][:])
         staged = table_gradient_half(0, 1, (0, 1), 5, "w_plane1")
         weave(on_vector, xm0_late, xm_raw[0][:, :, HALF:D])
         quantize(xm_r[0], E4M3, xm0_late, HALF, D)

@@ -386,4 +386,6 @@ def tile_attend_gbpr_wx_ts_kernel(tc, xT, wT, wt, ts, xm, offs, out_0, out_1):
         row_tile(1, 1, 2, on_vector, gx1)
         store_rows(1, 1, 2, nc.scalar, gx1)
         on_vector(window[3][:].indirect(offsets[:]), last[:])
-        store_window(3, nc.sync)
+        for half, queue in enumerate((nc.sync, nc.scalar)):
+            cols = slice(T // 2 * half, T // 2 * (half + 1))
+            queue.dma_start(out=out_0[3 * P:4 * P, cols], in_=window[3][:, cols])

@@ -86,23 +86,22 @@ def tile_attend_gbpr_wx_ts_kernel(tc, xT, wT, wt, ts, xm, offs, out_0, out_1):
         row_weight = held([P, B, PACK], F32, "row_weight")
         ts_row = held([P, T], F32, "ts_row")
         nc.sync.dma_start(out=ts_row[P - 1:P, :], in_=ts[0:1, :])
-        nc.gpsimd.memset(ts_row[0:P - 1, :], 0.0)
+        nc.vector.memset(ts_row[0:P - 1, :], 0.0)
 
         w_rows = wT.rearrange("(p t) c -> t p c", t=PACK)
         w_plane = [held([P, T], F32, "w_plane%d" % t) for t in range(PACK)]
         for t in range(PACK):
             nc.sync.dma_start(out=w_plane[t][:], in_=w_rows[t])
-        x0_raw = held([P, PACK, R], F32, "x0_raw")
-        nc.sync.dma_start(out=x0_raw[:], in_=xT[0].rearrange("(p j) r -> p j r", j=PACK))
-        x1_raw = held([P, PACK, R], F32, "x1_raw")
+        x_raw = [held([P, PACK, R], F32, "x_raw%d" % b) for b in range(B)]
         xm_raw = [held([P, PACK, D], F32, "xm_raw%d" % b) for b in range(B)]
-        nc.sync.dma_start(out=x1_raw[:], in_=xT[1].rearrange("(p j) r -> p j r", j=PACK))
+        for b in range(B):
+            nc.sync.dma_start(out=x_raw[b][:], in_=xT[b].rearrange("(p j) r -> p j r", j=PACK))
         nc.sync.dma_start(out=row_weight[:], in_=wt.rearrange("b (p t) o -> p b (t o)", t=PACK))
         for b in range(B):
             nc.sync.dma_start(out=xm_raw[b][:], in_=xm[b].rearrange("(p t) d -> p t d", t=PACK))
 
-        window = [held([P, T], F32, "window%d" % j) for j in range(PACK - 1)]
-        for j in range(PACK - 1):
+        window = [held([P, T], F32, "window%d" % j) for j in range(PACK)]
+        for j in range(PACK):
             nc.gpsimd.memset(window[j][:], 0.0)
 
         ts_listed = held([P, B * N], F32, "ts_listed")
@@ -118,144 +117,95 @@ def tile_attend_gbpr_wx_ts_kernel(tc, xT, wT, wt, ts, xm, offs, out_0, out_1):
             col = held([P, 2 * B], F32, "signed%d" % half)
             nc.scalar.activation(col[:], turned[:].rearrange("p (k c) -> p k c", c=P)[:, :, P - 1], COPY, scale=sign)
             signed.append(col)
-        ts_spread = []
-        for b in range(B):
-            spread = bank(6 + b, "ts_spread_bank%d" % b)
-            if b == 0:
-                spread0 = spread
-            for half in range(2):
-                for j in range(2):
-                    k = 2 * half + j
-                    nc.tensor.transpose(spread[:, P * k:P * (k + 1)],
-                                        signed[half][:, 2 * b + j:2 * b + j + 1].to_broadcast([P, P]), ident[:])
-            ts_spread.append(spread)
-        ts_spread[0] = held([P, N], F32, "ts_spread0")
-        on_scalar(ts_spread[0][:], spread0[:])
 
         w_planes = [held([P, PACK * N], BF16, "w_planes%d" % b) for b in range(B)]
-        woven_early = held([P, B * PACK * D + PACK * N + 2 * D], BF16, "woven_early")
-        w_turned = [woven_early[:, PACK * D * b:PACK * D * (b + 1)] for b in range(B)]
-        h_packed = [woven_early[:, B * PACK * D:B * PACK * D + PACK * N]]
-        xm0_late = woven_early[:, B * PACK * D + PACK * N:B * PACK * D + PACK * N + 2 * D]
-
-        def turn_words(source, g, k, name):
-            turn = bank(k, name)
-            for c in range(4):
-                t = 2 * g + c // 2
-                nc.tensor.transpose(turn[:, P * c:P * (c + 1)], source[:, N * t:N * (t + 1)].bitcast(F32)[:, c % 2::2], ident[:])
-            return turn[:].rearrange("q (t e p) -> q t p e", t=2, e=2)
-
-        def as_words(turned):
-            return turned.bitcast(F32).rearrange("q (t p e) -> q t p e", t=2, e=2)
+        w_turned = {(b, 0): held([P, 2 * D], BF16, "w_turned%d_0" % b) for b in range(B)}
 
         def turn_w(b, g, k, copy):
-            copy(as_words(w_turned[b][:, 2 * D * g:2 * D * (g + 1)]), turn_words(w_planes[b], g, k, "w_turn%d_%d" % (b, g)))
+            turn = bank(k, "w_turn%d_%d" % (b, g))
+            for c in range(4):
+                t = 2 * g + c // 2
+                nc.tensor.transpose(turn[:, P * c:P * (c + 1)], w_planes[b][:, N * t:N * (t + 1)].bitcast(F32)[:, c % 2::2], ident[:])
+            copy(w_turned[b, g][:].bitcast(F32).rearrange("q (t p e) -> q t p e", t=2, e=2),
+                 turn[:].rearrange("q (t e p) -> q t p e", t=2, e=2))
 
         for t in range(PACK):
             if t < PACK - 1:
                 on_vector(w_planes[0][:, N * t:N * (t + 1)], w_plane[t][:].indirect(listed(0)))
-                (indirect_on_scalar if t >= 1 else on_vector)(w_planes[1][:, N * t:N * (t + 1)], w_plane[t][:].indirect(listed(1)))
+                indirect_on_scalar(w_planes[1][:, N * t:N * (t + 1)], w_plane[t][:].indirect(listed(1)))
             else:
-                for b in range(B):
-                    for s0, gather in ((0, on_vector), (HALF, indirect_on_scalar)):
-                        gather(w_planes[b][:, N * t + s0:N * t + s0 + HALF], w_plane[t][:].indirect(listed(b, s0, s0 + HALF)))
+                on_vector(w_planes[0][:, N * t:N * t + HALF], w_plane[t][:].indirect(listed(0, 0, HALF)))
+                indirect_on_scalar(w_planes[0][:, N * t + HALF:N * (t + 1)], w_plane[t][:].indirect(listed(0, HALF, N)))
+                indirect_on_scalar(w_planes[1][:, N * t:N * (t + 1)], w_plane[t][:].indirect(listed(1)))
             if t == 1:
-                turn_w(0, 0, 2, on_scalar)
+                turn_w(0, 0, 2, on_vector)
                 turn_w(1, 0, 3, on_scalar)
 
-        w_d = [mx_operand("w_d%d" % b) for b in range(B)]
-        x_d = [mx_operand("x_d%d" % b) for b in range(B)]
-        w_i = [mx_operand("w_i%d" % b) for b in range(B)]
-        xm_r = [mx_operand("xm_r%d" % b) for b in range(B)]
-        h_r = [mx_operand("h_r%d" % b) for b in range(B)]
-        h_i = [mx_operand("h_i0"), None]
+        def columns(operand, c0, width=K):
+            return operand[0][:, c0:c0 + width], operand[1][:, c0:c0 + width]
 
-        def pack_w(b, half, packed):
-            weave(on_vector, packed, by_plane(w_planes[b][:])[:, :, HALF * half:HALF * (half + 1)])
-
-        def dealt(rows):
-            return rows.rearrange("p (m t) -> p t m", t=PACK)
-
-        def scale_items(b, half, j, score):
-            out = held([P, R], F32, "scaled%d_%d_%d" % (b, half, j), "scaled%d_%d" % (half, j))
-            nc.scalar.activation(by_plane(out[:]), dealt(score[:]), COPY, scale=signed[half][:, 2 * b + j:2 * b + j + 1])
-            return out
-
-        def scores_of(b, banks, row_runs):
-            scores = [bank(banks[c], "score%d_%d" % (b, c)) for c in range(4)]
-            for c in range(4):
-                for r0, r1 in row_runs:
-                    product(scores[c][:, r0:r1], w_d[b], E4M3, c, x_d[b], E4M3, r0, r1)
+        def scores_of(b, banks):
+            scores = {}
+            for j in range(2):
+                for half in range(2):
+                    scores[half, j] = bank(banks[2 * j + half], "score%d_%d_%d" % (b, half, j))
+                    product(scores[half, j][:], w_d[b], E4M3, 2 * half + j, x_d[b], E4M3)
             return scores
 
-        def sigmoids(b, scores, sum_banks):
-            sig = held([P, PACK * HALF], F32, "sig%d" % b)
-            summed = [None, None]
-            for half in range(2):
-                for j in range(2):
-                    scaled = scale_items(b, half, j, scores[2 * half + j])
-                    if half == 0:
-                        summed[j] = bank(sum_banks[j], "summed%d_%d" % (b, j))
-                    for t in range(PACK):
-                        nc.tensor.matmul(summed[j][:, P * t:P * (t + 1)], scaled[:, P * t:P * (t + 1)], ident[:],
-                                         start=(half == 0 and t == 0), stop=(half == 1 and t == PACK - 1), is_transpose=True)
-            for j in range(2):
-                nc.scalar.activation(by_plane(sig[:])[:, :, P * j:P * (j + 1)], by_plane(summed[j][:]), SIGMOID)
-            return [sig[:, HALF * t:HALF * (t + 1)] for t in range(PACK)]
-
-        h_planes = [held([P, PACK * N], BF16, "h_planes%d" % b) for b in range(B)]
-
-        def form_h(b, s0, s1, sig):
+        def spread_weights(b, k):
+            spread = bank(k, "weights%d" % b)
             for t in range(PACK):
-                nc.vector.scalar_tensor_tensor(h_planes[b][:, N * t + s0:N * t + s1], sig[t][:, s0 % HALF:s0 % HALF + s1 - s0],
-                                               row_weight[:, b, t:t + 1], ts_spread[b][:, s0:s1], MULT, MULT)
+                nc.tensor.transpose(spread[:, t::PACK], row_weight[:, b, t:t + 1].to_broadcast([P, P]), ident[:])
+            return spread[:]
 
-        def pack_h(b, s0, s1):
-            weave(on_vector, h_packed[b][:, PACK * s0:PACK * s1], by_plane(h_planes[b][:])[:, :, s0:s1])
+        def sigmoids(b, scores):
+            scaled = [held([P, R], F32, "scaled%d_%d" % (b, j)) for j in range(2)]
+            summed = [held([P, R], F32, "summed%d_%d" % (b, j)) for j in range(2)]
+            sig = [held([P, R], F32, "sig%d_%d" % (b, j)) for j in range(2)]
+            for j in range(2):
+                nc.scalar.activation(scaled[j][:], scores[0, j][:], COPY, scale=signed[0][:, 2 * b + j:2 * b + j + 1])
+                nc.vector.scalar_tensor_tensor(summed[j][:], scores[1, j][:], signed[1][:, 2 * b + j:2 * b + j + 1], scaled[j][:], MULT, ADD)
+            for j in range(2):
+                nc.scalar.activation(sig[j][:], summed[j][:], SIGMOID)
+            return sig
 
-        def quantize_h(b, half):
-            s0 = HALF * half
-            quantize(h_r[b], E5M2, h_packed[b][:, PACK * s0:PACK * (s0 + HALF)], s0, s0 + HALF)
+        h_cols = {}
+        both_planes = held([P, B * PACK * R], BF16, "h_planes")
+        h_planes = [both_planes[:, PACK * R * b:PACK * R * (b + 1)] for b in range(B)]
 
-        def table_gradient(b, j, k, copy, tag):
-            dw = bank(k, "dw%d_%d" % (b, j))
-            product(dw[:], xm_r[b], E4M3, j, h_r[b], E5M2)
-            staged = held([P, N], F32, "dw_staged%d_%d" % (b, j), tag)
-            copy(staged[:], dw[:])
-            return staged
+        def h_tile(b, c):
+            return h_cols[b, c // 2][:, R * (c % 2):R * (c % 2 + 1)]
 
-        def table_gradient_half(b, half, tiles, k, tag):
-            dw = bank(k, "dw_half%d_%d_%d" % (b, half, tiles[0]))
-            for n, j in enumerate(tiles):
-                product(dw[:, HALF * n:HALF * (n + 1)], xm_r[b], E4M3, j, h_r[b], E5M2, HALF * half, HALF * (half + 1))
-            staged = held([P, HALF * len(tiles)], F32, "dw_half_staged%d_%d_%d" % (b, half, tiles[0]), tag)
-            on_scalar(staged[:], dw[:, 0:HALF * len(tiles)])
-            return staged
+        def form_h(b, half, sig, weights, tag=None):
+            h_cols[b, half] = held([P, 2 * R], BF16, "h_cols%d_%d" % (b, half), tag)
+            for j in range(2):
+                c = 2 * half + j
+                nc.vector.scalar_tensor_tensor(h_tile(b, c), sig[j][:],
+                                               signed[half][:, 2 * b + j:2 * b + j + 1], weights, MULT, MULT)
+                nc.sync.dma_start(out=h_planes[b][P // PACK * c:P // PACK * (c + 1), :].rearrange("a (u r) -> a u r", u=PACK),
+                                  in_=h_tile(b, c))
 
-        def place_half(b, j, half, source):
-            indirect_on_scalar(window[j][:].indirect(listed(b, HALF * half, HALF * (half + 1))), source)
+        def turn_h(b, half, k, copy, packed):
+            turn = bank(k, "h_turn%d_%d" % (b, half))
+            for j in range(2):
+                for e in range(2):
+                    nc.tensor.transpose(turn[:, P * (2 * j + e):P * (2 * j + e + 1)], h_tile(b, 2 * half + j).bitcast(F32)[:, e::2], ident[:])
+            copy(packed.bitcast(F32).rearrange("p (j q e) -> p j q e", j=2, e=2),
+                 turn[:].rearrange("p (j e q) -> p j q e", j=2, e=2))
 
-        def place_halves(b, j, staged):
-            for s0 in (0, HALF):
-                indirect_on_scalar(window[j][:].indirect(listed(b, s0, s0 + HALF)), staged[:, s0:s0 + HALF])
+        def stage(parts, k, copy, staged):
+            dw = bank(k, "dw%d_%d_%d" % parts[0][:3])
+            c0 = 0
+            for b, j, s0, s1 in parts:
+                product(dw[:, c0:c0 + s1 - s0], xm_r[b], E4M3, j, h_r[b], E5M2, s0, s1)
+                c0 = c0 + s1 - s0
+            copy(staged, dw[:, 0:c0])
+
+        def place(scatter, b, j, s0, s1, source):
+            scatter(window[j][:].indirect(listed(b, s0, s1)), source)
 
         def store_window(j, queue):
             queue.dma_start(out=out_0[P * j:P * (j + 1), :], in_=window[j][:])
-
-        def turn_h(b, banks, copy, turned):
-            for g in range(2):
-                copy(as_words(turned[:, 2 * R * g:2 * R * (g + 1)]), turn_words(h_planes[b], g, banks[g], "h_turn%d_%d" % (b, g)))
-
-        def row_gradient(b, banks, copy, tag, stores):
-            staged = held([P, PACK * D], F32, "gx_staged%d" % b, tag)
-            rows = out_1[b].rearrange("(j p) d -> p j d", p=P)
-            for t in range(PACK):
-                gx = bank(banks[t], "gx%d_%d" % (b, t))
-                product(gx[:], h_i[b], E5M2, t, w_i[b], E4M3)
-                copy[t](staged[:, D * t:D * (t + 1)], gx[:])
-                if t + 1 in stores:
-                    t0, queue = stores[t + 1]
-                    queue.dma_start(out=rows[:, t0:t + 1, :], in_=by_plane(staged[:])[:, t0:t + 1, :])
 
         def row_tile(b, t, k, copy, staged):
             gx = bank(k, "gx%d_%d" % (b, t))
@@ -263,129 +213,143 @@ def tile_attend_gbpr_wx_ts_kernel(tc, xT, wT, wt, ts, xm, offs, out_0, out_1):
             copy(staged[:, D * t:D * (t + 1)].rearrange("r (p u) -> r p u", u=PACK), gx[:].rearrange("r (u p) -> r p u", u=PACK))
 
         def store_rows(b, t0, t1, queue, staged):
-            queue.dma_start(out=out_1[b].rearrange("(p t) d -> p (t d)", t=PACK)[:, D * t0:D * t1], in_=staged[:, D * t0:D * t1])
+            queue.dma_start(out=out_1[b].rearrange("(t p) d -> p t d", p=P)[:, t0:t1, :], in_=by_plane(staged[:])[:, t0:t1, :])
 
-        def pack_rows(name, raw, tag=None):
-            packed = held([P, PACK * K], BF16, name, tag)
-            for h in range(2):
-                weave(on_vector, packed[:, 2 * K * h:2 * K * (h + 1)], raw[:, :, HALF * h:HALF * (h + 1)])
-            return packed
-
-        x0_packed = held([P, PACK * R], BF16, "x0_packed")
-        weave(on_scalar, x0_packed[:, 0:2 * K], x0_raw[:, :, 0:HALF])
-        w0_packed = [held([P, 2 * N], BF16, "w0_packed%d" % half) for half in range(2)]
+        along_d = [mx_operand("along_d%d" % b, None, 2 * K) for b in range(B)]
+        w_d = [columns(along_d[b], 0) for b in range(B)]
+        x_d = [columns(along_d[b], K) for b in range(B)]
+        xm_r = [mx_operand("xm_r0"), None]
+        h_r = [mx_operand("h_r0"), None]
+        first = held([P, 2 * PACK * K], BF16, "w0_x0_packed", "first")
+        w0_packed, x0_packed = first[:, 0:PACK * K], first[:, PACK * K:2 * PACK * K]
+        weave(on_scalar, x0_packed[:, 2 * K:4 * K], x_raw[0][:, :, HALF:R])
         for half in range(2):
-            pack_w(0, half, w0_packed[half][:])
-        weave(on_vector, x0_packed[:, 2 * K:4 * K], x0_raw[:, :, HALF:R])
-        for half in range(2):
-            quantize(w_d[0], E4M3, w0_packed[half][:], HALF * half, HALF * (half + 1))
-        quantize(x_d[0], E4M3, x0_packed[:])
+            weave(on_vector, w0_packed[:, 2 * K * half:2 * K * (half + 1)], by_plane(w_planes[0][:])[:, :, HALF * half:HALF * (half + 1)])
+        weave(on_vector, x0_packed[:, 0:2 * K], x_raw[0][:, :, 0:HALF])
+        for c0, c1 in ((0, HALF), (HALF, 3 * HALF), (3 * HALF, 4 * HALF)):
+            quantize(along_d[0], E4M3, first[:, PACK * c0:PACK * c1], c0, c1)
+        scores0 = scores_of(0, (0, 1, 2, 3))
+        second = held([P, 2 * PACK * K], BF16, "w1_x1_packed", "x_raw0")
+        w1_packed, x1_packed = second[:, 0:PACK * K], second[:, PACK * K:2 * PACK * K]
+        weave(on_scalar, w1_packed, by_plane(w_planes[1][:]))
+        weave(on_vector, x1_packed, x_raw[1][:])
+        quantize(x_d[1], E4M3, x1_packed)
+        quantize(w_d[1], E4M3, w1_packed)
+        xm0_packed = held([P, PACK * D], BF16, "xm0_packed", "x_raw0")
+        weave_on_gpsimd(xm0_packed[:], xm_raw[0][:])
+        weights0 = spread_weights(0, 6)
+        sig0 = sigmoids(0, scores0)
+        turned_and_h0 = held([P, 4 * K], BF16, "w_turned0_1_h0_packed", "first")
+        w_turned[0, 1], h0_packed = turned_and_h0[:, 0:2 * K], turned_and_h0[:, 2 * K:4 * K]
         turn_w(0, 1, 4, on_scalar)
-        turn_w(1, 1, 5, on_scalar)
-        scores0 = scores_of(0, (0, 2, 1, 3), ((0, R),))
-        sig0 = sigmoids(0, scores0, (0, 2))
-        w1_packed = held([P, PACK * (N - P)], BF16, "w1_packed", "x0_packed")
-        w1_first = held([P, K], BF16, "w1_first")
-        weave(on_scalar, w1_first[:], by_plane(w_planes[1][:])[:, :, 0:P])
-        weave(on_scalar, w1_packed[:, 0:K], by_plane(w_planes[1][:])[:, :, P:HALF])
-        weave(on_vector, w1_packed[:, K:3 * K], by_plane(w_planes[1][:])[:, :, HALF:N])
-        x1_packed = held([P, PACK * R], BF16, "x1_packed")
-        weave(on_vector, x1_packed[:], x1_raw[:])
-        quantize(w_d[1], E4M3, w1_first[:], 0, P)
-        quantize(w_d[1], E4M3, w1_packed[:], P, N)
-        quantize(x_d[1], E4M3, x1_packed[:])
-        scores1 = scores_of(1, (4, 5, 1, 6), ((0, R),))
-        xm0_packed = held([P, 2 * D], BF16, "xm0_packed")
-        weave(on_vector, xm0_packed[:], xm_raw[0][:, :, 0:HALF])
-        quantize(xm_r[0], E4M3, xm0_packed[:], 0, HALF)
-        for s0, s1 in ((0, P), (P, HALF), (HALF, N)):
-            form_h(0, s0, s1, sig0)
-            pack_h(0, s0, s1)
-            if s1 % HALF == 0:
-                quantize_h(0, s0 // HALF)
-        sig1 = sigmoids(1, scores1, (3, 0))
-        first = [table_gradient_half(0, 0, (j,), (4, 1)[j], None) for j in range(2)]
-        for j in range(2):
-            place_half(0, j, 0, first[j][:])
-        staged = table_gradient_half(0, 1, (0, 1), 5, "w_plane1")
-        weave(on_vector, xm0_late, xm_raw[0][:, :, HALF:D])
-        quantize(xm_r[0], E4M3, xm0_late, HALF, D)
-        for b in range(B):
-            quantize(w_i[b], E4M3, w_turned[b])
-        staged2 = held([P, B * N], F32, "dw_staged2")
+        form_h(0, 0, sig0, weights0)
+        w_turned[1, 1] = held([P, 2 * D], BF16, "w_turned1_1", "scaled0_0")
+        turn_w(1, 1, 5, on_vector)
+        scores1 = scores_of(1, (7, 0, 2, 1))
+        turn_h(0, 0, 3, on_scalar, h0_packed)
+        sig1 = sigmoids(1, scores1)
+        quantize(xm_r[0], E4M3, xm0_packed[:, 0:2 * K], 0, HALF)
+        quantize(h_r[0], E5M2, h0_packed, 0, HALF)
+        quantize(xm_r[0], E4M3, xm0_packed[:, 2 * K:4 * K], HALF, D)
+        w_i = [mx_operand("w_i0", "xm_raw0"), None]
 
-        def stage_both(b, j, k, copy, staged):
-            dw = bank(k, "dw%d_%d" % (b, j))
-            product(dw[:], xm_r[b], E4M3, j, h_r[b], E5M2)
-            copy(staged[:, N * b:N * (b + 1)], dw[:])
+        def quantize_turned(b):
+            for g in range(2):
+                quantize(w_i[b], E4M3, w_turned[b, g][:], HALF * g, HALF * (g + 1))
 
-        def place_piece(s0, s1):
-            indirect_on_scalar(window[2][:].indirect(offsets[:, s0 // 16:s1 // 16]), staged2[:, s0:s1])
+        quantize_turned(0)
+        form_h(0, 1, sig0, weights0, "scaled1_1")
+        weights1 = spread_weights(1, 5)
 
-        stage_both(0, 2, 6, on_scalar, staged2)
-        place_half(0, 0, 1, staged[:, 0:HALF])
-        place_piece(0, 3 * P)
-        place_half(0, 1, 1, staged[:, HALF:N])
-        for t in range(PACK):
-            nc.vector.scalar_tensor_tensor(h_planes[1][:, N * t:N * (t + 1)].rearrange("p (h c) -> p h c", h=2),
-                                           sig1[t].rearrange("p (o c) -> p o c", o=1).to_broadcast([P, 2, HALF]),
-                                           row_weight[:, 1, t:t + 1], ts_spread[1][:].rearrange("p (h c) -> p h c", h=2), MULT, MULT)
-        both = held([P, PACK * (D + R)], BF16, "xm1_packed_h0_turned", "woven_early")
-        xm1_packed, h0_turned = both[:, 0:PACK * D], both[:, PACK * D:PACK * (D + R)]
+        positives = held([P, 3 * HALF], F32, "positives", "summed1_1")
+        for j, k in enumerate((7, 0, 2)):
+            stage([(0, j, 0, HALF)], k, on_scalar, positives[:, HALF * j:HALF * (j + 1)])
+            place(indirect_on_scalar, 0, j, 0, HALF, positives[:, HALF * j:HALF * (j + 1)])
+
+        third = held([P, 8 * K], BF16, "xm1_packed_h_negatives", "first")
+        xm1_packed, h_neg = third[:, 0:4 * K], [third[:, 4 * K:6 * K], third[:, 6 * K:8 * K]]
+        h1_pos = held([P, 2 * K], BF16, "h1_pos")
         weave_on_gpsimd(xm1_packed, xm_raw[1][:])
-        turn_h(0, (0, 1), on_vector, h0_turned)
+        for half in range(2):
+            form_h(1, half, sig1, weights1)
+        late = mx_operand("late", "xm_raw1", 5 * HALF)
+        h0_neg, h_r[1], xm_r[1] = columns(late, 0, HALF), columns(late, HALF), columns(late, 3 * HALF)
+        turn_h(0, 1, 4, on_vector, h_neg[0])
         quantize(xm_r[1], E4M3, xm1_packed)
-        quantize(h_i[0], E5M2, h0_turned)
-        h1_packed = held([P, PACK * N], BF16, "h_packed1", "woven_early")
-        weave_on_gpsimd(h1_packed[:], by_plane(h_planes[1][:]))
-        last = held([P, B * N], F32, "dw_staged_last")
+        turn_h(1, 0, 1, on_vector, h1_pos[:])
+        quantize(h0_neg, E5M2, h_neg[0], 0, HALF)
+        turn_h(1, 1, 6, on_vector, h_neg[1])
+        quantize(h_r[1], E5M2, h1_pos[:], 0, HALF)
+        quantize(h_r[1], E5M2, h_neg[1], HALF, N)
 
-        def stage_last(b, k):
-            dw = bank(k, "dw%d_3" % b)
-            product(dw[:], xm_r[b], E4M3, 3, h_r[b], E5M2)
-            on_vector(last[:, N * b:N * (b + 1)], dw[:])
+        def part(out, b, j, s0, s1):
+            if b == 0 and s0 == HALF:
+                product(out, xm_r[0], E4M3, j, h0_neg, E5M2, 0, HALF)
+            else:
+                product(out, xm_r[b], E4M3, j, h_r[b], E5M2, s0, s1)
 
-        def stage_last_half(half, k, copy):
-            dw = bank(k, "dw1_3_%d" % half)
-            product(dw[:, 0:HALF], xm_r[1], E4M3, 3, h_r[1], E5M2, HALF * half, HALF * (half + 1))
-            copy(last[:, N + HALF * half:N + HALF * (half + 1)], dw[:, 0:HALF])
+        def place_run(scatter, j, s0, s1, source):
+            scatter(window[j][:].indirect(offsets[:, s0 // 16:s1 // 16]), source)
 
-        gx0 = held([P, PACK * D], F32, "gx_staged0", "w_plane3")
-        stage_last(0, 4)
-        h1_turned = held([P, PACK * R], BF16, "h_turned1")
-        turn_h(1, (2, 3), on_vector, h1_turned[:])
-        for t, k in enumerate((7, 0, 1)):
-            row_tile(0, t, k, on_vector, gx0)
-        store_rows(0, 0, 3, nc.sync, gx0)
-        quantize(h_r[1], E5M2, h1_packed[:])
-        h_i[1] = mx_operand("h_i1", "h_planes1")
-        quantize(h_i[1], E5M2, h1_turned[:])
-        window.append(held([P, T], F32, "window3", "h_turned1"))
-        nc.gpsimd.memset(window[3][:], 0.0)
-        staged = table_gradient(1, 0, 2, on_vector, "w_plane2")
-        row_tile(0, 3, 4, on_vector, gx0)
-        store_rows(0, 3, 4, nc.sync, gx0)
-        gx1 = held([P, PACK * D], F32, "gx_staged1", "x1_raw")
-        row_tile(1, 2, 3, on_scalar, gx1)
-        row_tile(1, 3, 7, on_scalar, gx1)
-        store_rows(1, 2, 4, nc.scalar, gx1)
-        row_tile(1, 0, 0, on_vector, gx1)
-        store_rows(1, 0, 1, nc.sync, gx1)
-        on_vector(window[0][:].indirect(listed(1)), staged[:])
+        def stage_pair(k, name, tags, copies, parts):
+            dw = bank(k, "dw_" + name)
+            tiles = []
+            for n, (b, j, s0) in enumerate(parts):
+                part(dw[:, HALF * n:HALF * (n + 1)], b, j, s0, s0 + HALF)
+            for n in range(2):
+                tiles.append(held([P, HALF], F32, "staged_%s%d" % (name, n), tags[n]))
+                copies[n](tiles[n][:], dw[:, HALF * n:HALF * (n + 1)])
+            return tiles
+
+        tiles = stage_pair(7, "neg", ("sig0_0", "sig0_1"), (on_scalar, on_scalar), ((0, 0, HALF), (0, 1, HALF)))
+        for j in range(2):
+            place(indirect_on_scalar, 0, j, HALF, N, tiles[j][:])
+
+        h_turned = held([P, B * PACK * R], BF16, "h_turned", "first")
+        staged0_3 = held([P, HALF], F32, "staged0_3", "h1_pos")[:]
+        for b in range(B):
+            weave_on_gpsimd(h_turned[:, PACK * R * b:PACK * R * (b + 1)], by_plane(h_planes[b]))
+        staged = held([P, N], F32, "staged1_0", "w_plane0")
+        dw = bank(3, "dw1_0")
+        for s0 in (0, HALF):
+            part(dw[:, s0:s0 + HALF], 1, 0, s0, s0 + HALF)
+        on_vector(staged[:], dw[:])
+        stage([(0, 3, 0, HALF)], 0, on_vector, staged0_3)
+        place(on_vector, 0, 3, 0, HALF, staged0_3)
+        place(on_vector, 1, 0, 0, N, staged[:])
         store_window(0, nc.sync)
-        staged = table_gradient(1, 1, 5, on_scalar, None)
-        stage_both(1, 2, 6, on_scalar, staged2)
-        stage_last_half(0, 1, on_vector)
-        place_half(1, 1, 0, staged[:, 0:HALF])
-        place_piece(3 * P, 5 * P)
-        place_half(1, 1, 1, staged[:, HALF:N])
-        place_piece(5 * P, 8 * P)
+
+        tiles = stage_pair(7, "w1", ("scaled1_0", "w_plane1"), (on_scalar, on_scalar), ((1, 1, 0), (1, 1, HALF)))
+        place(indirect_on_scalar, 1, 1, 0, HALF, tiles[0][:])
+        held_back = held([P, 4 * HALF], F32, "staged0_3_neg_staged2", "scaled1_0")
+        staged2 = held_back[:, HALF:4 * HALF]
+        stage([(1, 2, 0, N)], 5, on_vector, staged2[:, HALF:3 * HALF])
+        dw = bank(2, "dw0_neg_3_2")
+        for n, j in enumerate((3, 2)):
+            part(dw[:, HALF * n:HALF * (n + 1)], 0, j, HALF, N)
+        on_scalar(held_back[:, 0:N], dw[:])
+        place(indirect_on_scalar, 1, 1, HALF, N, tiles[1][:])
         store_window(1, nc.sync)
+        place_run(indirect_on_scalar, 2, HALF, 5 * P, staged2[:, 0:3 * P])
+        place(indirect_on_scalar, 0, 3, HALF, N, held_back[:, 0:HALF])
+        place_run(indirect_on_scalar, 2, 5 * P, 8 * P, staged2[:, 3 * P:6 * P])
         store_window(2, nc.scalar)
-        stage_last_half(1, 4, on_vector)
-        row_tile(1, 1, 2, on_vector, gx1)
-        store_rows(1, 1, 2, nc.scalar, gx1)
-        on_vector(window[3][:].indirect(offsets[:]), last[:])
+
+        along_slots = mx_operand("along_slots", "h_planes", 3 * K)
+        h_i = [columns(along_slots, K * b) for b in range(B)]
+        w_i[1] = columns(along_slots, 2 * K)
+        quantize(h_i[0], E5M2, h_turned[:, 0:PACK * R])
+        quantize_turned(1)
+        quantize(h_i[1], E5M2, h_turned[:, PACK * R:B * PACK * R])
+        last = held([P, N], F32, "staged1_3", "first")
+        stage([(1, 3, 0, N)], 4, on_vector, last[:])
+        for b, tag in enumerate(("w_plane3", "x_raw1")):
+            gx = held([P, PACK * D], F32, "gx_staged%d" % b, tag)
+            for t, k in enumerate(((1, 6, 0, 3), (4, 1, 6, 0))[b]):
+                row_tile(b, t, k, on_vector, gx)
+                if t % 2 == 1:
+                    store_rows(b, t - 1, t + 1, nc.sync, gx)
+        place(on_vector, 1, 3, 0, N, last[:])
         for half, queue in enumerate((nc.sync, nc.scalar)):
             cols = slice(T // 2 * half, T // 2 * (half + 1))
             queue.dma_start(out=out_0[3 * P:4 * P, cols], in_=window[3][:, cols])

@@ -67,6 +67,10 @@ def tile_attend_gbpr_wx_ts_kernel(tc, xT, wT, wt, ts, xm, offs, out_0, out_1):
         def weave(copy, packed, source):
             copy(woven(packed), planes(source))
 
+        def weave_rows(copy, packed, raw, e):
+            copy(packed[:, 2 * K * e:2 * K * (e + 1)].rearrange("p (n s t) -> p n t s", s=2, t=PACK),
+                 raw.rearrange("p t (n e s) -> p e n t s", e=2, s=2)[:, e])
+
         def weave_on_gpsimd(packed, source):
             nc.gpsimd.tensor_scalar(packed.rearrange("p (c t) -> p c t", t=PACK), source.rearrange("p t c -> p c t"), 1.0, 0.0, MULT, ADD)
 
@@ -76,6 +80,8 @@ def tile_attend_gbpr_wx_ts_kernel(tc, xT, wT, wt, ts, xm, offs, out_0, out_1):
 
         ident = held([P, P], F32, "ident")
         make_identity(nc, ident[:])
+        ident_h = held([P, P], F32, "ident_h")
+        make_identity(nc, ident_h[:])
 
         offsets = lists.tile([P, B * N // 16], U16, name="offsets")
         nc.sync.dma_start(offsets[:], offs)
@@ -86,7 +92,7 @@ def tile_attend_gbpr_wx_ts_kernel(tc, xT, wT, wt, ts, xm, offs, out_0, out_1):
         row_weight = held([P, B, PACK], F32, "row_weight")
         ts_row = held([P, T], F32, "ts_row")
         nc.sync.dma_start(out=ts_row[P - 1:P, :], in_=ts[0:1, :])
-        nc.vector.memset(ts_row[0:P - 1, :], 0.0)
+        nc.vector.memset(ts_row[0:P - 1, :].bitcast(U32), 0)
 
         w_rows = wT.rearrange("(p t) c -> t p c", t=PACK)
         w_plane = [held([P, T], F32, "w_plane%d" % t) for t in range(PACK)]
@@ -155,19 +161,17 @@ def tile_attend_gbpr_wx_ts_kernel(tc, xT, wT, wt, ts, xm, offs, out_0, out_1):
         def spread_weights(b, k):
             spread = bank(k, "weights%d" % b)
             for t in range(PACK):
-                nc.tensor.transpose(spread[:, t::PACK], row_weight[:, b, t:t + 1].to_broadcast([P, P]), ident[:])
+                nc.tensor.transpose(spread[:, HALF * (t // 2) + t % 2:HALF * (t // 2 + 1):2], row_weight[:, b, t:t + 1].to_broadcast([P, P]), ident[:])
             return spread[:]
 
-        def sigmoids(b, scores):
-            scaled = [held([P, R], F32, "scaled%d_%d" % (b, j)) for j in range(2)]
-            summed = [held([P, R], F32, "summed%d_%d" % (b, j)) for j in range(2)]
-            sig = [held([P, R], F32, "sig%d_%d" % (b, j)) for j in range(2)]
+        def sigmoids(b, scores, scaled, summed, runs, tag=None):
+            sig = held([P, 2 * R], F32, "sig%d" % b, tag)
             for j in range(2):
-                nc.scalar.activation(scaled[j][:], scores[0, j][:], COPY, scale=signed[0][:, 2 * b + j:2 * b + j + 1])
-                nc.vector.scalar_tensor_tensor(summed[j][:], scores[1, j][:], signed[1][:, 2 * b + j:2 * b + j + 1], scaled[j][:], MULT, ADD)
-            for j in range(2):
-                nc.scalar.activation(sig[j][:], summed[j][:], SIGMOID)
-            return sig
+                nc.scalar.activation(scaled[j], scores[0, j][:], COPY, scale=signed[0][:, 2 * b + j:2 * b + j + 1])
+                nc.vector.scalar_tensor_tensor(summed[j], scores[1, j][:], signed[1][:, 2 * b + j:2 * b + j + 1], scaled[j], MULT, ADD)
+            for c0, c1, source in runs:
+                nc.scalar.activation(sig[:, c0:c1], source, SIGMOID)
+            return [sig[:, R * j:R * (j + 1)] for j in range(2)]
 
         h_cols = {}
         both_planes = held([P, B * PACK * R], BF16, "h_planes")
@@ -176,20 +180,21 @@ def tile_attend_gbpr_wx_ts_kernel(tc, xT, wT, wt, ts, xm, offs, out_0, out_1):
         def h_tile(b, c):
             return h_cols[b, c // 2][:, R * (c % 2):R * (c % 2 + 1)]
 
-        def form_h(b, half, sig, weights, tag=None):
-            h_cols[b, half] = held([P, 2 * R], BF16, "h_cols%d_%d" % (b, half), tag)
-            for j in range(2):
+        def form_h(b, half, sig, weights, place=None, tiles=(0, 1)):
+            if tiles[0] == 0:
+                h_cols[b, half] = held([P, 2 * R], BF16, "h_cols%d_%d" % (b, half))[:] if place is None else place
+            for j in tiles:
                 c = 2 * half + j
-                nc.vector.scalar_tensor_tensor(h_tile(b, c), sig[j][:],
+                nc.vector.scalar_tensor_tensor(h_tile(b, c), sig[j],
                                                signed[half][:, 2 * b + j:2 * b + j + 1], weights, MULT, MULT)
                 nc.sync.dma_start(out=h_planes[b][P // PACK * c:P // PACK * (c + 1), :].rearrange("a (u r) -> a u r", u=PACK),
                                   in_=h_tile(b, c))
 
-        def turn_h(b, half, k, copy, packed):
+        def turn_h(b, half, k, copy, packed, unit=ident):
             turn = bank(k, "h_turn%d_%d" % (b, half))
             for j in range(2):
                 for e in range(2):
-                    nc.tensor.transpose(turn[:, P * (2 * j + e):P * (2 * j + e + 1)], h_tile(b, 2 * half + j).bitcast(F32)[:, e::2], ident[:])
+                    nc.tensor.transpose(turn[:, P * (2 * j + e):P * (2 * j + e + 1)], h_tile(b, 2 * half + j).bitcast(F32)[:, P * e:P * (e + 1)], unit[:])
             copy(packed.bitcast(F32).rearrange("p (j q e) -> p j q e", j=2, e=2),
                  turn[:].rearrange("p (j e q) -> p j q e", j=2, e=2))
 
@@ -213,7 +218,7 @@ def tile_attend_gbpr_wx_ts_kernel(tc, xT, wT, wt, ts, xm, offs, out_0, out_1):
             copy(staged[:, D * t:D * (t + 1)].rearrange("r (p u) -> r p u", u=PACK), gx[:].rearrange("r (u p) -> r p u", u=PACK))
 
         def store_rows(b, t0, t1, queue, staged):
-            queue.dma_start(out=out_1[b].rearrange("(t p) d -> p t d", p=P)[:, t0:t1, :], in_=by_plane(staged[:])[:, t0:t1, :])
+            queue.dma_start(out=out_1[b].rearrange("(p t) d -> p (t d)", t=PACK)[:, D * t0:D * t1], in_=staged[:, D * t0:D * t1])
 
         along_d = [mx_operand("along_d%d" % b, None, 2 * K) for b in range(B)]
         w_d = [columns(along_d[b], 0) for b in range(B)]
@@ -222,62 +227,60 @@ def tile_attend_gbpr_wx_ts_kernel(tc, xT, wT, wt, ts, xm, offs, out_0, out_1):
         h_r = [mx_operand("h_r0"), None]
         first = held([P, 2 * PACK * K], BF16, "w0_x0_packed", "first")
         w0_packed, x0_packed = first[:, 0:PACK * K], first[:, PACK * K:2 * PACK * K]
-        weave(on_scalar, x0_packed[:, 2 * K:4 * K], x_raw[0][:, :, HALF:R])
+        weave_rows(on_scalar, x0_packed, x_raw[0][:], 1)
         for half in range(2):
             weave(on_vector, w0_packed[:, 2 * K * half:2 * K * (half + 1)], by_plane(w_planes[0][:])[:, :, HALF * half:HALF * (half + 1)])
-        weave(on_vector, x0_packed[:, 0:2 * K], x_raw[0][:, :, 0:HALF])
+        weave_rows(on_vector, x0_packed, x_raw[0][:], 0)
         for c0, c1 in ((0, HALF), (HALF, 3 * HALF), (3 * HALF, 4 * HALF)):
             quantize(along_d[0], E4M3, first[:, PACK * c0:PACK * c1], c0, c1)
         scores0 = scores_of(0, (0, 1, 2, 3))
         second = held([P, 2 * PACK * K], BF16, "w1_x1_packed", "x_raw0")
         w1_packed, x1_packed = second[:, 0:PACK * K], second[:, PACK * K:2 * PACK * K]
         weave(on_scalar, w1_packed, by_plane(w_planes[1][:]))
-        weave(on_vector, x1_packed, x_raw[1][:])
+        on_vector(x1_packed.rearrange("p (e n s t) -> p n t e s", e=2, s=2, t=PACK), x_raw[1][:].rearrange("p t (n e s) -> p n t e s", e=2, s=2))
         quantize(x_d[1], E4M3, x1_packed)
         quantize(w_d[1], E4M3, w1_packed)
         xm0_packed = held([P, PACK * D], BF16, "xm0_packed", "x_raw0")
         weave_on_gpsimd(xm0_packed[:], xm_raw[0][:])
         weights0 = spread_weights(0, 6)
-        sig0 = sigmoids(0, scores0)
-        turned_and_h0 = held([P, 4 * K], BF16, "w_turned0_1_h0_packed", "first")
-        w_turned[0, 1], h0_packed = turned_and_h0[:, 0:2 * K], turned_and_h0[:, 2 * K:4 * K]
+        scaled = [held([P, R], F32, "scaled0_%d" % j)[:] for j in range(2)]
+        summed = [held([P, R], F32, "summed0_%d" % j)[:] for j in range(2)]
+        sig0 = sigmoids(0, scores0, scaled, summed, ((0, R, summed[0]), (R, 2 * R, summed[1])))
+        w_turned[0, 1] = held([P, 2 * D], BF16, "w_turned0_1", "first")
+        h0_packed = held([P, 2 * K], BF16, "h0_packed", "ts_listed")[:]
         turn_w(0, 1, 4, on_scalar)
         form_h(0, 0, sig0, weights0)
         w_turned[1, 1] = held([P, 2 * D], BF16, "w_turned1_1", "scaled0_0")
         turn_w(1, 1, 5, on_vector)
         scores1 = scores_of(1, (7, 0, 2, 1))
-        turn_h(0, 0, 3, on_scalar, h0_packed)
-        sig1 = sigmoids(1, scores1)
+        turn_h(0, 0, 3, on_scalar, h0_packed, ident_h)
+        scaled = held([P, 2 * R], F32, "scaled1", "summed0_0")
+        summed = held([P, 2 * R], F32, "summed1")
+        sig1 = sigmoids(1, scores1, [scaled[:, 0:R], scaled[:, R:2 * R]], [summed[:, 0:R], summed[:, R:2 * R]], ((0, 2 * R, summed[:]),), "ident_h")
         quantize(xm_r[0], E4M3, xm0_packed[:, 0:2 * K], 0, HALF)
         quantize(h_r[0], E5M2, h0_packed, 0, HALF)
         quantize(xm_r[0], E4M3, xm0_packed[:, 2 * K:4 * K], HALF, D)
-        w_i = [mx_operand("w_i0", "xm_raw0"), None]
-
-        def quantize_turned(b):
-            for g in range(2):
-                quantize(w_i[b], E4M3, w_turned[b, g][:], HALF * g, HALF * (g + 1))
-
-        quantize_turned(0)
-        form_h(0, 1, sig0, weights0, "scaled1_1")
+        third = held([P, 10 * K], BF16, "xm1_packed_h_negatives", "ts_listed")
+        xm1_packed, h_neg = third[:, 0:4 * K], [third[:, 4 * K:6 * K], third[:, 6 * K:8 * K]]
+        form_h(0, 1, sig0, weights0, third[:, 8 * K:10 * K])
         weights1 = spread_weights(1, 5)
 
-        positives = held([P, 3 * HALF], F32, "positives", "summed1_1")
+        positives = held([P, 3 * HALF], F32, "positives", "summed1")
         for j, k in enumerate((7, 0, 2)):
             stage([(0, j, 0, HALF)], k, on_scalar, positives[:, HALF * j:HALF * (j + 1)])
             place(indirect_on_scalar, 0, j, 0, HALF, positives[:, HALF * j:HALF * (j + 1)])
 
-        third = held([P, 8 * K], BF16, "xm1_packed_h_negatives", "first")
-        xm1_packed, h_neg = third[:, 0:4 * K], [third[:, 4 * K:6 * K], third[:, 6 * K:8 * K]]
         h1_pos = held([P, 2 * K], BF16, "h1_pos")
         weave_on_gpsimd(xm1_packed, xm_raw[1][:])
-        for half in range(2):
-            form_h(1, half, sig1, weights1)
+        form_h(1, 0, sig1, weights1)
+        form_h(1, 1, sig1, weights1, None, (0,))
+        turn_h(0, 1, 4, on_vector, h_neg[0])
+        form_h(1, 1, sig1, weights1, None, (1,))
         late = mx_operand("late", "xm_raw1", 5 * HALF)
         h0_neg, h_r[1], xm_r[1] = columns(late, 0, HALF), columns(late, HALF), columns(late, 3 * HALF)
-        turn_h(0, 1, 4, on_vector, h_neg[0])
-        quantize(xm_r[1], E4M3, xm1_packed)
-        turn_h(1, 0, 1, on_vector, h1_pos[:])
         quantize(h0_neg, E5M2, h_neg[0], 0, HALF)
+        turn_h(1, 0, 1, on_vector, h1_pos[:])
+        quantize(xm_r[1], E4M3, xm1_packed)
         turn_h(1, 1, 6, on_vector, h_neg[1])
         quantize(h_r[1], E5M2, h1_pos[:], 0, HALF)
         quantize(h_r[1], E5M2, h_neg[1], HALF, N)
@@ -301,51 +304,63 @@ def tile_attend_gbpr_wx_ts_kernel(tc, xT, wT, wt, ts, xm, offs, out_0, out_1):
                 copies[n](tiles[n][:], dw[:, HALF * n:HALF * (n + 1)])
             return tiles
 
-        tiles = stage_pair(7, "neg", ("sig0_0", "sig0_1"), (on_scalar, on_scalar), ((0, 0, HALF), (0, 1, HALF)))
+        w_both = mx_operand("w_i", "h1_pos", B * K)
+        w_i = [columns(w_both, K * b) for b in range(B)]
+        for b in range(B):
+            for g in range(2):
+                quantize(w_i[b], E4M3, w_turned[b, g][:], HALF * g, HALF * (g + 1))
+        h_turned = held([P, B * PACK * R], BF16, "h_turned", "scaled0_0")
+        for b in range(B):
+            for e in range(2):
+                c0 = PACK * R * b + 2 * K * e
+                nc.gpsimd.tensor_scalar(h_turned[:, c0:c0 + 2 * K].rearrange("q (s n u) -> q s n u", s=2, u=PACK),
+                                        by_plane(h_planes[b])[:, :, HALF * e:HALF * (e + 1)].rearrange("q u (n s) -> q s n u", s=2), 1.0, 0.0, MULT, ADD)
+        tiles = stage_pair(7, "neg", ("sig0", "summed0_1"), (on_scalar, on_scalar), ((0, 0, HALF), (0, 1, HALF)))
         for j in range(2):
             place(indirect_on_scalar, 0, j, HALF, N, tiles[j][:])
-
-        h_turned = held([P, B * PACK * R], BF16, "h_turned", "first")
-        staged0_3 = held([P, HALF], F32, "staged0_3", "h1_pos")[:]
-        for b in range(B):
-            weave_on_gpsimd(h_turned[:, PACK * R * b:PACK * R * (b + 1)], by_plane(h_planes[b]))
         staged = held([P, N], F32, "staged1_0", "w_plane0")
         dw = bank(3, "dw1_0")
         for s0 in (0, HALF):
             part(dw[:, s0:s0 + HALF], 1, 0, s0, s0 + HALF)
         on_vector(staged[:], dw[:])
-        stage([(0, 3, 0, HALF)], 0, on_vector, staged0_3)
-        place(on_vector, 0, 3, 0, HALF, staged0_3)
+        staged0_3 = held([P, HALF], F32, "staged0_3", "w_turned1_0")
+        stage([(0, 3, 0, HALF)], 0, on_vector, staged0_3[:])
+        second_run = held([P, 3 * P], F32, "second_run")
+        dw = bank(2, "dw2_second_run")
+        part(dw[:, 0:P], 1, 2, P, HALF)
+        part(dw[:, P:3 * P], 1, 2, HALF, N)
+        on_vector(second_run[:], dw[:, 0:3 * P])
         place(on_vector, 1, 0, 0, N, staged[:])
         store_window(0, nc.sync)
+        place(on_vector, 0, 3, 0, HALF, staged0_3[:])
 
-        tiles = stage_pair(7, "w1", ("scaled1_0", "w_plane1"), (on_scalar, on_scalar), ((1, 1, 0), (1, 1, HALF)))
+        tiles = stage_pair(3, "w1", ("scaled1_0", "w_plane1"), (on_scalar, on_scalar), ((1, 1, 0), (1, 1, HALF)))
         place(indirect_on_scalar, 1, 1, 0, HALF, tiles[0][:])
-        held_back = held([P, 4 * HALF], F32, "staged0_3_neg_staged2", "scaled1_0")
-        staged2 = held_back[:, HALF:4 * HALF]
-        stage([(1, 2, 0, N)], 5, on_vector, staged2[:, HALF:3 * HALF])
-        dw = bank(2, "dw0_neg_3_2")
-        for n, j in enumerate((3, 2)):
-            part(dw[:, HALF * n:HALF * (n + 1)], 0, j, HALF, N)
-        on_scalar(held_back[:, 0:N], dw[:])
+        held_back = held([P, HALF + 3 * P], F32, "staged0_3_neg_first_run", "scaled1_0")
+        runs = [held_back[:, HALF:HALF + 3 * P], second_run[:]]
+        dw = bank(4, "dw2_first_run")
+        part(dw[:, 0:HALF], 0, 2, HALF, N)
+        part(dw[:, HALF:3 * P], 1, 2, 0, P)
+        on_scalar(runs[0], dw[:, 0:3 * P])
+        dw = bank(6, "dw0_3_neg")
+        part(dw[:, 0:HALF], 0, 3, HALF, N)
+        on_scalar(held_back[:, 0:HALF], dw[:, 0:HALF])
         place(indirect_on_scalar, 1, 1, HALF, N, tiles[1][:])
         store_window(1, nc.sync)
-        place_run(indirect_on_scalar, 2, HALF, 5 * P, staged2[:, 0:3 * P])
+        place_run(indirect_on_scalar, 2, HALF, 5 * P, runs[0])
         place(indirect_on_scalar, 0, 3, HALF, N, held_back[:, 0:HALF])
-        place_run(indirect_on_scalar, 2, 5 * P, 8 * P, staged2[:, 3 * P:6 * P])
+        place_run(indirect_on_scalar, 2, 5 * P, 8 * P, runs[1])
         store_window(2, nc.scalar)
 
-        along_slots = mx_operand("along_slots", "h_planes", 3 * K)
-        h_i = [columns(along_slots, K * b) for b in range(B)]
-        w_i[1] = columns(along_slots, 2 * K)
-        quantize(h_i[0], E5M2, h_turned[:, 0:PACK * R])
-        quantize_turned(1)
-        quantize(h_i[1], E5M2, h_turned[:, PACK * R:B * PACK * R])
-        last = held([P, N], F32, "staged1_3", "first")
-        stage([(1, 3, 0, N)], 4, on_vector, last[:])
+        h_both = mx_operand("h_i", "h_planes", B * K)
+        h_i = [columns(h_both, K * b) for b in range(B)]
+        for b in range(B):
+            quantize(h_i[b], E5M2, h_turned[:, PACK * R * b:PACK * R * (b + 1)])
+        last = held([P, N], F32, "staged1_3", "scaled0_0")
+        stage([(1, 3, 0, N)], 0, on_vector, last[:])
         for b, tag in enumerate(("w_plane3", "x_raw1")):
             gx = held([P, PACK * D], F32, "gx_staged%d" % b, tag)
-            for t, k in enumerate(((1, 6, 0, 3), (4, 1, 6, 0))[b]):
+            for t, k in enumerate(((1, 5, 7, 3), (0, 1, 5, 7))[b]):
                 row_tile(b, t, k, on_vector, gx)
                 if t % 2 == 1:
                     store_rows(b, t - 1, t + 1, nc.sync, gx)

@@ -68,7 +68,7 @@ def tile_attend_gbpr_wx_ts_kernel(tc, xT, wT, wt, ts, xm, offs, out_0, out_1):
             copy(woven(packed), planes(source))
 
         def weave_rows(copy, packed, raw, e):
-            copy(packed[:, 2 * K * e:2 * K * (e + 1)].rearrange("p (n s t) -> p n t s", s=2, t=PACK),
+            copy(packed.rearrange("p (n s t) -> p n t s", s=2, t=PACK),
                  raw.rearrange("p t (n e s) -> p e n t s", e=2, s=2)[:, e])
 
         def weave_on_gpsimd(packed, source):
@@ -125,7 +125,7 @@ def tile_attend_gbpr_wx_ts_kernel(tc, xT, wT, wt, ts, xm, offs, out_0, out_1):
             signed.append(col)
 
         w_planes = [held([P, PACK * N], BF16, "w_planes%d" % b) for b in range(B)]
-        w_turned = {(b, 0): held([P, 2 * D], BF16, "w_turned%d_0" % b) for b in range(B)}
+        w_turned = {(0, 0): held([P, 2 * D], BF16, "w_turned0_0")}
 
         def turn_w(b, g, k, copy):
             turn = bank(k, "w_turn%d_%d" % (b, g))
@@ -134,6 +134,12 @@ def tile_attend_gbpr_wx_ts_kernel(tc, xT, wT, wt, ts, xm, offs, out_0, out_1):
                 nc.tensor.transpose(turn[:, P * c:P * (c + 1)], w_planes[b][:, N * t:N * (t + 1)].bitcast(F32)[:, c % 2::2], ident[:])
             copy(w_turned[b, g][:].bitcast(F32).rearrange("q (t p e) -> q t p e", t=2, e=2),
                  turn[:].rearrange("q (t e p) -> q t p e", t=2, e=2))
+
+        w_packed = [held([P, PACK * K], BF16, "w_packed%d" % b)[:] for b in range(B)]
+
+        def weave_pair(copy, b, g, s0=0, s1=N):
+            copy(woven(w_packed[b][:, PACK * s0:PACK * s1])[:, :, 2 * g:2 * g + 2, :],
+                 planes(by_plane(w_planes[b][:])[:, :, s0:s1])[:, :, 2 * g:2 * g + 2, :])
 
         for t in range(PACK):
             if t < PACK - 1:
@@ -144,16 +150,16 @@ def tile_attend_gbpr_wx_ts_kernel(tc, xT, wT, wt, ts, xm, offs, out_0, out_1):
                 indirect_on_scalar(w_planes[0][:, N * t + HALF:N * (t + 1)], w_plane[t][:].indirect(listed(0, HALF, N)))
                 indirect_on_scalar(w_planes[1][:, N * t:N * (t + 1)], w_plane[t][:].indirect(listed(1)))
             if t == 1:
+                weave_pair(on_scalar, 0, 0)
                 turn_w(0, 0, 2, on_vector)
-                turn_w(1, 0, 3, on_scalar)
 
         def columns(operand, c0, width=K):
             return operand[0][:, c0:c0 + width], operand[1][:, c0:c0 + width]
 
         def scores_of(b, banks):
             scores = {}
-            for j in range(2):
-                for half in range(2):
+            for half in range(2):
+                for j in range(2):
                     scores[half, j] = bank(banks[2 * j + half], "score%d_%d_%d" % (b, half, j))
                     product(scores[half, j][:], w_d[b], E4M3, 2 * half + j, x_d[b], E4M3)
             return scores
@@ -214,49 +220,56 @@ def tile_attend_gbpr_wx_ts_kernel(tc, xT, wT, wt, ts, xm, offs, out_0, out_1):
 
         def row_tile(b, t, k, copy, staged):
             gx = bank(k, "gx%d_%d" % (b, t))
-            product(gx[:], h_i[b], E5M2, t, w_i[b], E4M3)
+            for g in range(2):
+                product(gx[:, HALF * g:HALF * (g + 1)], h_i[b], E5M2, t, w_i[b, g], E4M3, 0, HALF)
             copy(staged[:, D * t:D * (t + 1)].rearrange("r (p u) -> r p u", u=PACK), gx[:].rearrange("r (u p) -> r p u", u=PACK))
 
         def store_rows(b, t0, t1, queue, staged):
             queue.dma_start(out=out_1[b].rearrange("(p t) d -> p (t d)", t=PACK)[:, D * t0:D * t1], in_=staged[:, D * t0:D * t1])
 
-        along_d = [mx_operand("along_d%d" % b, None, 2 * K) for b in range(B)]
-        w_d = [columns(along_d[b], 0) for b in range(B)]
-        x_d = [columns(along_d[b], K) for b in range(B)]
+        w_d = [mx_operand("w_d0"), None]
+        x_d = [mx_operand("x_d%d" % b) for b in range(B)]
         xm_r = [mx_operand("xm_r0"), None]
         h_r = [mx_operand("h_r0"), None]
-        first = held([P, 2 * PACK * K], BF16, "w0_x0_packed", "first")
-        w0_packed, x0_packed = first[:, 0:PACK * K], first[:, PACK * K:2 * PACK * K]
-        weave_rows(on_scalar, x0_packed, x_raw[0][:], 1)
-        for half in range(2):
-            weave(on_vector, w0_packed[:, 2 * K * half:2 * K * (half + 1)], by_plane(w_planes[0][:])[:, :, HALF * half:HALF * (half + 1)])
-        weave_rows(on_vector, x0_packed, x_raw[0][:], 0)
-        for c0, c1 in ((0, HALF), (HALF, 3 * HALF), (3 * HALF, 4 * HALF)):
-            quantize(along_d[0], E4M3, first[:, PACK * c0:PACK * c1], c0, c1)
+        for s0 in (0, HALF):
+            weave_pair(on_vector, 0, 1, s0, s0 + HALF)
+        weave(on_scalar, w_packed[1], by_plane(w_planes[1][:]))
+        quantize(w_d[0], E4M3, w_packed[0])
+        x0_packed = [held([P, 2 * K], BF16, "x0_packed%d" % e) for e in range(2)]
+        for e in range(2):
+            weave_rows(on_vector, x0_packed[e][:], x_raw[0][:], e)
+        for e in range(2):
+            quantize(x_d[0], E4M3, x0_packed[e][:], HALF * e, HALF * (e + 1))
         scores0 = scores_of(0, (0, 1, 2, 3))
-        second = held([P, 2 * PACK * K], BF16, "w1_x1_packed", "x_raw0")
-        w1_packed, x1_packed = second[:, 0:PACK * K], second[:, PACK * K:2 * PACK * K]
-        weave(on_scalar, w1_packed, by_plane(w_planes[1][:]))
-        on_vector(x1_packed.rearrange("p (e n s t) -> p n t e s", e=2, s=2, t=PACK), x_raw[1][:].rearrange("p t (n e s) -> p n t e s", e=2, s=2))
-        quantize(x_d[1], E4M3, x1_packed)
-        quantize(w_d[1], E4M3, w1_packed)
-        xm0_packed = held([P, PACK * D], BF16, "xm0_packed", "x_raw0")
+        w_i = {(0, 0): mx_operand("w_i0_0", "x_raw0", HALF)}
+        quantize(w_i[0, 0], E4M3, w_turned[0, 0][:], 0, HALF)
+        x1_packed = [held([P, 2 * K], BF16, "x1_packed%d" % e, ("x0_packed1", None)[e]) for e in range(2)]
+        weave_rows(on_scalar, x1_packed[1][:], x_raw[1][:], 1)
+        weave_rows(on_vector, x1_packed[0][:], x_raw[1][:], 0)
+        w_d[1] = mx_operand("w_d1", "x0_packed0")
+        quantize(w_d[1], E4M3, w_packed[1])
+        for e in (1, 0):
+            quantize(x_d[1], E4M3, x1_packed[e][:], HALF * e, HALF * (e + 1))
+        xm0_packed = held([P, PACK * D], BF16, "xm0_packed", "x0_packed1")
         weave_on_gpsimd(xm0_packed[:], xm_raw[0][:])
         weights0 = spread_weights(0, 6)
-        scaled = [held([P, R], F32, "scaled0_%d" % j)[:] for j in range(2)]
+        scaled = held([P, 2 * R], F32, "scaled0", "x_raw1")
+        scaled = [scaled[:, 0:R], scaled[:, R:2 * R]]
         summed = [held([P, R], F32, "summed0_%d" % j)[:] for j in range(2)]
         sig0 = sigmoids(0, scores0, scaled, summed, ((0, R, summed[0]), (R, 2 * R, summed[1])))
-        w_turned[0, 1] = held([P, 2 * D], BF16, "w_turned0_1", "first")
+        w_turned[1, 0] = held([P, 2 * D], BF16, "w_turned1_0", "w_packed1")
+        turn_w(1, 0, 7, on_scalar)
         h0_packed = held([P, 2 * K], BF16, "h0_packed", "ts_listed")[:]
-        turn_w(0, 1, 4, on_scalar)
         form_h(0, 0, sig0, weights0)
-        w_turned[1, 1] = held([P, 2 * D], BF16, "w_turned1_1", "scaled0_0")
+        w_turned[1, 1] = held([P, 2 * D], BF16, "w_turned1_1", "x_raw1")
         turn_w(1, 1, 5, on_vector)
-        scores1 = scores_of(1, (7, 0, 2, 1))
-        turn_h(0, 0, 3, on_scalar, h0_packed, ident_h)
+        scores1 = scores_of(1, (0, 1, 2, 3))
+        turn_h(0, 0, 7, on_scalar, h0_packed, ident_h)
         scaled = held([P, 2 * R], F32, "scaled1", "summed0_0")
         summed = held([P, 2 * R], F32, "summed1")
         sig1 = sigmoids(1, scores1, [scaled[:, 0:R], scaled[:, R:2 * R]], [summed[:, 0:R], summed[:, R:2 * R]], ((0, 2 * R, summed[:]),), "ident_h")
+        w_turned[0, 1] = held([P, 2 * D], BF16, "w_turned0_1", "summed0_1")
+        turn_w(0, 1, 4, on_scalar)
         quantize(xm_r[0], E4M3, xm0_packed[:, 0:2 * K], 0, HALF)
         quantize(h_r[0], E5M2, h0_packed, 0, HALF)
         quantize(xm_r[0], E4M3, xm0_packed[:, 2 * K:4 * K], HALF, D)
@@ -266,7 +279,7 @@ def tile_attend_gbpr_wx_ts_kernel(tc, xT, wT, wt, ts, xm, offs, out_0, out_1):
         weights1 = spread_weights(1, 5)
 
         positives = held([P, 3 * HALF], F32, "positives", "summed1")
-        for j, k in enumerate((7, 0, 2)):
+        for j, k in enumerate((1, 0, 2)):
             stage([(0, j, 0, HALF)], k, on_scalar, positives[:, HALF * j:HALF * (j + 1)])
             place(indirect_on_scalar, 0, j, 0, HALF, positives[:, HALF * j:HALF * (j + 1)])
 
@@ -304,18 +317,17 @@ def tile_attend_gbpr_wx_ts_kernel(tc, xT, wT, wt, ts, xm, offs, out_0, out_1):
                 copies[n](tiles[n][:], dw[:, HALF * n:HALF * (n + 1)])
             return tiles
 
-        w_both = mx_operand("w_i", "h1_pos", B * K)
-        w_i = [columns(w_both, K * b) for b in range(B)]
-        for b in range(B):
-            for g in range(2):
-                quantize(w_i[b], E4M3, w_turned[b, g][:], HALF * g, HALF * (g + 1))
-        h_turned = held([P, B * PACK * R], BF16, "h_turned", "scaled0_0")
+        rest = mx_operand("w_i_rest", "h1_pos", 3 * HALF)
+        for n, key in enumerate(((0, 1), (1, 0), (1, 1))):
+            w_i[key] = columns(rest, HALF * n, HALF)
+            quantize(w_i[key], E4M3, w_turned[key][:], 0, HALF)
+        h_turned = held([P, B * PACK * R], BF16, "h_turned", "x_raw1")
         for b in range(B):
             for e in range(2):
                 c0 = PACK * R * b + 2 * K * e
                 nc.gpsimd.tensor_scalar(h_turned[:, c0:c0 + 2 * K].rearrange("q (s n u) -> q s n u", s=2, u=PACK),
                                         by_plane(h_planes[b])[:, :, HALF * e:HALF * (e + 1)].rearrange("q u (n s) -> q s n u", s=2), 1.0, 0.0, MULT, ADD)
-        tiles = stage_pair(7, "neg", ("sig0", "summed0_1"), (on_scalar, on_scalar), ((0, 0, HALF), (0, 1, HALF)))
+        tiles = stage_pair(7, "neg", ("sig0", "w_plane1"), (on_scalar, on_scalar), ((0, 0, HALF), (0, 1, HALF)))
         for j in range(2):
             place(indirect_on_scalar, 0, j, HALF, N, tiles[j][:])
         staged = held([P, N], F32, "staged1_0", "w_plane0")
@@ -323,18 +335,18 @@ def tile_attend_gbpr_wx_ts_kernel(tc, xT, wT, wt, ts, xm, offs, out_0, out_1):
         for s0 in (0, HALF):
             part(dw[:, s0:s0 + HALF], 1, 0, s0, s0 + HALF)
         on_vector(staged[:], dw[:])
-        staged0_3 = held([P, HALF], F32, "staged0_3", "w_turned1_0")
+        staged0_3 = held([P, HALF], F32, "staged0_3", "summed0_1")
         stage([(0, 3, 0, HALF)], 0, on_vector, staged0_3[:])
         second_run = held([P, 3 * P], F32, "second_run")
         dw = bank(2, "dw2_second_run")
         part(dw[:, 0:P], 1, 2, P, HALF)
         part(dw[:, P:3 * P], 1, 2, HALF, N)
         on_vector(second_run[:], dw[:, 0:3 * P])
+        tiles = stage_pair(5, "w1", ("scaled1_0", "scaled1_1"), (on_vector, on_vector), ((1, 1, 0), (1, 1, HALF)))
         place(on_vector, 1, 0, 0, N, staged[:])
         store_window(0, nc.sync)
         place(on_vector, 0, 3, 0, HALF, staged0_3[:])
 
-        tiles = stage_pair(3, "w1", ("scaled1_0", "w_plane1"), (on_scalar, on_scalar), ((1, 1, 0), (1, 1, HALF)))
         place(indirect_on_scalar, 1, 1, 0, HALF, tiles[0][:])
         held_back = held([P, HALF + 3 * P], F32, "staged0_3_neg_first_run", "scaled1_0")
         runs = [held_back[:, HALF:HALF + 3 * P], second_run[:]]
@@ -356,9 +368,9 @@ def tile_attend_gbpr_wx_ts_kernel(tc, xT, wT, wt, ts, xm, offs, out_0, out_1):
         h_i = [columns(h_both, K * b) for b in range(B)]
         for b in range(B):
             quantize(h_i[b], E5M2, h_turned[:, PACK * R * b:PACK * R * (b + 1)])
-        last = held([P, N], F32, "staged1_3", "scaled0_0")
+        last = held([P, N], F32, "staged1_3", "x_raw1")
         stage([(1, 3, 0, N)], 0, on_vector, last[:])
-        for b, tag in enumerate(("w_plane3", "x_raw1")):
+        for b, tag in enumerate(("w_plane3", "xm_raw0")):
             gx = held([P, PACK * D], F32, "gx_staged%d" % b, tag)
             for t, k in enumerate(((1, 5, 7, 3), (0, 1, 5, 7))[b]):
                 row_tile(b, t, k, on_vector, gx)

@@ -148,7 +148,8 @@ def tile_attend_gbpr_wx_ts_kernel(tc, xT, wT, wt, ts, xm, offs, out_0, out_1):
             else:
                 on_vector(w_planes[0][:, N * t:N * t + HALF], w_plane[t][:].indirect(listed(0, 0, HALF)))
                 indirect_on_scalar(w_planes[0][:, N * t + HALF:N * (t + 1)], w_plane[t][:].indirect(listed(0, HALF, N)))
-                indirect_on_scalar(w_planes[1][:, N * t:N * (t + 1)], w_plane[t][:].indirect(listed(1)))
+                for s0 in (0, HALF):
+                    indirect_on_scalar(w_planes[1][:, N * t + s0:N * t + s0 + HALF], w_plane[t][:].indirect(listed(1, s0, s0 + HALF)))
             if t == 1:
                 weave_pair(on_scalar, 0, 0)
                 turn_w(0, 0, 2, on_vector)
@@ -233,8 +234,9 @@ def tile_attend_gbpr_wx_ts_kernel(tc, xT, wT, wt, ts, xm, offs, out_0, out_1):
         h_r = [mx_operand("h_r0"), None]
         for s0 in (0, HALF):
             weave_pair(on_vector, 0, 1, s0, s0 + HALF)
-        weave(on_scalar, w_packed[1], by_plane(w_planes[1][:]))
-        quantize(w_d[0], E4M3, w_packed[0])
+        for s0 in (0, HALF):
+            weave(on_scalar, w_packed[1][:, PACK * s0:PACK * (s0 + HALF)], by_plane(w_planes[1][:])[:, :, s0:s0 + HALF])
+            quantize(w_d[0], E4M3, w_packed[0][:, PACK * s0:PACK * (s0 + HALF)], s0, s0 + HALF)
         x0_packed = [held([P, 2 * K], BF16, "x0_packed%d" % e) for e in range(2)]
         for e in range(2):
             weave_rows(on_vector, x0_packed[e][:], x_raw[0][:], e)
@@ -273,9 +275,9 @@ def tile_attend_gbpr_wx_ts_kernel(tc, xT, wT, wt, ts, xm, offs, out_0, out_1):
         quantize(xm_r[0], E4M3, xm0_packed[:, 0:2 * K], 0, HALF)
         quantize(h_r[0], E5M2, h0_packed, 0, HALF)
         quantize(xm_r[0], E4M3, xm0_packed[:, 2 * K:4 * K], HALF, D)
-        third = held([P, 10 * K], BF16, "xm1_packed_h_negatives", "ts_listed")
+        third = held([P, 8 * K], BF16, "xm1_packed_h_negatives", "ts_listed")
         xm1_packed, h_neg = third[:, 0:4 * K], [third[:, 4 * K:6 * K], third[:, 6 * K:8 * K]]
-        form_h(0, 1, sig0, weights0, third[:, 8 * K:10 * K])
+        form_h(0, 1, sig0, weights0, held([P, 2 * R], BF16, "h_cols0_1", "x0_packed1")[:])
         weights1 = spread_weights(1, 5)
 
         positives = held([P, 3 * HALF], F32, "positives", "summed1")
@@ -307,34 +309,33 @@ def tile_attend_gbpr_wx_ts_kernel(tc, xT, wT, wt, ts, xm, offs, out_0, out_1):
         def place_run(scatter, j, s0, s1, source):
             scatter(window[j][:].indirect(offsets[:, s0 // 16:s1 // 16]), source)
 
-        def stage_pair(k, name, tags, copies, parts):
-            dw = bank(k, "dw_" + name)
-            tiles = []
-            for n, (b, j, s0) in enumerate(parts):
-                part(dw[:, HALF * n:HALF * (n + 1)], b, j, s0, s0 + HALF)
-            for n in range(2):
-                tiles.append(held([P, HALF], F32, "staged_%s%d" % (name, n), tags[n]))
-                copies[n](tiles[n][:], dw[:, HALF * n:HALF * (n + 1)])
-            return tiles
-
         rest = mx_operand("w_i_rest", "h1_pos", 3 * HALF)
         for n, key in enumerate(((0, 1), (1, 0), (1, 1))):
             w_i[key] = columns(rest, HALF * n, HALF)
             quantize(w_i[key], E4M3, w_turned[key][:], 0, HALF)
-        h_turned = held([P, B * PACK * R], BF16, "h_turned", "x_raw1")
+        h_turned = [held([P, PACK * R], BF16, "h_turned%d" % b, ("x_raw1", "w_packed1")[b]) for b in range(B)]
         for b in range(B):
             for e in range(2):
-                c0 = PACK * R * b + 2 * K * e
-                nc.gpsimd.tensor_scalar(h_turned[:, c0:c0 + 2 * K].rearrange("q (s n u) -> q s n u", s=2, u=PACK),
+                nc.gpsimd.tensor_scalar(h_turned[b][:, 2 * K * e:2 * K * (e + 1)].rearrange("q (s n u) -> q s n u", s=2, u=PACK),
                                         by_plane(h_planes[b])[:, :, HALF * e:HALF * (e + 1)].rearrange("q u (n s) -> q s n u", s=2), 1.0, 0.0, MULT, ADD)
-        tiles = stage_pair(7, "neg", ("sig0", "w_plane1"), (on_scalar, on_scalar), ((0, 0, HALF), (0, 1, HALF)))
+        staged = held([P, HALF], F32, "staged0_0_neg", "sig0")
+        w1_runs = [held([P, 3 * P], F32, "window1_run%d" % n, "scaled1_%d" % n) for n in range(2)]
+        dw = bank(7, "dw0_neg")
         for j in range(2):
-            place(indirect_on_scalar, 0, j, HALF, N, tiles[j][:])
+            part(dw[:, HALF * j:HALF * (j + 1)], 0, j, HALF, N)
+        on_scalar(staged[:], dw[:, 0:HALF])
+        on_scalar(w1_runs[0][:, 0:HALF], dw[:, HALF:N])
+        place(indirect_on_scalar, 0, 0, HALF, N, staged[:])
         staged = held([P, N], F32, "staged1_0", "w_plane0")
         dw = bank(3, "dw1_0")
         for s0 in (0, HALF):
             part(dw[:, s0:s0 + HALF], 1, 0, s0, s0 + HALF)
         on_vector(staged[:], dw[:])
+        dw = bank(5, "dw1_1")
+        for s0 in (0, HALF):
+            part(dw[:, s0:s0 + HALF], 1, 1, s0, s0 + HALF)
+        on_vector(w1_runs[0][:, HALF:3 * P], dw[:, 0:P])
+        on_vector(w1_runs[1][:], dw[:, P:N])
         staged0_3 = held([P, HALF], F32, "staged0_3", "summed0_1")
         stage([(0, 3, 0, HALF)], 0, on_vector, staged0_3[:])
         second_run = held([P, 3 * P], F32, "second_run")
@@ -342,12 +343,11 @@ def tile_attend_gbpr_wx_ts_kernel(tc, xT, wT, wt, ts, xm, offs, out_0, out_1):
         part(dw[:, 0:P], 1, 2, P, HALF)
         part(dw[:, P:3 * P], 1, 2, HALF, N)
         on_vector(second_run[:], dw[:, 0:3 * P])
-        tiles = stage_pair(5, "w1", ("scaled1_0", "scaled1_1"), (on_vector, on_vector), ((1, 1, 0), (1, 1, HALF)))
         place(on_vector, 1, 0, 0, N, staged[:])
         store_window(0, nc.sync)
         place(on_vector, 0, 3, 0, HALF, staged0_3[:])
 
-        place(indirect_on_scalar, 1, 1, 0, HALF, tiles[0][:])
+        place_run(indirect_on_scalar, 1, HALF, 5 * P, w1_runs[0][:])
         held_back = held([P, HALF + 3 * P], F32, "staged0_3_neg_first_run", "scaled1_0")
         runs = [held_back[:, HALF:HALF + 3 * P], second_run[:]]
         dw = bank(4, "dw2_first_run")
@@ -357,7 +357,7 @@ def tile_attend_gbpr_wx_ts_kernel(tc, xT, wT, wt, ts, xm, offs, out_0, out_1):
         dw = bank(6, "dw0_3_neg")
         part(dw[:, 0:HALF], 0, 3, HALF, N)
         on_scalar(held_back[:, 0:HALF], dw[:, 0:HALF])
-        place(indirect_on_scalar, 1, 1, HALF, N, tiles[1][:])
+        place_run(indirect_on_scalar, 1, 5 * P, 8 * P, w1_runs[1][:])
         store_window(1, nc.sync)
         place_run(indirect_on_scalar, 2, HALF, 5 * P, runs[0])
         place(indirect_on_scalar, 0, 3, HALF, N, held_back[:, 0:HALF])
@@ -367,7 +367,7 @@ def tile_attend_gbpr_wx_ts_kernel(tc, xT, wT, wt, ts, xm, offs, out_0, out_1):
         h_both = mx_operand("h_i", "h_planes", B * K)
         h_i = [columns(h_both, K * b) for b in range(B)]
         for b in range(B):
-            quantize(h_i[b], E5M2, h_turned[:, PACK * R * b:PACK * R * (b + 1)])
+            quantize(h_i[b], E5M2, h_turned[b][:])
         last = held([P, N], F32, "staged1_3", "x_raw1")
         stage([(1, 3, 0, N)], 0, on_vector, last[:])
         for b, tag in enumerate(("w_plane3", "xm_raw0")):

@@ -67,9 +67,9 @@ def tile_attend_gbpr_wx_ts_kernel(tc, xT, wT, wt, ts, xm, offs, out_0, out_1):
         def weave(copy, packed, source):
             copy(woven(packed), planes(source))
 
-        def weave_rows(copy, packed, raw, e):
-            copy(packed.rearrange("p (n s t) -> p n t s", s=2, t=PACK),
-                 raw.rearrange("p t (n e s) -> p e n t s", e=2, s=2)[:, e])
+        def weave_rows(copy, packed, raw, half):
+            copy(packed.rearrange("p (e n s t) -> p n t e s", e=2, s=2, t=PACK),
+                 raw[:, :, HALF * half:HALF * (half + 1)].rearrange("p t (n e s) -> p n t e s", e=2, s=2))
 
         def weave_on_gpsimd(packed, source):
             nc.gpsimd.tensor_scalar(packed.rearrange("p (c t) -> p c t", t=PACK), source.rearrange("p t c -> p c t"), 1.0, 0.0, MULT, ADD)
@@ -237,11 +237,17 @@ def tile_attend_gbpr_wx_ts_kernel(tc, xT, wT, wt, ts, xm, offs, out_0, out_1):
         for s0 in (0, HALF):
             weave(on_scalar, w_packed[1][:, PACK * s0:PACK * (s0 + HALF)], by_plane(w_planes[1][:])[:, :, s0:s0 + HALF])
             quantize(w_d[0], E4M3, w_packed[0][:, PACK * s0:PACK * (s0 + HALF)], s0, s0 + HALF)
+
+        def quantize_rows(b, packed, half):
+            for e in range(2):
+                c0 = HALF * e + P * half
+                quantize(x_d[b], E4M3, packed[:, K * e:K * (e + 1)], c0, c0 + P)
+
         x0_packed = [held([P, 2 * K], BF16, "x0_packed%d" % e) for e in range(2)]
         for e in range(2):
             weave_rows(on_vector, x0_packed[e][:], x_raw[0][:], e)
-        for e in range(2):
-            quantize(x_d[0], E4M3, x0_packed[e][:], HALF * e, HALF * (e + 1))
+        for half in range(2):
+            quantize_rows(0, x0_packed[half], half)
         scores0 = scores_of(0, (0, 1, 2, 3))
         w_i = {(0, 0): mx_operand("w_i0_0", "x_raw0", HALF)}
         quantize(w_i[0, 0], E4M3, w_turned[0, 0][:], 0, HALF)
@@ -250,8 +256,8 @@ def tile_attend_gbpr_wx_ts_kernel(tc, xT, wT, wt, ts, xm, offs, out_0, out_1):
         weave_rows(on_vector, x1_packed[0][:], x_raw[1][:], 0)
         w_d[1] = mx_operand("w_d1", "x0_packed0")
         quantize(w_d[1], E4M3, w_packed[1])
-        for e in (1, 0):
-            quantize(x_d[1], E4M3, x1_packed[e][:], HALF * e, HALF * (e + 1))
+        for half in (1, 0):
+            quantize_rows(1, x1_packed[half], half)
         xm0_packed = held([P, PACK * D], BF16, "xm0_packed", "x0_packed1")
         weave_on_gpsimd(xm0_packed[:], xm_raw[0][:])
         weights0 = spread_weights(0, 6)

@@ -131,9 +131,9 @@ def tile_attend_gbpr_wx_ts_kernel(tc, xT, wT, wt, ts, xm, offs, out_0, out_1):
             turn = bank(k, "w_turn%d_%d" % (b, g))
             for c in range(4):
                 t = 2 * g + c // 2
-                nc.tensor.transpose(turn[:, P * c:P * (c + 1)], w_planes[b][:, N * t:N * (t + 1)].bitcast(F32)[:, c % 2::2], ident[:])
-            copy(w_turned[b, g][:].bitcast(F32).rearrange("q (t p e) -> q t p e", t=2, e=2),
-                 turn[:].rearrange("q (t e p) -> q t p e", t=2, e=2))
+                nc.tensor.transpose(turn[:, HALF * (c % 2) + c // 2:HALF * (c % 2 + 1):2], w_planes[b][:, N * t:N * (t + 1)].bitcast(F32)[:, c % 2::2], ident[:])
+            copy(w_turned[b, g][:].bitcast(F32).rearrange("q (c e) -> q c e", e=2),
+                 turn[:].rearrange("q (e c) -> q c e", e=2))
 
         w_packed = [held([P, PACK * K], BF16, "w_packed%d" % b)[:] for b in range(B)]
 
@@ -223,7 +223,7 @@ def tile_attend_gbpr_wx_ts_kernel(tc, xT, wT, wt, ts, xm, offs, out_0, out_1):
             gx = bank(k, "gx%d_%d" % (b, t))
             for g in range(2):
                 product(gx[:, HALF * g:HALF * (g + 1)], h_i[b], E5M2, t, w_i[b, g], E4M3, 0, HALF)
-            copy(staged[:, D * t:D * (t + 1)].rearrange("r (p u) -> r p u", u=PACK), gx[:].rearrange("r (u p) -> r p u", u=PACK))
+            copy(staged[:, D * t:D * (t + 1)].rearrange("r (p g t) -> r p g t", g=2, t=2), gx[:].rearrange("r (g p t) -> r p g t", g=2, t=2))
 
         def store_rows(b, t0, t1, queue, staged):
             queue.dma_start(out=out_1[b].rearrange("(p t) d -> p (t d)", t=PACK)[:, D * t0:D * t1], in_=staged[:, D * t0:D * t1])

@@ -22,6 +22,7 @@ P = 128
 PACK = 4
 K = P * PACK
 HALF = N // 2
+RUN = 3 * P
 ALIGN = 64
 
 
@@ -55,11 +56,11 @@ def tile_attend_gbpr_wx_ts_kernel(tc, xT, wT, wt, ts, xm, offs, out_0, out_1):
         def indirect_on_scalar(out, in_):
             nc.scalar.activation(out, in_, COPY)
 
-        def woven(packed, run=4):
-            return packed.rearrange("p (c i t) -> p c t i", i=run, t=PACK)
+        def woven(packed):
+            return packed.rearrange("p (c i t) -> p c t i", i=PACK, t=PACK)
 
-        def planes(ap, run=4):
-            return ap.rearrange("p t (c i) -> p c t i", i=run)
+        def planes(ap):
+            return ap.rearrange("p t (c i) -> p c t i", i=PACK)
 
         def by_plane(flat):
             return flat.rearrange("p (t c) -> p t c", t=PACK)
@@ -83,6 +84,8 @@ def tile_attend_gbpr_wx_ts_kernel(tc, xT, wT, wt, ts, xm, offs, out_0, out_1):
         ident_h = held([P, P], F32, "ident_h")
         make_identity(nc, ident_h[:])
 
+        ts_row = held([P, T], F32, "ts_row")
+        nc.sync.dma_start(out=ts_row[P - 1:P, :], in_=ts[0:1, :])
         offsets = lists.tile([P, B * N // 16], U16, name="offsets")
         nc.sync.dma_start(offsets[:], offs)
 
@@ -90,8 +93,6 @@ def tile_attend_gbpr_wx_ts_kernel(tc, xT, wT, wt, ts, xm, offs, out_0, out_1):
             return offsets[:, (N * b + s0) // 16:(N * b + s1) // 16]
 
         row_weight = held([P, B, PACK], F32, "row_weight")
-        ts_row = held([P, T], F32, "ts_row")
-        nc.sync.dma_start(out=ts_row[P - 1:P, :], in_=ts[0:1, :])
         nc.vector.memset(ts_row[0:P - 1, :].bitcast(U32), 0)
 
         w_rows = wT.rearrange("(p t) c -> t p c", t=PACK)
@@ -131,15 +132,16 @@ def tile_attend_gbpr_wx_ts_kernel(tc, xT, wT, wt, ts, xm, offs, out_0, out_1):
             turn = bank(k, "w_turn%d_%d" % (b, g))
             for c in range(4):
                 t = 2 * g + c // 2
-                nc.tensor.transpose(turn[:, HALF * (c % 2) + c // 2:HALF * (c % 2 + 1):2], w_planes[b][:, N * t:N * (t + 1)].bitcast(F32)[:, c % 2::2], ident[:])
+                nc.tensor.transpose(turn[:, HALF * (c % 2) + c // 2:HALF * (c % 2 + 1):2],
+                                    w_planes[b][:, N * t:N * (t + 1)].bitcast(F32)[:, c % 2::2], ident[:])
             copy(w_turned[b, g][:].bitcast(F32).rearrange("q (c e) -> q c e", e=2),
                  turn[:].rearrange("q (e c) -> q c e", e=2))
 
         w_packed = [held([P, PACK * K], BF16, "w_packed%d" % b)[:] for b in range(B)]
 
-        def weave_pair(copy, b, g, s0=0, s1=N):
-            copy(woven(w_packed[b][:, PACK * s0:PACK * s1])[:, :, 2 * g:2 * g + 2, :],
-                 planes(by_plane(w_planes[b][:])[:, :, s0:s1])[:, :, 2 * g:2 * g + 2, :])
+        def weave_pair(copy, g, s0, s1):
+            copy(woven(w_packed[0][:, PACK * s0:PACK * s1])[:, :, 2 * g:2 * g + 2, :],
+                 planes(by_plane(w_planes[0][:])[:, :, s0:s1])[:, :, 2 * g:2 * g + 2, :])
 
         for t in range(PACK):
             if t < PACK - 1:
@@ -151,169 +153,164 @@ def tile_attend_gbpr_wx_ts_kernel(tc, xT, wT, wt, ts, xm, offs, out_0, out_1):
                 for s0 in (0, HALF):
                     indirect_on_scalar(w_planes[1][:, N * t + s0:N * t + s0 + HALF], w_plane[t][:].indirect(listed(1, s0, s0 + HALF)))
             if t == 1:
-                weave_pair(on_scalar, 0, 0)
+                weave_pair(on_scalar, 0, 0, N)
                 turn_w(0, 0, 2, on_vector)
 
-        def columns(operand, c0, width=K):
+        def columns(operand, c0, width):
             return operand[0][:, c0:c0 + width], operand[1][:, c0:c0 + width]
 
-        def scores_of(b, banks):
+        def scores_of(b):
             scores = {}
             for half in range(2):
                 for j in range(2):
-                    scores[half, j] = bank(banks[2 * j + half], "score%d_%d_%d" % (b, half, j))
+                    scores[half, j] = bank(2 * j + half, "score%d_%d_%d" % (b, half, j))
                     product(scores[half, j][:], w_d[b], E4M3, 2 * half + j, x_d[b], E4M3)
             return scores
 
         def spread_weights(b, k):
             spread = bank(k, "weights%d" % b)
             for t in range(PACK):
-                nc.tensor.transpose(spread[:, HALF * (t // 2) + t % 2:HALF * (t // 2 + 1):2], row_weight[:, b, t:t + 1].to_broadcast([P, P]), ident[:])
+                nc.tensor.transpose(spread[:, HALF * (t // 2) + t % 2:HALF * (t // 2 + 1):2],
+                                    row_weight[:, b, t:t + 1].to_broadcast([P, P]), ident[:])
             return spread[:]
 
-        def sigmoids(b, scores, scaled, summed, runs, tag=None):
+        def sigmoids(b, scores, scaled, summed, runs, tag):
             sig = held([P, 2 * R], F32, "sig%d" % b, tag)
             for j in range(2):
-                nc.scalar.activation(scaled[j], scores[0, j][:], COPY, scale=signed[0][:, 2 * b + j:2 * b + j + 1])
-                nc.vector.scalar_tensor_tensor(summed[j], scores[1, j][:], signed[1][:, 2 * b + j:2 * b + j + 1], scaled[j], MULT, ADD)
+                nc.scalar.activation(scaled[:, R * j:R * (j + 1)], scores[0, j][:], COPY, scale=signed[0][:, 2 * b + j:2 * b + j + 1])
+                nc.vector.scalar_tensor_tensor(summed[j], scores[1, j][:], signed[1][:, 2 * b + j:2 * b + j + 1],
+                                               scaled[:, R * j:R * (j + 1)], MULT, ADD)
             for c0, c1, source in runs:
                 nc.scalar.activation(sig[:, c0:c1], source, SIGMOID)
             return [sig[:, R * j:R * (j + 1)] for j in range(2)]
 
-        h_cols = {}
+        h_cols = {key: held([P, 2 * R], BF16, "h_cols%d_%d" % key) for key in ((0, 0), (1, 0), (1, 1))}
         both_planes = held([P, B * PACK * R], BF16, "h_planes")
         h_planes = [both_planes[:, PACK * R * b:PACK * R * (b + 1)] for b in range(B)]
 
         def h_tile(b, c):
             return h_cols[b, c // 2][:, R * (c % 2):R * (c % 2 + 1)]
 
-        def form_h(b, half, sig, weights, place=None, tiles=(0, 1)):
-            if tiles[0] == 0:
-                h_cols[b, half] = held([P, 2 * R], BF16, "h_cols%d_%d" % (b, half))[:] if place is None else place
+        def form_h(b, half, tiles, sig, weights):
             for j in tiles:
                 c = 2 * half + j
-                nc.vector.scalar_tensor_tensor(h_tile(b, c), sig[j],
-                                               signed[half][:, 2 * b + j:2 * b + j + 1], weights, MULT, MULT)
+                nc.vector.scalar_tensor_tensor(h_tile(b, c), sig[j], signed[half][:, 2 * b + j:2 * b + j + 1], weights, MULT, MULT)
                 nc.sync.dma_start(out=h_planes[b][P // PACK * c:P // PACK * (c + 1), :].rearrange("a (u r) -> a u r", u=PACK),
                                   in_=h_tile(b, c))
 
-        def turn_h(b, half, k, copy, packed, unit=ident):
+        def turn_h(b, half, k, copy, packed, unit):
             turn = bank(k, "h_turn%d_%d" % (b, half))
             for j in range(2):
                 for e in range(2):
-                    nc.tensor.transpose(turn[:, P * (2 * j + e):P * (2 * j + e + 1)], h_tile(b, 2 * half + j).bitcast(F32)[:, P * e:P * (e + 1)], unit[:])
+                    nc.tensor.transpose(turn[:, P * (2 * j + e):P * (2 * j + e + 1)],
+                                        h_tile(b, 2 * half + j).bitcast(F32)[:, P * e:P * (e + 1)], unit[:])
             copy(packed.bitcast(F32).rearrange("p (j q e) -> p j q e", j=2, e=2),
                  turn[:].rearrange("p (j e q) -> p j q e", j=2, e=2))
 
-        def stage(parts, k, copy, staged):
-            dw = bank(k, "dw%d_%d_%d" % parts[0][:3])
+        def table_gradient(k, name, parts):
+            dw = bank(k, name)
             c0 = 0
             for b, j, s0, s1 in parts:
-                product(dw[:, c0:c0 + s1 - s0], xm_r[b], E4M3, j, h_r[b], E5M2, s0, s1)
+                half = s0 // HALF
+                product(dw[:, c0:c0 + s1 - s0], xm_r[b], E4M3, j, h_r[b, half], E5M2, s0 - HALF * half, s1 - HALF * half)
                 c0 = c0 + s1 - s0
-            copy(staged, dw[:, 0:c0])
+            return dw
 
-        def place(scatter, b, j, s0, s1, source):
-            scatter(window[j][:].indirect(listed(b, s0, s1)), source)
+        def place(scatter, j, s0, s1, source):
+            scatter(window[j][:].indirect(offsets[:, s0 // 16:s1 // 16]), source)
 
-        def store_window(j, queue):
-            queue.dma_start(out=out_0[P * j:P * (j + 1), :], in_=window[j][:])
+        def store_window(j, queues):
+            width = T // len(queues)
+            for n, queue in enumerate(queues):
+                cols = slice(width * n, width * (n + 1))
+                queue.dma_start(out=out_0[P * j:P * (j + 1), cols], in_=window[j][:, cols])
 
-        def row_tile(b, t, k, copy, staged):
+        def row_tile(b, t, k, staged):
             gx = bank(k, "gx%d_%d" % (b, t))
             for g in range(2):
                 product(gx[:, HALF * g:HALF * (g + 1)], h_i[b], E5M2, t, w_i[b, g], E4M3, 0, HALF)
-            copy(staged[:, D * t:D * (t + 1)].rearrange("r (p g t) -> r p g t", g=2, t=2), gx[:].rearrange("r (g p t) -> r p g t", g=2, t=2))
-
-        def store_rows(b, t0, t1, queue, staged):
-            queue.dma_start(out=out_1[b].rearrange("(p t) d -> p (t d)", t=PACK)[:, D * t0:D * t1], in_=staged[:, D * t0:D * t1])
-
-        w_d = [mx_operand("w_d0"), None]
-        x_d = [mx_operand("x_d%d" % b) for b in range(B)]
-        xm_r = [mx_operand("xm_r0"), None]
-        h_r = [mx_operand("h_r0"), None]
-        for s0 in (0, HALF):
-            weave_pair(on_vector, 0, 1, s0, s0 + HALF)
-        for s0 in (0, HALF):
-            weave(on_scalar, w_packed[1][:, PACK * s0:PACK * (s0 + HALF)], by_plane(w_planes[1][:])[:, :, s0:s0 + HALF])
-            quantize(w_d[0], E4M3, w_packed[0][:, PACK * s0:PACK * (s0 + HALF)], s0, s0 + HALF)
+            on_vector(staged[:, D * t:D * (t + 1)].rearrange("r (p g t) -> r p g t", g=2, t=2), gx[:].rearrange("r (g p t) -> r p g t", g=2, t=2))
 
         def quantize_rows(b, packed, half):
             for e in range(2):
                 c0 = HALF * e + P * half
                 quantize(x_d[b], E4M3, packed[:, K * e:K * (e + 1)], c0, c0 + P)
 
-        x0_packed = [held([P, 2 * K], BF16, "x0_packed%d" % e) for e in range(2)]
-        for e in range(2):
-            weave_rows(on_vector, x0_packed[e][:], x_raw[0][:], e)
+        w_d = [mx_operand("w_d0"), None]
+        x_d = [mx_operand("x_d%d" % b) for b in range(B)]
+        for s0 in (0, HALF):
+            weave_pair(on_vector, 1, s0, s0 + HALF)
+        for s0 in (0, HALF):
+            weave(on_scalar, w_packed[1][:, PACK * s0:PACK * (s0 + HALF)], by_plane(w_planes[1][:])[:, :, s0:s0 + HALF])
+            quantize(w_d[0], E4M3, w_packed[0][:, PACK * s0:PACK * (s0 + HALF)], s0, s0 + HALF)
+        x0_packed = [held([P, 2 * K], BF16, "x0_packed%d" % half) for half in range(2)]
+        for half in range(2):
+            weave_rows(on_vector, x0_packed[half][:], x_raw[0][:], half)
         for half in range(2):
             quantize_rows(0, x0_packed[half], half)
-        scores0 = scores_of(0, (0, 1, 2, 3))
+        scores0 = scores_of(0)
         w_i = {(0, 0): mx_operand("w_i0_0", "x_raw0", HALF)}
         quantize(w_i[0, 0], E4M3, w_turned[0, 0][:], 0, HALF)
-        x1_packed = [held([P, 2 * K], BF16, "x1_packed%d" % e, ("x0_packed1", None)[e]) for e in range(2)]
+        x1_packed = [held([P, 2 * K], BF16, "x1_packed%d" % half, ("x0_packed1", None)[half]) for half in range(2)]
         weave_rows(on_scalar, x1_packed[1][:], x_raw[1][:], 1)
         weave_rows(on_vector, x1_packed[0][:], x_raw[1][:], 0)
         w_d[1] = mx_operand("w_d1", "x0_packed0")
         quantize(w_d[1], E4M3, w_packed[1])
         for half in (1, 0):
             quantize_rows(1, x1_packed[half], half)
+
         xm0_packed = held([P, PACK * D], BF16, "xm0_packed", "x0_packed1")
         weave_on_gpsimd(xm0_packed[:], xm_raw[0][:])
         weights0 = spread_weights(0, 6)
         scaled = held([P, 2 * R], F32, "scaled0", "x_raw1")
-        scaled = [scaled[:, 0:R], scaled[:, R:2 * R]]
         summed = [held([P, R], F32, "summed0_%d" % j)[:] for j in range(2)]
-        sig0 = sigmoids(0, scores0, scaled, summed, ((0, R, summed[0]), (R, 2 * R, summed[1])))
+        sig0 = sigmoids(0, scores0, scaled, summed, ((0, R, summed[0]), (R, 2 * R, summed[1])), None)
         w_turned[1, 0] = held([P, 2 * D], BF16, "w_turned1_0", "w_packed1")
         turn_w(1, 0, 7, on_scalar)
-        h0_packed = held([P, 2 * K], BF16, "h0_packed", "ts_listed")[:]
-        form_h(0, 0, sig0, weights0)
+        h0_pos = held([P, 2 * K], BF16, "h0_pos", "ts_listed")
+        form_h(0, 0, (0, 1), sig0, weights0)
         w_turned[1, 1] = held([P, 2 * D], BF16, "w_turned1_1", "x_raw1")
         turn_w(1, 1, 5, on_vector)
-        scores1 = scores_of(1, (0, 1, 2, 3))
-        turn_h(0, 0, 7, on_scalar, h0_packed, ident_h)
+        scores1 = scores_of(1)
+        turn_h(0, 0, 7, on_scalar, h0_pos[:], ident_h)
         scaled = held([P, 2 * R], F32, "scaled1", "summed0_0")
         summed = held([P, 2 * R], F32, "summed1")
-        sig1 = sigmoids(1, scores1, [scaled[:, 0:R], scaled[:, R:2 * R]], [summed[:, 0:R], summed[:, R:2 * R]], ((0, 2 * R, summed[:]),), "ident_h")
+        sig1 = sigmoids(1, scores1, scaled, [summed[:, 0:R], summed[:, R:2 * R]], ((0, 2 * R, summed[:]),), "ident_h")
         w_turned[0, 1] = held([P, 2 * D], BF16, "w_turned0_1", "summed0_1")
         turn_w(0, 1, 4, on_scalar)
+        xm_r = [mx_operand("xm_r0"), None]
+        h_r = {(0, 0): mx_operand("h_r0_pos", None, HALF)}
         quantize(xm_r[0], E4M3, xm0_packed[:, 0:2 * K], 0, HALF)
-        quantize(h_r[0], E5M2, h0_packed, 0, HALF)
+        quantize(h_r[0, 0], E5M2, h0_pos[:], 0, HALF)
         quantize(xm_r[0], E4M3, xm0_packed[:, 2 * K:4 * K], HALF, D)
-        third = held([P, 8 * K], BF16, "xm1_packed_h_negatives", "ts_listed")
-        xm1_packed, h_neg = third[:, 0:4 * K], [third[:, 4 * K:6 * K], third[:, 6 * K:8 * K]]
-        form_h(0, 1, sig0, weights0, held([P, 2 * R], BF16, "h_cols0_1", "x0_packed1")[:])
+        h_cols[0, 1] = held([P, 2 * R], BF16, "h_cols0_1", "x0_packed1")
+        form_h(0, 1, (0, 1), sig0, weights0)
         weights1 = spread_weights(1, 5)
 
         positives = held([P, 3 * HALF], F32, "positives", "summed1")
         for j, k in enumerate((1, 0, 2)):
-            stage([(0, j, 0, HALF)], k, on_scalar, positives[:, HALF * j:HALF * (j + 1)])
-            place(indirect_on_scalar, 0, j, 0, HALF, positives[:, HALF * j:HALF * (j + 1)])
+            dw = table_gradient(k, "dw0_%d_pos" % j, [(0, j, 0, HALF)])
+            on_scalar(positives[:, HALF * j:HALF * (j + 1)], dw[:, 0:HALF])
+            place(indirect_on_scalar, j, 0, HALF, positives[:, HALF * j:HALF * (j + 1)])
 
+        xm1_h_neg = held([P, 8 * K], BF16, "xm1_packed_h_negatives", "ts_listed")
+        xm1_packed, h_neg = xm1_h_neg[:, 0:4 * K], [xm1_h_neg[:, 4 * K:6 * K], xm1_h_neg[:, 6 * K:8 * K]]
         h1_pos = held([P, 2 * K], BF16, "h1_pos")
         weave_on_gpsimd(xm1_packed, xm_raw[1][:])
-        form_h(1, 0, sig1, weights1)
-        form_h(1, 1, sig1, weights1, None, (0,))
-        turn_h(0, 1, 4, on_vector, h_neg[0])
-        form_h(1, 1, sig1, weights1, None, (1,))
-        late = mx_operand("late", "xm_raw1", 5 * HALF)
-        h0_neg, h_r[1], xm_r[1] = columns(late, 0, HALF), columns(late, HALF), columns(late, 3 * HALF)
-        quantize(h0_neg, E5M2, h_neg[0], 0, HALF)
-        turn_h(1, 0, 1, on_vector, h1_pos[:])
+        form_h(1, 0, (0, 1), sig1, weights1)
+        form_h(1, 1, (0,), sig1, weights1)
+        turn_h(0, 1, 4, on_vector, h_neg[0], ident)
+        form_h(1, 1, (1,), sig1, weights1)
+        along_rows = mx_operand("along_rows", "xm_raw1", 5 * HALF)
+        for n, key in enumerate(((0, 1), (1, 0), (1, 1))):
+            h_r[key] = columns(along_rows, HALF * n, HALF)
+        xm_r[1] = columns(along_rows, 3 * HALF, K)
+        quantize(h_r[0, 1], E5M2, h_neg[0], 0, HALF)
+        turn_h(1, 0, 1, on_vector, h1_pos[:], ident)
         quantize(xm_r[1], E4M3, xm1_packed)
-        turn_h(1, 1, 6, on_vector, h_neg[1])
-        quantize(h_r[1], E5M2, h1_pos[:], 0, HALF)
-        quantize(h_r[1], E5M2, h_neg[1], HALF, N)
-
-        def part(out, b, j, s0, s1):
-            if b == 0 and s0 == HALF:
-                product(out, xm_r[0], E4M3, j, h0_neg, E5M2, 0, HALF)
-            else:
-                product(out, xm_r[b], E4M3, j, h_r[b], E5M2, s0, s1)
-
-        def place_run(scatter, j, s0, s1, source):
-            scatter(window[j][:].indirect(offsets[:, s0 // 16:s1 // 16]), source)
+        turn_h(1, 1, 6, on_vector, h_neg[1], ident)
+        quantize(h_r[1, 0], E5M2, h1_pos[:], 0, HALF)
+        quantize(h_r[1, 1], E5M2, h_neg[1], 0, HALF)
 
         rest = mx_operand("w_i_rest", "h1_pos", 3 * HALF)
         for n, key in enumerate(((0, 1), (1, 0), (1, 1))):
@@ -323,66 +320,53 @@ def tile_attend_gbpr_wx_ts_kernel(tc, xT, wT, wt, ts, xm, offs, out_0, out_1):
         for b in range(B):
             for e in range(2):
                 nc.gpsimd.tensor_scalar(h_turned[b][:, 2 * K * e:2 * K * (e + 1)].rearrange("q (s n u) -> q s n u", s=2, u=PACK),
-                                        by_plane(h_planes[b])[:, :, HALF * e:HALF * (e + 1)].rearrange("q u (n s) -> q s n u", s=2), 1.0, 0.0, MULT, ADD)
-        staged = held([P, HALF], F32, "staged0_0_neg", "sig0")
-        w1_runs = [held([P, 3 * P], F32, "window1_run%d" % n, "scaled1_%d" % n) for n in range(2)]
-        dw = bank(7, "dw0_neg")
-        for j in range(2):
-            part(dw[:, HALF * j:HALF * (j + 1)], 0, j, HALF, N)
-        on_scalar(staged[:], dw[:, 0:HALF])
-        on_scalar(w1_runs[0][:, 0:HALF], dw[:, HALF:N])
-        place(indirect_on_scalar, 0, 0, HALF, N, staged[:])
-        staged = held([P, N], F32, "staged1_0", "w_plane0")
-        dw = bank(3, "dw1_0")
-        for s0 in (0, HALF):
-            part(dw[:, s0:s0 + HALF], 1, 0, s0, s0 + HALF)
-        on_vector(staged[:], dw[:])
-        dw = bank(5, "dw1_1")
-        for s0 in (0, HALF):
-            part(dw[:, s0:s0 + HALF], 1, 1, s0, s0 + HALF)
-        on_vector(w1_runs[0][:, HALF:3 * P], dw[:, 0:P])
-        on_vector(w1_runs[1][:], dw[:, P:N])
-        staged0_3 = held([P, HALF], F32, "staged0_3", "summed0_1")
-        stage([(0, 3, 0, HALF)], 0, on_vector, staged0_3[:])
-        second_run = held([P, 3 * P], F32, "second_run")
-        dw = bank(2, "dw2_second_run")
-        part(dw[:, 0:P], 1, 2, P, HALF)
-        part(dw[:, P:3 * P], 1, 2, HALF, N)
-        on_vector(second_run[:], dw[:, 0:3 * P])
-        place(on_vector, 1, 0, 0, N, staged[:])
-        store_window(0, nc.sync)
-        place(on_vector, 0, 3, 0, HALF, staged0_3[:])
+                                        by_plane(h_planes[b])[:, :, HALF * e:HALF * (e + 1)].rearrange("q u (n s) -> q s n u", s=2),
+                                        1.0, 0.0, MULT, ADD)
 
-        place_run(indirect_on_scalar, 1, HALF, 5 * P, w1_runs[0][:])
-        held_back = held([P, HALF + 3 * P], F32, "staged0_3_neg_first_run", "scaled1_0")
-        runs = [held_back[:, HALF:HALF + 3 * P], second_run[:]]
-        dw = bank(4, "dw2_first_run")
-        part(dw[:, 0:HALF], 0, 2, HALF, N)
-        part(dw[:, HALF:3 * P], 1, 2, 0, P)
-        on_scalar(runs[0], dw[:, 0:3 * P])
-        dw = bank(6, "dw0_3_neg")
-        part(dw[:, 0:HALF], 0, 3, HALF, N)
-        on_scalar(held_back[:, 0:HALF], dw[:, 0:HALF])
-        place_run(indirect_on_scalar, 1, 5 * P, 8 * P, w1_runs[1][:])
-        store_window(1, nc.sync)
-        place_run(indirect_on_scalar, 2, HALF, 5 * P, runs[0])
-        place(indirect_on_scalar, 0, 3, HALF, N, held_back[:, 0:HALF])
-        place_run(indirect_on_scalar, 2, 5 * P, 8 * P, runs[1])
-        store_window(2, nc.scalar)
+        staged = held([P, HALF], F32, "staged0_0_neg", "sig0")
+        window1_runs = [held([P, RUN], F32, "window1_run%d" % n) for n in range(2)]
+        dw = table_gradient(7, "dw0_neg", [(0, j, HALF, N) for j in range(2)])
+        on_scalar(staged[:], dw[:, 0:HALF])
+        on_scalar(window1_runs[0][:, 0:HALF], dw[:, HALF:N])
+        place(indirect_on_scalar, 0, HALF, N, staged[:])
+        staged = held([P, N], F32, "staged1_0", "w_plane0")
+        on_vector(staged[:], table_gradient(3, "dw1_0", [(1, 0, 0, HALF), (1, 0, HALF, N)])[:])
+        dw = table_gradient(5, "dw1_1", [(1, 1, 0, HALF), (1, 1, HALF, N)])
+        on_vector(window1_runs[0][:, HALF:RUN], dw[:, 0:P])
+        on_vector(window1_runs[1][:], dw[:, P:N])
+        staged0_3 = held([P, HALF], F32, "staged0_3", "summed0_1")
+        on_vector(staged0_3[:], table_gradient(0, "dw0_3_pos", [(0, 3, 0, HALF)])[:, 0:HALF])
+        window2_last = held([P, RUN], F32, "window2_last")
+        on_vector(window2_last[:], table_gradient(2, "dw2_last", [(1, 2, P, HALF), (1, 2, HALF, N)])[:, 0:RUN])
+        place(on_vector, 0, N, B * N, staged[:])
+        store_window(0, (nc.sync,))
+        place(on_vector, 3, 0, HALF, staged0_3[:])
+
+        place(indirect_on_scalar, 1, HALF, HALF + RUN, window1_runs[0][:])
+        staged = held([P, HALF + RUN], F32, "staged0_3_neg_window2_first", "window1_run0")
+        on_scalar(staged[:, HALF:HALF + RUN], table_gradient(4, "dw2_first", [(0, 2, HALF, N), (1, 2, 0, P)])[:, 0:RUN])
+        on_scalar(staged[:, 0:HALF], table_gradient(6, "dw0_3_neg", [(0, 3, HALF, N)])[:, 0:HALF])
+        place(indirect_on_scalar, 1, HALF + RUN, B * N, window1_runs[1][:])
+        store_window(1, (nc.sync,))
+        place(indirect_on_scalar, 2, HALF, HALF + RUN, staged[:, HALF:HALF + RUN])
+        place(indirect_on_scalar, 3, HALF, N, staged[:, 0:HALF])
+        place(indirect_on_scalar, 2, HALF + RUN, B * N, window2_last[:])
+        store_window(2, (nc.scalar, nc.scalar))
 
         h_both = mx_operand("h_i", "h_planes", B * K)
-        h_i = [columns(h_both, K * b) for b in range(B)]
+        h_i = [columns(h_both, K * b, K) for b in range(B)]
         for b in range(B):
             quantize(h_i[b], E5M2, h_turned[b][:])
         last = held([P, N], F32, "staged1_3", "x_raw1")
-        stage([(1, 3, 0, N)], 0, on_vector, last[:])
+        dw = bank(0, "dw1_3")
+        product(dw[:], xm_r[1], E4M3, 3, columns(along_rows, HALF, N), E5M2)
+        on_vector(last[:], dw[:])
         for b, tag in enumerate(("w_plane3", "xm_raw0")):
-            gx = held([P, PACK * D], F32, "gx_staged%d" % b, tag)
+            staged = held([P, PACK * D], F32, "gx_staged%d" % b, tag)
+            rows = out_1[b].rearrange("(p t) d -> p (t d)", t=PACK)
             for t, k in enumerate(((1, 5, 7, 3), (0, 1, 5, 7))[b]):
-                row_tile(b, t, k, on_vector, gx)
+                row_tile(b, t, k, staged)
                 if t % 2 == 1:
-                    store_rows(b, t - 1, t + 1, nc.sync, gx)
-        place(on_vector, 1, 3, 0, N, last[:])
-        for half, queue in enumerate((nc.sync, nc.scalar)):
-            cols = slice(T // 2 * half, T // 2 * (half + 1))
-            queue.dma_start(out=out_0[3 * P:4 * P, cols], in_=window[3][:, cols])
+                    nc.sync.dma_start(out=rows[:, D * (t - 1):D * (t + 1)], in_=staged[:, D * (t - 1):D * (t + 1)])
+        place(on_vector, 3, N, B * N, last[:])
+        store_window(3, (nc.sync, nc.scalar))

from contextlib import ExitStack

import concourse.mybir as mybir
from concourse.masks import make_identity

B, N, T, D, R = 2, 512, 2048, 512, 512
FLOPS = 3 * 2 * B * N * D * R

F32 = mybir.dt.float32
BF16 = mybir.dt.bfloat16
U32 = mybir.dt.uint32
U16 = mybir.dt.uint16
U8 = mybir.dt.uint8
E4M3 = mybir.dt.float8_e4m3fn_x4
E5M2 = mybir.dt.float8_e5m2_x4
MULT = mybir.AluOpType.mult
ADD = mybir.AluOpType.add
COPY = mybir.ActivationFunctionType.Copy
SIGMOID = mybir.ActivationFunctionType.Sigmoid

P = 128
PACK = 4
K = P * PACK
HALF = N // 2
RUN = 3 * P
ALIGN = 64


def tile_attend_gbpr_wx_ts_kernel(tc, xT, wT, wt, ts, xm, offs, out_0, out_1):
    nc = tc.nc
    with ExitStack() as ctx:
        lists = ctx.enter_context(tc.tile_pool(name="lists", bufs=1))
        sb = ctx.enter_context(tc.tile_pool(name="sb", bufs=1))
        ps = ctx.enter_context(tc.psum_pool(name="ps", bufs=1))

        def held(shape, dtype, name, tag=None):
            return sb.tile(shape, dtype, name=name, tag=tag or name, align_bytes=ALIGN)

        def bank(k, name):
            return ps.tile([P, K], F32, name=name, tag="bank%d" % k)

        def mx_operand(name, tag=None, width=K):
            return held([P, width], U32, name + "_codes", tag), held([P, width], U8, name + "_scales")

        def quantize(operand, fmt, src, c0=0, c1=K):
            codes, scales = operand
            nc.vector.quantize_mx(out=codes[:, c0:c1].bitcast(fmt), scales=scales[:, c0:c1], in_=src)

        def product(out, fixed, fixed_fmt, j, moving, moving_fmt, c0=0, c1=K):
            cols = slice(P * j, P * (j + 1))
            nc.tensor.matmul_mx(out=out, lhsT=fixed[0][:, cols].bitcast(fixed_fmt), lhsT_scale=fixed[1][:, cols],
                                rhs=moving[0][:, c0:c1].bitcast(moving_fmt), rhs_scale=moving[1][:, c0:c1], start=True, stop=True)

        on_vector, on_scalar = nc.vector.tensor_copy, nc.scalar.copy

        def indirect_on_scalar(out, in_):
            nc.scalar.activation(out, in_, COPY)

        def woven(packed):
            return packed.rearrange("p (c i t) -> p c t i", i=PACK, t=PACK)

        def planes(ap):
            return ap.rearrange("p t (c i) -> p c t i", i=PACK)

        def by_plane(flat):
            return flat.rearrange("p (t c) -> p t c", t=PACK)

        def weave(copy, packed, source):
            copy(woven(packed), planes(source))

        def weave_rows(copy, packed, raw, half):
            copy(packed.rearrange("p (e n s t) -> p n t e s", e=2, s=2, t=PACK),
                 raw[:, :, HALF * half:HALF * (half + 1)].rearrange("p t (n e s) -> p n t e s", e=2, s=2))

        def weave_on_gpsimd(packed, source):
            nc.gpsimd.tensor_scalar(packed.rearrange("p (c t) -> p c t", t=PACK), source.rearrange("p t c -> p c t"), 1.0, 0.0, MULT, ADD)

        warm = held([P, 2], F32, "warm")
        nc.gpsimd.memset(warm[:, 0:1], 0.0)
        nc.scalar.activation(warm[:, 1:2], warm[:, 0:1], SIGMOID)

        ident = held([P, P], F32, "ident")
        make_identity(nc, ident[:])
        ident_h = held([P, P], F32, "ident_h")
        make_identity(nc, ident_h[:])

        ts_row = held([P, T], F32, "ts_row")
        nc.sync.dma_start(out=ts_row[P - 1:P, :], in_=ts[0:1, :])
        offsets = lists.tile([P, B * N // 16], U16, name="offsets")
        nc.sync.dma_start(offsets[:], offs)

        def listed(b, s0=0, s1=N):
            return offsets[:, (N * b + s0) // 16:(N * b + s1) // 16]

        row_weight = held([P, B, PACK], F32, "row_weight")
        nc.vector.memset(ts_row[0:P - 1, :].bitcast(U32), 0)

        w_rows = wT.rearrange("(p t) c -> t p c", t=PACK)
        w_plane = [held([P, T], F32, "w_plane%d" % t) for t in range(PACK)]
        for t in range(PACK):
            nc.sync.dma_start(out=w_plane[t][:], in_=w_rows[t])
        x_raw = [held([P, PACK, R], F32, "x_raw%d" % b) for b in range(B)]
        xm_raw = [held([P, PACK, D], F32, "xm_raw%d" % b) for b in range(B)]
        for b in range(B):
            nc.sync.dma_start(out=x_raw[b][:], in_=xT[b].rearrange("(p j) r -> p j r", j=PACK))
        nc.sync.dma_start(out=row_weight[:], in_=wt.rearrange("b (p t) o -> p b (t o)", t=PACK))
        for b in range(B):
            nc.sync.dma_start(out=xm_raw[b][:], in_=xm[b].rearrange("(p t) d -> p t d", t=PACK))

        window = [held([P, T], F32, "window%d" % j) for j in range(PACK)]
        for j in range(PACK):
            nc.gpsimd.memset(window[j][:], 0.0)

        ts_listed = held([P, B * N], F32, "ts_listed")
        for b, gather in enumerate((on_vector, indirect_on_scalar)):
            gather(ts_listed[:, N * b:N * (b + 1)], ts_row[:].indirect(listed(b)))
        signed = []
        for half, sign in ((0, -1.0), (1, 1.0)):
            turned = bank(half, "ts_turned%d" % half)
            for b in range(B):
                for j in range(2):
                    c0 = N * b + HALF * half + P * j
                    nc.tensor.transpose(turned[:, P * (2 * b + j):P * (2 * b + j + 1)], ts_listed[:, c0:c0 + P], ident[:])
            col = held([P, 2 * B], F32, "signed%d" % half)
            nc.scalar.activation(col[:], turned[:].rearrange("p (k c) -> p k c", c=P)[:, :, P - 1], COPY, scale=sign)
            signed.append(col)

        w_planes = [held([P, PACK * N], BF16, "w_planes%d" % b) for b in range(B)]
        w_turned = {(0, 0): held([P, 2 * D], BF16, "w_turned0_0")}

        def turn_w(b, g, k, copy):
            turn = bank(k, "w_turn%d_%d" % (b, g))
            for c in range(4):
                t = 2 * g + c // 2
                nc.tensor.transpose(turn[:, HALF * (c % 2) + c // 2:HALF * (c % 2 + 1):2],
                                    w_planes[b][:, N * t:N * (t + 1)].bitcast(F32)[:, c % 2::2], ident[:])
            copy(w_turned[b, g][:].bitcast(F32).rearrange("q (c e) -> q c e", e=2),
                 turn[:].rearrange("q (e c) -> q c e", e=2))

        w_packed = [held([P, PACK * K], BF16, "w_packed%d" % b)[:] for b in range(B)]

        def weave_pair(copy, g, s0, s1):
            copy(woven(w_packed[0][:, PACK * s0:PACK * s1])[:, :, 2 * g:2 * g + 2, :],
                 planes(by_plane(w_planes[0][:])[:, :, s0:s1])[:, :, 2 * g:2 * g + 2, :])

        for t in range(PACK):
            if t < PACK - 1:
                on_vector(w_planes[0][:, N * t:N * (t + 1)], w_plane[t][:].indirect(listed(0)))
                indirect_on_scalar(w_planes[1][:, N * t:N * (t + 1)], w_plane[t][:].indirect(listed(1)))
            else:
                on_vector(w_planes[0][:, N * t:N * t + HALF], w_plane[t][:].indirect(listed(0, 0, HALF)))
                indirect_on_scalar(w_planes[0][:, N * t + HALF:N * (t + 1)], w_plane[t][:].indirect(listed(0, HALF, N)))
                for s0 in (0, HALF):
                    indirect_on_scalar(w_planes[1][:, N * t + s0:N * t + s0 + HALF], w_plane[t][:].indirect(listed(1, s0, s0 + HALF)))
            if t == 1:
                weave_pair(on_scalar, 0, 0, N)
                turn_w(0, 0, 2, on_vector)

        def columns(operand, c0, width):
            return operand[0][:, c0:c0 + width], operand[1][:, c0:c0 + width]

        def scores_of(b):
            scores = {}
            for half in range(2):
                for j in range(2):
                    scores[half, j] = bank(2 * j + half, "score%d_%d_%d" % (b, half, j))
                    product(scores[half, j][:], w_d[b], E4M3, 2 * half + j, x_d[b], E4M3)
            return scores

        def spread_weights(b, k):
            spread = bank(k, "weights%d" % b)
            for t in range(PACK):
                nc.tensor.transpose(spread[:, HALF * (t // 2) + t % 2:HALF * (t // 2 + 1):2],
                                    row_weight[:, b, t:t + 1].to_broadcast([P, P]), ident[:])
            return spread[:]

        def sigmoids(b, scores, scaled, summed, runs, tag):
            sig = held([P, 2 * R], F32, "sig%d" % b, tag)
            for j in range(2):
                nc.scalar.activation(scaled[:, R * j:R * (j + 1)], scores[0, j][:], COPY, scale=signed[0][:, 2 * b + j:2 * b + j + 1])
                nc.vector.scalar_tensor_tensor(summed[j], scores[1, j][:], signed[1][:, 2 * b + j:2 * b + j + 1],
                                               scaled[:, R * j:R * (j + 1)], MULT, ADD)
            for c0, c1, source in runs:
                nc.scalar.activation(sig[:, c0:c1], source, SIGMOID)
            return [sig[:, R * j:R * (j + 1)] for j in range(2)]

        h_cols = {key: held([P, 2 * R], BF16, "h_cols%d_%d" % key) for key in ((0, 0), (1, 0), (1, 1))}
        both_planes = held([P, B * PACK * R], BF16, "h_planes")
        h_planes = [both_planes[:, PACK * R * b:PACK * R * (b + 1)] for b in range(B)]

        def h_tile(b, c):
            return h_cols[b, c // 2][:, R * (c % 2):R * (c % 2 + 1)]

        def form_h(b, half, tiles, sig, weights):
            for j in tiles:
                c = 2 * half + j
                nc.vector.scalar_tensor_tensor(h_tile(b, c), sig[j], signed[half][:, 2 * b + j:2 * b + j + 1], weights, MULT, MULT)
                nc.sync.dma_start(out=h_planes[b][P // PACK * c:P // PACK * (c + 1), :].rearrange("a (u r) -> a u r", u=PACK),
                                  in_=h_tile(b, c))

        def turn_h(b, half, k, copy, packed, unit):
            turn = bank(k, "h_turn%d_%d" % (b, half))
            for j in range(2):
                for e in range(2):
                    nc.tensor.transpose(turn[:, P * (2 * j + e):P * (2 * j + e + 1)],
                                        h_tile(b, 2 * half + j).bitcast(F32)[:, P * e:P * (e + 1)], unit[:])
            copy(packed.bitcast(F32).rearrange("p (j q e) -> p j q e", j=2, e=2),
                 turn[:].rearrange("p (j e q) -> p j q e", j=2, e=2))

        def table_gradient(k, name, parts):
            dw = bank(k, name)
            c0 = 0
            for b, j, s0, s1 in parts:
                half = s0 // HALF
                product(dw[:, c0:c0 + s1 - s0], xm_r[b], E4M3, j, h_r[b, half], E5M2, s0 - HALF * half, s1 - HALF * half)
                c0 = c0 + s1 - s0
            return dw

        def place(scatter, j, s0, s1, source):
            scatter(window[j][:].indirect(offsets[:, s0 // 16:s1 // 16]), source)

        def store_window(j, queues):
            width = T // len(queues)
            for n, queue in enumerate(queues):
                cols = slice(width * n, width * (n + 1))
                queue.dma_start(out=out_0[P * j:P * (j + 1), cols], in_=window[j][:, cols])

        def row_tile(b, t, k, staged):
            gx = bank(k, "gx%d_%d" % (b, t))
            for g in range(2):
                product(gx[:, HALF * g:HALF * (g + 1)], h_i[b], E5M2, t, w_i[b, g], E4M3, 0, HALF)
            on_vector(staged[:, D * t:D * (t + 1)].rearrange("r (p g t) -> r p g t", g=2, t=2), gx[:].rearrange("r (g p t) -> r p g t", g=2, t=2))

        def quantize_rows(b, packed, half):
            for e in range(2):
                c0 = HALF * e + P * half
                quantize(x_d[b], E4M3, packed[:, K * e:K * (e + 1)], c0, c0 + P)

        w_d = [mx_operand("w_d0"), None]
        x_d = [mx_operand("x_d%d" % b) for b in range(B)]
        for s0 in (0, HALF):
            weave_pair(on_vector, 1, s0, s0 + HALF)
        for s0 in (0, HALF):
            weave(on_scalar, w_packed[1][:, PACK * s0:PACK * (s0 + HALF)], by_plane(w_planes[1][:])[:, :, s0:s0 + HALF])
            quantize(w_d[0], E4M3, w_packed[0][:, PACK * s0:PACK * (s0 + HALF)], s0, s0 + HALF)
        x0_packed = [held([P, 2 * K], BF16, "x0_packed%d" % half) for half in range(2)]
        for half in range(2):
            weave_rows(on_vector, x0_packed[half][:], x_raw[0][:], half)
        for half in range(2):
            quantize_rows(0, x0_packed[half], half)
        scores0 = scores_of(0)
        w_i = {(0, 0): mx_operand("w_i0_0", "x_raw0", HALF)}
        quantize(w_i[0, 0], E4M3, w_turned[0, 0][:], 0, HALF)
        x1_packed = [held([P, 2 * K], BF16, "x1_packed%d" % half, ("x0_packed1", None)[half]) for half in range(2)]
        weave_rows(on_scalar, x1_packed[1][:], x_raw[1][:], 1)
        weave_rows(on_vector, x1_packed[0][:], x_raw[1][:], 0)
        w_d[1] = mx_operand("w_d1", "x0_packed0")
        quantize(w_d[1], E4M3, w_packed[1])
        for half in (1, 0):
            quantize_rows(1, x1_packed[half], half)

        xm0_packed = held([P, PACK * D], BF16, "xm0_packed", "x0_packed1")
        weave_on_gpsimd(xm0_packed[:], xm_raw[0][:])
        weights0 = spread_weights(0, 6)
        scaled = held([P, 2 * R], F32, "scaled0", "x_raw1")
        summed = [held([P, R], F32, "summed0_%d" % j)[:] for j in range(2)]
        sig0 = sigmoids(0, scores0, scaled, summed, ((0, R, summed[0]), (R, 2 * R, summed[1])), None)
        w_turned[1, 0] = held([P, 2 * D], BF16, "w_turned1_0", "w_packed1")
        turn_w(1, 0, 7, on_scalar)
        h0_pos = held([P, 2 * K], BF16, "h0_pos", "ts_listed")
        form_h(0, 0, (0, 1), sig0, weights0)
        w_turned[1, 1] = held([P, 2 * D], BF16, "w_turned1_1", "x_raw1")
        turn_w(1, 1, 5, on_vector)
        scores1 = scores_of(1)
        turn_h(0, 0, 7, on_scalar, h0_pos[:], ident_h)
        scaled = held([P, 2 * R], F32, "scaled1", "summed0_0")
        summed = held([P, 2 * R], F32, "summed1")
        sig1 = sigmoids(1, scores1, scaled, [summed[:, 0:R], summed[:, R:2 * R]], ((0, 2 * R, summed[:]),), "ident_h")
        w_turned[0, 1] = held([P, 2 * D], BF16, "w_turned0_1", "summed0_1")
        turn_w(0, 1, 4, on_scalar)
        xm_r = [mx_operand("xm_r0"), None]
        h_r = {(0, 0): mx_operand("h_r0_pos", None, HALF)}
        quantize(xm_r[0], E4M3, xm0_packed[:, 0:2 * K], 0, HALF)
        quantize(h_r[0, 0], E5M2, h0_pos[:], 0, HALF)
        quantize(xm_r[0], E4M3, xm0_packed[:, 2 * K:4 * K], HALF, D)
        h_cols[0, 1] = held([P, 2 * R], BF16, "h_cols0_1", "x0_packed1")
        form_h(0, 1, (0, 1), sig0, weights0)
        weights1 = spread_weights(1, 5)

        positives = held([P, 3 * HALF], F32, "positives", "summed1")
        for j, k in enumerate((1, 0, 2)):
            dw = table_gradient(k, "dw0_%d_pos" % j, [(0, j, 0, HALF)])
            on_scalar(positives[:, HALF * j:HALF * (j + 1)], dw[:, 0:HALF])
            place(indirect_on_scalar, j, 0, HALF, positives[:, HALF * j:HALF * (j + 1)])

        xm1_h_neg = held([P, 8 * K], BF16, "xm1_packed_h_negatives", "ts_listed")
        xm1_packed, h_neg = xm1_h_neg[:, 0:4 * K], [xm1_h_neg[:, 4 * K:6 * K], xm1_h_neg[:, 6 * K:8 * K]]
        h1_pos = held([P, 2 * K], BF16, "h1_pos")
        weave_on_gpsimd(xm1_packed, xm_raw[1][:])
        form_h(1, 0, (0, 1), sig1, weights1)
        form_h(1, 1, (0,), sig1, weights1)
        turn_h(0, 1, 4, on_vector, h_neg[0], ident)
        form_h(1, 1, (1,), sig1, weights1)
        along_rows = mx_operand("along_rows", "xm_raw1", 5 * HALF)
        for n, key in enumerate(((0, 1), (1, 0), (1, 1))):
            h_r[key] = columns(along_rows, HALF * n, HALF)
        xm_r[1] = columns(along_rows, 3 * HALF, K)
        quantize(h_r[0, 1], E5M2, h_neg[0], 0, HALF)
        turn_h(1, 0, 1, on_vector, h1_pos[:], ident)
        quantize(xm_r[1], E4M3, xm1_packed)
        turn_h(1, 1, 6, on_vector, h_neg[1], ident)
        quantize(h_r[1, 0], E5M2, h1_pos[:], 0, HALF)
        quantize(h_r[1, 1], E5M2, h_neg[1], 0, HALF)

        rest = mx_operand("w_i_rest", "h1_pos", 3 * HALF)
        for n, key in enumerate(((0, 1), (1, 0), (1, 1))):
            w_i[key] = columns(rest, HALF * n, HALF)
            quantize(w_i[key], E4M3, w_turned[key][:], 0, HALF)
        h_turned = [held([P, PACK * R], BF16, "h_turned%d" % b, ("x_raw1", "w_packed1")[b]) for b in range(B)]
        for b in range(B):
            for e in range(2):
                nc.gpsimd.tensor_scalar(h_turned[b][:, 2 * K * e:2 * K * (e + 1)].rearrange("q (s n u) -> q s n u", s=2, u=PACK),
                                        by_plane(h_planes[b])[:, :, HALF * e:HALF * (e + 1)].rearrange("q u (n s) -> q s n u", s=2),
                                        1.0, 0.0, MULT, ADD)

        staged = held([P, HALF], F32, "staged0_0_neg", "sig0")
        window1_runs = [held([P, RUN], F32, "window1_run%d" % n) for n in range(2)]
        dw = table_gradient(7, "dw0_neg", [(0, j, HALF, N) for j in range(2)])
        on_scalar(staged[:], dw[:, 0:HALF])
        on_scalar(window1_runs[0][:, 0:HALF], dw[:, HALF:N])
        place(indirect_on_scalar, 0, HALF, N, staged[:])
        staged = held([P, N], F32, "staged1_0", "w_plane0")
        on_vector(staged[:], table_gradient(3, "dw1_0", [(1, 0, 0, HALF), (1, 0, HALF, N)])[:])
        dw = table_gradient(5, "dw1_1", [(1, 1, 0, HALF), (1, 1, HALF, N)])
        on_vector(window1_runs[0][:, HALF:RUN], dw[:, 0:P])
        on_vector(window1_runs[1][:], dw[:, P:N])
        staged0_3 = held([P, HALF], F32, "staged0_3", "summed0_1")
        on_vector(staged0_3[:], table_gradient(0, "dw0_3_pos", [(0, 3, 0, HALF)])[:, 0:HALF])
        window2_last = held([P, RUN], F32, "window2_last")
        on_vector(window2_last[:], table_gradient(2, "dw2_last", [(1, 2, P, HALF), (1, 2, HALF, N)])[:, 0:RUN])
        place(on_vector, 0, N, B * N, staged[:])
        store_window(0, (nc.sync,))
        place(on_vector, 3, 0, HALF, staged0_3[:])

        place(indirect_on_scalar, 1, HALF, HALF + RUN, window1_runs[0][:])
        staged = held([P, HALF + RUN], F32, "staged0_3_neg_window2_first", "window1_run0")
        on_scalar(staged[:, HALF:HALF + RUN], table_gradient(4, "dw2_first", [(0, 2, HALF, N), (1, 2, 0, P)])[:, 0:RUN])
        on_scalar(staged[:, 0:HALF], table_gradient(6, "dw0_3_neg", [(0, 3, HALF, N)])[:, 0:HALF])
        place(indirect_on_scalar, 1, HALF + RUN, B * N, window1_runs[1][:])
        store_window(1, (nc.sync,))
        place(indirect_on_scalar, 2, HALF, HALF + RUN, staged[:, HALF:HALF + RUN])
        place(indirect_on_scalar, 3, HALF, N, staged[:, 0:HALF])
        place(indirect_on_scalar, 2, HALF + RUN, B * N, window2_last[:])
        store_window(2, (nc.scalar, nc.scalar))

        h_both = mx_operand("h_i", "h_planes", B * K)
        h_i = [columns(h_both, K * b, K) for b in range(B)]
        for b in range(B):
            quantize(h_i[b], E5M2, h_turned[b][:])
        last = held([P, N], F32, "staged1_3", "x_raw1")
        dw = bank(0, "dw1_3")
        product(dw[:], xm_r[1], E4M3, 3, columns(along_rows, HALF, N), E5M2)
        on_vector(last[:], dw[:])
        for b, tag in enumerate(("w_plane3", "xm_raw0")):
            staged = held([P, PACK * D], F32, "gx_staged%d" % b, tag)
            rows = out_1[b].rearrange("(p t) d -> p (t d)", t=PACK)
            for t, k in enumerate(((1, 5, 7, 3), (0, 1, 5, 7))[b]):
                row_tile(b, t, k, staged)
                if t % 2 == 1:
                    nc.sync.dma_start(out=rows[:, D * (t - 1):D * (t + 1)], in_=staged[:, D * (t - 1):D * (t + 1)])
        place(on_vector, 3, N, B * N, last[:])
        store_window(3, (nc.sync, nc.scalar))
